import numpy as np
import ml_dtypes


def mxq(x, axis, fmt="e4m3"):
    dtype, down = {"e4m3": (ml_dtypes.float8_e4m3fn, 7), "e5m2": (ml_dtypes.float8_e5m2, 14)}[fmt]
    v = np.moveaxis(np.asarray(x, np.float32).astype(ml_dtypes.bfloat16).astype(np.float64), axis, -1)
    blocks = v.reshape(v.shape[:-1] + (-1, 32))
    amax = np.abs(blocks).max(-1, keepdims=True)
    byte = np.maximum(np.where(amax > 0, np.frexp(amax)[1] - 1 + 127, 0) - down, 1)
    scale = np.exp2(byte - 127.0)
    codes = (blocks / scale).astype(np.float32).astype(dtype).astype(np.float64)
    return np.moveaxis((codes * scale).reshape(v.shape), -1, axis)


WIDE = False


def mx_kscale(k):
    if not WIDE:
        return np.ones(k)
    levels = np.array([18, -18])
    if k % 512:
        return np.exp2(np.random.permutation(np.resize(levels, k // 32))).repeat(32)
    a = np.empty((k // 512, 16))
    for p in range(k // 512):
        a[p, :8] = np.random.permutation(np.resize(levels, 8))
        for g in range(8):
            far = levels[np.abs(levels - a[p, g]) >= 10]
            a[p, g + 8] = far[np.random.randint(len(far))]
    return np.exp2(a.ravel()).repeat(32)


def f64(x):
    return np.asarray(x).astype(np.float64)


def striped(idx):
    return np.tile(np.asarray(idx).reshape(-1, 16).T, (8, 1)).astype(np.uint16)


def unstriped(offs):
    return offs[:16].T.reshape(-1).astype(np.int64)


B, N, T, D, R = 1, 512, 2048, 512, 1024
CLIP = 1.4


def setup_inputs():
    n = np.random.standard_normal
    idx = np.random.permutation(T)[:B * N]
    s = mx_kscale(D)[:, None]
    z = mx_kscale(R)[:, None]
    x = n((B, D, R))
    teach = np.exp(n((B, R, N)))
    teach = teach / teach.sum(-1, keepdims=True)
    return {
        "xT": (x * s).astype(np.float32),
        "wT": (n((D, T)) * (0.50 / np.sqrt(D)) / s).astype(np.float32),
        "y": teach.astype(np.float32),
        "wt": (np.random.uniform(0.5, 1.5, (B, R, 1)) * N / np.sqrt(R) * z).astype(np.float32),
        "xn": np.square(x).sum(1)[:, :, None].astype(np.float32),
        "xm": (x.transpose(0, 2, 1) / z).astype(np.float32),
        "offs": striped(idx),
    }


def reference(xT, wT, y, wt, xn, xm, offs):
    idx = unstriped(offs)
    pick = lambda x: x[:, idx].reshape(x.shape[0], B, N).transpose(1, 0, 2)
    a = mxq(f64(xT), 1, "e4m3").transpose(0, 2, 1) @ mxq(pick(f64(wT)), 1, "e4m3")
    e = np.exp(a - a.max(-1, keepdims=True))
    g = (e / e.sum(-1, keepdims=True) - f64(y))
    g = f64(wt) * np.minimum(1.0, CLIP / np.sqrt(f64(xn) * np.square(g).sum(-1, keepdims=True))) * g
    dw = mxq(f64(xm), 1, "e4m3").transpose(0, 2, 1) @ mxq(g, 1, "e5m2")
    gw = np.zeros((D, T))
    gw[:, idx] = dw.transpose(1, 0, 2).reshape(D, B * N)
    return gw

@@ -1,0 +1,333 @@
+from contextlib import ExitStack
+
+import concourse.mybir as mybir
+
+N, T, D, R = 512, 2048, 512, 1024
+CLIP = 1.4
+FLOPS = 2 * 2 * N * D * R
+
+F32 = mybir.dt.float32
+BF16 = mybir.dt.bfloat16
+U32 = mybir.dt.uint32
+U16 = mybir.dt.uint16
+U8 = mybir.dt.uint8
+E4M3 = mybir.dt.float8_e4m3fn_x4
+E5M2 = mybir.dt.float8_e5m2_x4
+ALU = mybir.AluOpType
+ACT = mybir.ActivationFunctionType
+AXIS = mybir.AxisListType
+
+P = 128
+PACK = 4
+K_PASS = P * PACK
+PASSES = R // K_PASS
+D_BLOCKS = D // P
+LINE = 4
+
+
+def tile_attend_gkl_w_clip_kernel(tc, xT, wT, y, wt, xn, xm, offs, out):
+    nc = tc.nc
+    with ExitStack() as ctx:
+        keep = ctx.enter_context(tc.tile_pool(name="keep", bufs=1))
+        psum = ctx.enter_context(tc.psum_pool(name="psum", bufs=1))
+
+        def sb(shape, dtype, name):
+            return keep.tile(shape, dtype, name=name, align_bytes=64)
+
+        offsets = keep.tile([P, N // 16], U16, name="offsets")
+        nc.sync.dma_start(offsets[:], offs)
+        w_rows = wT.rearrange("(p j) c -> p j c", j=PACK)
+        w_plane = []
+        for j in range(PACK):
+            plane = sb([P, T], F32, f"w_plane{j}")
+            nc.sync.dma_start(plane[:], w_rows[:, j, :])
+            w_plane.append(plane)
+        x_rows = xT.rearrange("b (p j) r -> p (b j) r", j=PACK)
+        y_rows = y.rearrange("b (g p t) i -> p (b g) t i", g=PASSES, t=PACK)
+        xm_rows = xm.rearrange("b (g p t) d -> p (b g) t d", g=PASSES, t=PACK)
+        HALF = K_PASS // 2
+        x_raw = {}
+        y_raw = {}
+
+        def load_x(g):
+            for h in range(2):
+                x_raw[g, h] = sb([P, PACK, HALF], F32, f"x_raw{g}_{h}")
+                c0 = g * K_PASS + h * HALF
+                nc.sync.dma_start(x_raw[g, h][:], x_rows[:, :, c0 : c0 + HALF])
+
+        def load_y(g):
+            for h in range(2):
+                y_raw[g, h] = sb([P, 2, N], F32, f"y_raw{g}_{h}")
+                nc.sync.dma_start(y_raw[g, h][:], y_rows[:, g, 2 * h : 2 * h + 2, :])
+
+        load_x(0)
+        load_x(1)
+        load_y(0)
+        load_y(1)
+        xm_raw = []
+        for g in range(PASSES):
+            raw = sb([P, PACK, D], F32, f"xm_raw{g}")
+            nc.sync.dma_start(raw[:], xm_rows[:, g, :, :])
+            xm_raw.append(raw)
+
+        xn_sb = sb([P, PASSES, PACK], F32, "xn_sb")
+        wt_sb = sb([P, PASSES, PACK], F32, "wt_sb")
+        nc.scalar.dma_start(xn_sb[:], xn.rearrange("b (g p t) o -> p (b g) (t o)", g=PASSES, t=PACK))
+        nc.scalar.dma_start(wt_sb[:], wt.rearrange("b (g p t) o -> p (b g) (t o)", g=PASSES, t=PACK))
+        xn_scaled = sb([P, PASSES, PACK], F32, "xn_scaled")
+        wt_neg = sb([P, PASSES, PACK], F32, "wt_neg")
+        nc.scalar.activation(xn_scaled[:], xn_sb[:], ACT.Copy, scale=1.0 / (CLIP * CLIP))
+        nc.scalar.activation(wt_neg[:], wt_sb[:], ACT.Copy, scale=-1.0)
+        minus_half = sb([P, PACK], F32, "minus_half")
+        nc.gpsimd.memset(minus_half[:], -0.5)
+
+        windows = []
+        for b in range(D_BLOCKS):
+            window = sb([P, T], F32, f"window{b}")
+            nc.vector.memset(window[:], 0.0)
+            windows.append(window)
+
+        def shared(shape, dtype, name, tag):
+            return keep.tile(shape, dtype, name=name, tag=tag, align_bytes=64)
+
+        w_bf = shared([P, N, PACK], BF16, "w_bf", "after_w")
+        for j in range(PACK):
+            nc.vector.tensor_copy(w_bf[:, :, j], w_plane[j][:].indirect(offsets[:]))
+        w_codes = sb([P, N], U32, "w_codes")
+        w_scales = sb([P, N], U8, "w_scales")
+        nc.vector.quantize_mx(out=w_codes[:].bitcast(E4M3), scales=w_scales[:], in_=w_bf[:].rearrange("p i j -> p (i j)"))
+
+        x_codes = shared([P, PASSES, PACK, P], U32, "x_codes", "x_raw0_1")
+        x_scales = sb([P, PASSES, PACK, P], U8, "x_scales")
+        x_bf = {}
+
+        def round_x(g, h, tag, on_vector):
+            x_bf[g, h] = shared([P, PACK, P // 2, PACK], BF16, f"x_bf{g}_{h}", tag)
+            dst = x_bf[g, h][:].rearrange("p t m j -> p m j t")
+            src = x_raw[g, h][:].rearrange("p j (m t) -> p m j t", t=PACK)
+            if on_vector:
+                nc.vector.tensor_copy(dst, src)
+            else:
+                nc.scalar.copy(dst, src)
+
+        def quantize_x(g, h, t):
+            cols = slice(h * (P // 2), (h + 1) * (P // 2))
+            nc.vector.quantize_mx(
+                out=x_codes[:, g, t, cols].bitcast(E4M3),
+                scales=x_scales[:, g, t, cols],
+                in_=x_bf[g, h][:, t, :, :].rearrange("p m j -> p (m j)"),
+            )
+
+        diff = [sb([P, PACK, N], F32, f"diff{g}") for g in range(PASSES)]
+        sums = [sb([P, PACK], F32, f"sums{g}") for g in range(PASSES)]
+        sumsq = [sb([P, PACK], F32, f"sumsq{g}") for g in range(PASSES)]
+        scores = {}
+        neg_max = {}
+        e = {}
+        tags = {"e1_3": "late", "m_bf0": "late", "g_rows1": "woven", "m_bf2": "woven", "m_codes0": "first", "m_bf3": "first"}
+
+        def tagged(shape, dtype, name):
+            return shared(shape, dtype, name, tags.get(name, name))
+
+        def score(g, t):
+            scores[g, t] = psum.tile([P, N], F32, name=f"scores{g}_{t}", tag=f"bank{PACK * g + t}")
+            nc.tensor.matmul_mx(
+                out=scores[g, t][:],
+                lhsT=x_codes[:, g, t, :].bitcast(E4M3),
+                lhsT_scale=x_scales[:, g, t, :],
+                rhs=w_codes[:].bitcast(E4M3),
+                rhs_scale=w_scales[:],
+                start=True,
+                stop=True,
+            )
+
+        def row_max(g, t):
+            neg_max[g, t] = tagged([P, 1], F32, f"neg_max{g}_{t}")
+            nc.vector.tensor_reduce(neg_max[g, t][:], scores[g, t][:], AXIS.X, ALU.max, negate=True)
+
+        def row_exp(g, t):
+            e[g, t] = tagged([P, N], F32, f"e{g}_{t}")
+            nc.scalar.activation(
+                e[g, t][:], scores[g, t][:], ACT.Exp, bias=neg_max[g, t][:], accum_out=sums[g][:, t : t + 1]
+            )
+
+        def row_diff(g, t):
+            nc.vector.scalar_tensor_tensor(
+                diff[g][:, t, :], y_raw[g, t // 2][:, t % 2, :], sums[g][:, t : t + 1], e[g, t][:], ALU.mult, ALU.subtract
+            )
+
+        def row_square(g, t):
+            nc.scalar.activation(e[g, t][:], diff[g][:, t, :], ACT.Square, accum_out=sumsq[g][:, t : t + 1])
+
+        sums_sq = {}
+        root = {}
+
+        def square_sums(g):
+            sums_sq[g] = tagged([P, PACK], F32, f"sums_sq{g}")
+            nc.vector.tensor_tensor(sums_sq[g][:], sums[g][:], sums[g][:], ALU.mult)
+
+        larger = {}
+
+        def row_larger(g, t, t0, n):
+            if (g, t0) not in larger:
+                larger[g, t0] = tagged([P, n], F32, f"larger{g}_{t0}")
+            col = slice(t, t + 1)
+            nc.vector.tensor_scalar(
+                larger[g, t0][:, t - t0 : t - t0 + 1], sumsq[g][:, col], xn_scaled[:, g, col], sums_sq[g][:, col], ALU.mult, ALU.max
+            )
+
+        def row_roots(g, t0, t1):
+            n = t1 - t0
+            for t in range(t0, t1):
+                row_larger(g, t, t0, n)
+            tile = tagged([P, n], F32, f"root{g}_{t0}")
+            nc.gpsimd.tensor_tensor(tile[:], larger[g, t0][:], minus_half[:, 0:n], ALU.pow)
+            for t in range(t0, t1):
+                root[g, t] = tile[:, t - t0 : t - t0 + 1]
+
+        def row_roots_sqrt(g, t0, t1):
+            n = t1 - t0
+            length = tagged([P, n], F32, f"length{g}_{t0}")
+            if n == 1:
+                nc.scalar.activation(length[:], sumsq[g][:, t0:t1], ACT.Sqrt, scale=xn_scaled[:, g, t0:t1])
+            else:
+                product = tagged([P, n], F32, f"product{g}_{t0}")
+                nc.vector.tensor_tensor(product[:], sumsq[g][:, t0:t1], xn_scaled[:, g, t0:t1], ALU.mult)
+                nc.scalar.activation(length[:], product[:], ACT.Sqrt)
+            bound = tagged([P, n], F32, f"bound{g}_{t0}")
+            nc.vector.tensor_tensor(bound[:], length[:], sums[g][:, t0:t1], ALU.max)
+            tile = tagged([P, n], F32, f"root{g}_{t0}")
+            nc.vector.reciprocal(tile[:], bound[:])
+            for t in range(t0, t1):
+                root[g, t] = tile[:, t - t0 : t - t0 + 1]
+
+        g_codes = sb([P, PASSES, N], U32, "g_codes")
+        g_scales = sb([P, PASSES, N], U8, "g_scales")
+        g_rows = {}
+        g_bf = {}
+
+        def scale_rows(g, t):
+            if g not in g_rows:
+                g_rows[g] = tagged([P, PACK, N], BF16, f"g_rows{g}")
+            nc.vector.tensor_scalar(
+                g_rows[g][:, t, :], diff[g][:, t, :], root[g, t], wt_neg[:, g, t : t + 1], ALU.mult, ALU.mult
+            )
+
+        def scale_rows_scalar(g, t):
+            if g not in g_rows:
+                g_rows[g] = tagged([P, PACK, N], BF16, f"g_rows{g}")
+            factor = tagged([P, 1], F32, f"factor{g}_{t}")
+            nc.scalar.activation(factor[:], root[g, t], ACT.Copy, scale=wt_neg[:, g, t : t + 1])
+            nc.scalar.activation(g_rows[g][:, t, :], diff[g][:, t, :], ACT.Copy, scale=factor[:])
+
+        def weave_g(g, c0, c1, on_vector):
+            if g not in g_bf:
+                g_bf[g] = tagged([P, N, PACK], BF16, f"g_bf{g}")
+            dst = g_bf[g][:, c0:c1, :].rearrange("p (c i) t -> p c t i", i=LINE)
+            src = g_rows[g][:, :, c0:c1].rearrange("p t (c i) -> p c t i", i=LINE)
+            if on_vector:
+                nc.vector.tensor_copy(dst, src)
+            else:
+                nc.scalar.copy(dst, src)
+
+        def quantize_g(g):
+            nc.vector.quantize_mx(
+                out=g_codes[:, g, :].bitcast(E5M2),
+                scales=g_scales[:, g, :],
+                in_=g_bf[g][:].rearrange("p i t -> p (i t)"),
+            )
+
+        m_bf = {}
+        m_codes = {}
+        m_scales = {}
+
+        def round_m(b0, b1):
+            tile = tagged([P, b1 - b0, PASSES, P, PACK], BF16, f"m_bf{b0}")
+            for b in range(b0, b1):
+                m_bf[b] = tile[:, b - b0, :, :, :]
+                for g in range(PASSES):
+                    nc.scalar.copy(
+                        m_bf[b][:, g, :, :].rearrange("p (c i) t -> p c t i", i=LINE),
+                        xm_raw[g][:, :, b * P : (b + 1) * P].rearrange("p t (c i) -> p c t i", i=LINE),
+                    )
+
+        def quantize_m(b):
+            m_codes[b] = tagged([P, PASSES, P], U32, f"m_codes{b}")
+            m_scales[b] = tagged([P, PASSES, P], U8, f"m_scales{b}")
+            nc.vector.quantize_mx(
+                out=m_codes[b][:].rearrange("p g m -> p (g m)").bitcast(E4M3),
+                scales=m_scales[b][:].rearrange("p g m -> p (g m)"),
+                in_=m_bf[b].rearrange("p g m t -> p (g m t)"),
+            )
+
+        dw = {}
+
+        def multiply(b):
+            acc = psum.tile([P, N], F32, name=f"acc{b}", tag=f"bank{b}")
+            for g in range(PASSES):
+                nc.tensor.matmul_mx(
+                    out=acc[:],
+                    lhsT=m_codes[b][:, g, :].bitcast(E4M3),
+                    lhsT_scale=m_scales[b][:, g, :],
+                    rhs=g_codes[:, g, :].bitcast(E5M2),
+                    rhs_scale=g_scales[:, g, :],
+                    start=(g == 0),
+                    stop=(g == PASSES - 1),
+                )
+            dw[b] = sb([P, N], F32, f"dw{b}")
+            nc.scalar.copy(dw[b][:], acc[:])
+
+        def place(b):
+            nc.vector.tensor_copy(windows[b][:].indirect(offsets[:]), dw[b][:])
+            nc.sync.dma_start(out[b * P : (b + 1) * P, :], windows[b][:])
+
+        round_x(0, 0, "x00", False)
+        round_x(0, 1, "after_w", True)
+        for t in range(PACK):
+            quantize_x(0, 0, t)
+            quantize_x(0, 1, t)
+            score(0, t)
+        round_x(1, 0, "x00", True)
+        round_x(1, 1, "after_w", False)
+        for t in range(PACK):
+            row_max(0, t)
+            row_exp(0, t)
+        for t in range(PACK):
+            quantize_x(1, 0, t)
+            quantize_x(1, 1, t)
+            score(1, t)
+        for t in range(PACK):
+            row_diff(0, t)
+            row_square(0, t)
+        square_sums(0)
+        row_roots(0, 0, PACK)
+        for t in range(PACK):
+            row_max(1, t)
+            row_exp(1, t)
+        for t in range(PACK):
+            row_diff(1, t)
+            row_square(1, t)
+        square_sums(1)
+        row_roots(1, 0, 4)
+        for t in range(4):
+            scale_rows(1, t)
+        weave_g(1, 0, 352, True)
+        weave_g(1, 352, 512, False)
+        for t in range(PACK):
+            scale_rows(0, t)
+        weave_g(0, 0, 256, True)
+        weave_g(0, 256, 512, False)
+        quantize_g(0)
+        quantize_g(1)
+        round_m(0, 2)
+        quantize_m(0)
+        multiply(0)
+        place(0)
+        quantize_m(1)
+        multiply(1)
+        for b in (2, 3):
+            round_m(b, b + 1)
+            quantize_m(b)
+            multiply(b)
+        for b in (1, 2, 3):
+            place(b)

@@ -23,6 +23,7 @@ K_PASS = P * PACK
 PASSES = R // K_PASS
 D_BLOCKS = D // P
 LINE = 4
+WINDOWS = 3
 
 
 def tile_attend_gkl_w_clip_kernel(tc, xT, wT, y, wt, xn, xm, offs, out):
@@ -82,40 +83,43 @@ def tile_attend_gkl_w_clip_kernel(tc, xT, wT, y, wt, xn, xm, offs, out):
         nc.gpsimd.memset(minus_half[:], -0.5)
 
         windows = []
-        for b in range(D_BLOCKS):
+        for b in range(WINDOWS):
             window = sb([P, T], F32, f"window{b}")
-            nc.vector.memset(window[:], 0.0)
+            if b < 2:
+                nc.vector.memset(window[:], 0.0)
+            else:
+                nc.gpsimd.memset(window[:], 0.0)
             windows.append(window)
 
         def shared(shape, dtype, name, tag):
             return keep.tile(shape, dtype, name=name, tag=tag, align_bytes=64)
 
-        w_bf = shared([P, N, PACK], BF16, "w_bf", "after_w")
+        w_bf = sb([P, N, PACK], BF16, "w_bf")
         for j in range(PACK):
             nc.vector.tensor_copy(w_bf[:, :, j], w_plane[j][:].indirect(offsets[:]))
         w_codes = sb([P, N], U32, "w_codes")
         w_scales = sb([P, N], U8, "w_scales")
         nc.vector.quantize_mx(out=w_codes[:].bitcast(E4M3), scales=w_scales[:], in_=w_bf[:].rearrange("p i j -> p (i j)"))
 
-        x_codes = shared([P, PASSES, PACK, P], U32, "x_codes", "x_raw0_1")
+        x_codes = sb([P, PASSES, PACK, P], U32, "x_codes")
         x_scales = sb([P, PASSES, PACK, P], U8, "x_scales")
         x_bf = {}
 
         def round_x(g, h, tag, on_vector):
-            x_bf[g, h] = shared([P, PACK, P // 2, PACK], BF16, f"x_bf{g}_{h}", tag)
-            dst = x_bf[g, h][:].rearrange("p t m j -> p m j t")
+            if g not in x_bf:
+                x_bf[g] = shared([P, PACK, P, PACK], BF16, f"x_bf{g}", tag)
+            dst = x_bf[g][:, :, h * (P // 2) : (h + 1) * (P // 2), :].rearrange("p t m j -> p m j t")
             src = x_raw[g, h][:].rearrange("p j (m t) -> p m j t", t=PACK)
             if on_vector:
                 nc.vector.tensor_copy(dst, src)
             else:
                 nc.scalar.copy(dst, src)
 
-        def quantize_x(g, h, t):
-            cols = slice(h * (P // 2), (h + 1) * (P // 2))
+        def quantize_x(g, t0, t1):
             nc.vector.quantize_mx(
-                out=x_codes[:, g, t, cols].bitcast(E4M3),
-                scales=x_scales[:, g, t, cols],
-                in_=x_bf[g, h][:, t, :, :].rearrange("p m j -> p (m j)"),
+                out=x_codes[:, g, t0:t1, :].rearrange("p t m -> p (t m)").bitcast(E4M3),
+                scales=x_scales[:, g, t0:t1, :].rearrange("p t m -> p (t m)"),
+                in_=x_bf[g][:, t0:t1, :, :].rearrange("p t m j -> p (t m j)"),
             )
 
         diff = [sb([P, PACK, N], F32, f"diff{g}") for g in range(PASSES)]
@@ -124,7 +128,7 @@ def tile_attend_gkl_w_clip_kernel(tc, xT, wT, y, wt, xn, xm, offs, out):
         scores = {}
         neg_max = {}
         e = {}
-        tags = {"e1_3": "late", "m_bf0": "late", "g_rows1": "woven", "m_bf2": "woven", "m_codes0": "first", "m_bf3": "first"}
+        tags = {"e1_3": "late", "m_bf0": "late", "g_rows1": "woven", "m_bf3": "woven", "g_bf1": "coded", "m_bf6": "coded", "dw1": "xm_raw1"}
 
         def tagged(shape, dtype, name):
             return shared(shape, dtype, name, tags.get(name, name))
@@ -230,6 +234,16 @@ def tile_attend_gkl_w_clip_kernel(tc, xT, wT, y, wt, xn, xm, offs, out):
             else:
                 nc.scalar.copy(dst, src)
 
+        def weave_plain(g, c0, c1, on_vector):
+            if g not in g_bf:
+                g_bf[g] = tagged([P, N, PACK], BF16, f"g_bf{g}")
+            dst = g_bf[g][:, c0:c1, :]
+            src = g_rows[g][:, :, c0:c1].rearrange("p t i -> p i t")
+            if on_vector:
+                nc.vector.tensor_copy(dst, src)
+            else:
+                nc.scalar.copy(dst, src)
+
         def quantize_g(g):
             nc.vector.quantize_mx(
                 out=g_codes[:, g, :].bitcast(E5M2),
@@ -238,26 +252,27 @@ def tile_attend_gkl_w_clip_kernel(tc, xT, wT, y, wt, xn, xm, offs, out):
             )
 
         m_bf = {}
-        m_codes = {}
-        m_scales = {}
+        m_codes = sb([P, D_BLOCKS * PASSES, P], U32, "m_codes")
+        m_scales = sb([P, D_BLOCKS * PASSES, P], U8, "m_scales")
 
-        def round_m(b0, b1):
-            tile = tagged([P, b1 - b0, PASSES, P, PACK], BF16, f"m_bf{b0}")
-            for b in range(b0, b1):
-                m_bf[b] = tile[:, b - b0, :, :, :]
-                for g in range(PASSES):
-                    nc.scalar.copy(
-                        m_bf[b][:, g, :, :].rearrange("p (c i) t -> p c t i", i=LINE),
-                        xm_raw[g][:, :, b * P : (b + 1) * P].rearrange("p t (c i) -> p c t i", i=LINE),
-                    )
+        def round_m(u0, u1, on_vector):
+            tile = tagged([P, u1 - u0, P, PACK], BF16, f"m_bf{u0}")
+            for u in range(u0, u1):
+                b, g = divmod(u, PASSES)
+                m_bf[u] = (tile, u - u0)
+                dst = tile[:, u - u0, :, :].rearrange("p (c i) t -> p c t i", i=LINE)
+                src = xm_raw[g][:, :, b * P : (b + 1) * P].rearrange("p t (c i) -> p c t i", i=LINE)
+                if on_vector:
+                    nc.vector.tensor_copy(dst, src)
+                else:
+                    nc.scalar.copy(dst, src)
 
-        def quantize_m(b):
-            m_codes[b] = tagged([P, PASSES, P], U32, f"m_codes{b}")
-            m_scales[b] = tagged([P, PASSES, P], U8, f"m_scales{b}")
+        def quantize_m(u0, u1):
+            tile, k = m_bf[u0]
             nc.vector.quantize_mx(
-                out=m_codes[b][:].rearrange("p g m -> p (g m)").bitcast(E4M3),
-                scales=m_scales[b][:].rearrange("p g m -> p (g m)"),
-                in_=m_bf[b].rearrange("p g m t -> p (g m t)"),
+                out=m_codes[:, u0:u1, :].rearrange("p u m -> p (u m)").bitcast(E4M3),
+                scales=m_scales[:, u0:u1, :].rearrange("p u m -> p (u m)"),
+                in_=tile[:, k : k + u1 - u0, :, :].rearrange("p u m t -> p (u m t)"),
             )
 
         dw = {}
@@ -267,34 +282,32 @@ def tile_attend_gkl_w_clip_kernel(tc, xT, wT, y, wt, xn, xm, offs, out):
             for g in range(PASSES):
                 nc.tensor.matmul_mx(
                     out=acc[:],
-                    lhsT=m_codes[b][:, g, :].bitcast(E4M3),
-                    lhsT_scale=m_scales[b][:, g, :],
+                    lhsT=m_codes[:, PASSES * b + g, :].bitcast(E4M3),
+                    lhsT_scale=m_scales[:, PASSES * b + g, :],
                     rhs=g_codes[:, g, :].bitcast(E5M2),
                     rhs_scale=g_scales[:, g, :],
                     start=(g == 0),
                     stop=(g == PASSES - 1),
                 )
-            dw[b] = sb([P, N], F32, f"dw{b}")
+            dw[b] = tagged([P, N], F32, f"dw{b}")
             nc.scalar.copy(dw[b][:], acc[:])
 
         def place(b):
-            nc.vector.tensor_copy(windows[b][:].indirect(offsets[:]), dw[b][:])
-            nc.sync.dma_start(out[b * P : (b + 1) * P, :], windows[b][:])
+            nc.vector.tensor_copy(windows[b % WINDOWS][:].indirect(offsets[:]), dw[b][:])
+            nc.sync.dma_start(out[b * P : (b + 1) * P, :], windows[b % WINDOWS][:])
 
-        round_x(0, 0, "x00", False)
-        round_x(0, 1, "after_w", True)
+        round_x(0, 0, "w_plane3", False)
+        round_x(0, 1, "w_plane3", True)
         for t in range(PACK):
-            quantize_x(0, 0, t)
-            quantize_x(0, 1, t)
+            quantize_x(0, t, t + 1)
             score(0, t)
-        round_x(1, 0, "x00", True)
-        round_x(1, 1, "after_w", False)
+        round_x(1, 0, "x_raw0_0", False)
+        round_x(1, 1, "x_raw0_0", False)
         for t in range(PACK):
             row_max(0, t)
             row_exp(0, t)
+        quantize_x(1, 0, PACK)
         for t in range(PACK):
-            quantize_x(1, 0, t)
-            quantize_x(1, 1, t)
             score(1, t)
         for t in range(PACK):
             row_diff(0, t)
@@ -309,25 +322,28 @@ def tile_attend_gkl_w_clip_kernel(tc, xT, wT, y, wt, xn, xm, offs, out):
             row_square(1, t)
         square_sums(1)
         row_roots(1, 0, 4)
-        for t in range(4):
+        scale_rows_scalar(1, 3)
+        for t in range(3):
             scale_rows(1, t)
         weave_g(1, 0, 352, True)
         weave_g(1, 352, 512, False)
         for t in range(PACK):
             scale_rows(0, t)
-        weave_g(0, 0, 256, True)
-        weave_g(0, 256, 512, False)
-        quantize_g(0)
+        weave_plain(0, 0, 255, True)
+        weave_plain(0, 255, 512, False)
         quantize_g(1)
-        round_m(0, 2)
-        quantize_m(0)
+        quantize_g(0)
+        round_m(0, 3, False)
+        quantize_m(0, 2)
         multiply(0)
         place(0)
-        quantize_m(1)
-        multiply(1)
-        for b in (2, 3):
-            round_m(b, b + 1)
-            quantize_m(b)
+        round_m(3, 6, False)
+        round_m(6, 8, True)
+        quantize_m(2, 3)
+        quantize_m(3, 4)
+        quantize_m(6, 8)
+        quantize_m(4, 6)
+        for b in (1, 2, 3):
             multiply(b)
         for b in (1, 2, 3):
             place(b)

@@ -56,14 +56,26 @@ def tile_attend_gkl_w_clip_kernel(tc, xT, wT, y, wt, xn, xm, offs, out):
                 c0 = g * K_PASS + h * HALF
                 nc.sync.dma_start(x_raw[g, h][:], x_rows[:, :, c0 : c0 + HALF])
 
+        xn_sb = sb([P, PASSES, PACK], F32, "xn_sb")
+        wt_sb = sb([P, PASSES, PACK], F32, "wt_sb")
+
+        def load_row_values():
+            nc.sync.dma_start(xn_sb[:], xn.rearrange("b (g p t) o -> p (b g) (t o)", g=PASSES, t=PACK))
+            nc.sync.dma_start(wt_sb[:], wt.rearrange("b (g p t) o -> p (b g) (t o)", g=PASSES, t=PACK))
+
+        def load_x_whole(g):
+            x_raw[g] = sb([P, PACK, K_PASS], F32, f"x_raw{g}")
+            nc.sync.dma_start(x_raw[g][:], x_rows[:, :, g * K_PASS : (g + 1) * K_PASS])
+
         def load_y(g):
             for h in range(2):
                 y_raw[g, h] = sb([P, 2, N], F32, f"y_raw{g}_{h}")
                 nc.sync.dma_start(y_raw[g, h][:], y_rows[:, g, 2 * h : 2 * h + 2, :])
 
-        load_x(0)
+        load_x_whole(0)
         load_x(1)
         load_y(0)
+        load_row_values()
         load_y(1)
         xm_raw = []
         for g in range(PASSES):
@@ -71,14 +83,6 @@ def tile_attend_gkl_w_clip_kernel(tc, xT, wT, y, wt, xn, xm, offs, out):
             nc.sync.dma_start(raw[:], xm_rows[:, g, :, :])
             xm_raw.append(raw)
 
-        xn_sb = sb([P, PASSES, PACK], F32, "xn_sb")
-        wt_sb = sb([P, PASSES, PACK], F32, "wt_sb")
-        nc.scalar.dma_start(xn_sb[:], xn.rearrange("b (g p t) o -> p (b g) (t o)", g=PASSES, t=PACK))
-        nc.scalar.dma_start(wt_sb[:], wt.rearrange("b (g p t) o -> p (b g) (t o)", g=PASSES, t=PACK))
-        xn_scaled = sb([P, PASSES, PACK], F32, "xn_scaled")
-        wt_neg = sb([P, PASSES, PACK], F32, "wt_neg")
-        nc.scalar.activation(xn_scaled[:], xn_sb[:], ACT.Copy, scale=1.0 / (CLIP * CLIP))
-        nc.scalar.activation(wt_neg[:], wt_sb[:], ACT.Copy, scale=-1.0)
         minus_half = sb([P, PACK], F32, "minus_half")
         nc.gpsimd.memset(minus_half[:], -0.5)
 
@@ -113,7 +117,17 @@ def tile_attend_gkl_w_clip_kernel(tc, xT, wT, y, wt, xn, xm, offs, out):
             if on_vector:
                 nc.vector.tensor_copy(dst, src)
             else:
-                nc.scalar.copy(dst, src)
+                nc.scalar.activation(dst, src, ACT.Copy)
+
+        def round_x_part(g, m0, m1, tag, on_vector):
+            if g not in x_bf:
+                x_bf[g] = shared([P, PACK, P, PACK], BF16, f"x_bf{g}", tag)
+            dst = x_bf[g][:, :, m0:m1, :].rearrange("p t m j -> p m j t")
+            src = x_raw[g][:, :, PACK * m0 : PACK * m1].rearrange("p j (m t) -> p m j t", t=PACK)
+            if on_vector:
+                nc.vector.tensor_copy(dst, src)
+            else:
+                nc.scalar.activation(dst, src, ACT.Copy)
 
         def quantize_x(g, t0, t1):
             nc.vector.quantize_mx(
@@ -124,11 +138,11 @@ def tile_attend_gkl_w_clip_kernel(tc, xT, wT, y, wt, xn, xm, offs, out):
 
         diff = [sb([P, PACK, N], F32, f"diff{g}") for g in range(PASSES)]
         sums = [sb([P, PACK], F32, f"sums{g}") for g in range(PASSES)]
-        sumsq = [sb([P, PACK], F32, f"sumsq{g}") for g in range(PASSES)]
+        sumsq = [shared([P, PACK], F32, f"sumsq{g}", f"sumsq{g}") for g in range(PASSES)]
         scores = {}
         neg_max = {}
         e = {}
-        tags = {"e1_3": "late", "m_bf0": "late", "g_rows1": "woven", "m_bf3": "woven", "g_bf1": "coded", "m_bf6": "coded", "dw1": "xm_raw1"}
+        tags = {"e1_3": "late", "m_bf0": "late", "g_rows1": "woven", "m_bf3": "woven", "g_bf1": "coded", "m_bf6": "coded", "dw1": "xm_raw1", "g_bf0": "sumsq1"}
 
         def tagged(shape, dtype, name):
             return shared(shape, dtype, name, tags.get(name, name))
@@ -161,7 +175,13 @@ def tile_attend_gkl_w_clip_kernel(tc, xT, wT, y, wt, xn, xm, offs, out):
             )
 
         def row_square(g, t):
-            nc.scalar.activation(e[g, t][:], diff[g][:, t, :], ACT.Square, accum_out=sumsq[g][:, t : t + 1])
+            nc.scalar.activation(e[g, t][:], diff[g][:, t, :], ACT.Square, scale=1.0 / CLIP, accum_out=sumsq[g][:, t : t + 1])
+
+        def row_square_vector(g, t):
+            nc.vector.scalar_tensor_tensor(
+                e[g, t][:], diff[g][:, t, :], 1.0 / (CLIP * CLIP), diff[g][:, t, :], ALU.mult, ALU.mult,
+                accum_out=sumsq[g][:, t : t + 1],
+            )
 
         sums_sq = {}
         root = {}
@@ -177,8 +197,18 @@ def tile_attend_gkl_w_clip_kernel(tc, xT, wT, y, wt, xn, xm, offs, out):
                 larger[g, t0] = tagged([P, n], F32, f"larger{g}_{t0}")
             col = slice(t, t + 1)
             nc.vector.tensor_scalar(
-                larger[g, t0][:, t - t0 : t - t0 + 1], sumsq[g][:, col], xn_scaled[:, g, col], sums_sq[g][:, col], ALU.mult, ALU.max
+                larger[g, t0][:, t - t0 : t - t0 + 1], sumsq[g][:, col], xn_sb[:, g, col], sums_sq[g][:, col], ALU.mult, ALU.max
             )
+
+        def row_roots_batch(g):
+            length = tagged([P, PACK], F32, f"length{g}")
+            nc.vector.tensor_tensor(length[:], sumsq[g][:], xn_sb[:, g, :], ALU.mult)
+            bound = tagged([P, PACK], F32, f"bound{g}")
+            nc.vector.tensor_tensor(bound[:], length[:], sums_sq[g][:], ALU.max)
+            tile = tagged([P, PACK], F32, f"root{g}")
+            nc.gpsimd.tensor_tensor(tile[:], bound[:], minus_half[:], ALU.pow)
+            for t in range(PACK):
+                root[g, t] = tile[:, t : t + 1]
 
         def row_roots(g, t0, t1):
             n = t1 - t0
@@ -193,10 +223,10 @@ def tile_attend_gkl_w_clip_kernel(tc, xT, wT, y, wt, xn, xm, offs, out):
             n = t1 - t0
             length = tagged([P, n], F32, f"length{g}_{t0}")
             if n == 1:
-                nc.scalar.activation(length[:], sumsq[g][:, t0:t1], ACT.Sqrt, scale=xn_scaled[:, g, t0:t1])
+                nc.scalar.activation(length[:], sumsq[g][:, t0:t1], ACT.Sqrt, scale=xn_sb[:, g, t0:t1])
             else:
                 product = tagged([P, n], F32, f"product{g}_{t0}")
-                nc.vector.tensor_tensor(product[:], sumsq[g][:, t0:t1], xn_scaled[:, g, t0:t1], ALU.mult)
+                nc.vector.tensor_tensor(product[:], sumsq[g][:, t0:t1], xn_sb[:, g, t0:t1], ALU.mult)
                 nc.scalar.activation(length[:], product[:], ACT.Sqrt)
             bound = tagged([P, n], F32, f"bound{g}_{t0}")
             nc.vector.tensor_tensor(bound[:], length[:], sums[g][:, t0:t1], ALU.max)
@@ -210,18 +240,25 @@ def tile_attend_gkl_w_clip_kernel(tc, xT, wT, y, wt, xn, xm, offs, out):
         g_rows = {}
         g_bf = {}
 
-        def scale_rows(g, t):
+        def scale_rows(g, t, c0=0, c1=N):
             if g not in g_rows:
                 g_rows[g] = tagged([P, PACK, N], BF16, f"g_rows{g}")
             nc.vector.tensor_scalar(
-                g_rows[g][:, t, :], diff[g][:, t, :], root[g, t], wt_neg[:, g, t : t + 1], ALU.mult, ALU.mult
+                g_rows[g][:, t, c0:c1], diff[g][:, t, c0:c1], root[g, t], wt_sb[:, g, t : t + 1], ALU.mult, ALU.mult
             )
 
         def scale_rows_scalar(g, t):
             if g not in g_rows:
                 g_rows[g] = tagged([P, PACK, N], BF16, f"g_rows{g}")
             factor = tagged([P, 1], F32, f"factor{g}_{t}")
-            nc.scalar.activation(factor[:], root[g, t], ACT.Copy, scale=wt_neg[:, g, t : t + 1])
+            nc.scalar.activation(factor[:], root[g, t], ACT.Copy, scale=wt_sb[:, g, t : t + 1])
+            nc.scalar.activation(g_rows[g][:, t, :], diff[g][:, t, :], ACT.Copy, scale=factor[:])
+
+        def scale_rows_shared(g, t):
+            if g not in g_rows:
+                g_rows[g] = tagged([P, PACK, N], BF16, f"g_rows{g}")
+            factor = tagged([P, 1], F32, f"factor{g}_{t}")
+            nc.vector.tensor_tensor(factor[:], root[g, t], wt_sb[:, g, t : t + 1], ALU.mult)
             nc.scalar.activation(g_rows[g][:, t, :], diff[g][:, t, :], ACT.Copy, scale=factor[:])
 
         def weave_g(g, c0, c1, on_vector):
@@ -244,11 +281,11 @@ def tile_attend_gkl_w_clip_kernel(tc, xT, wT, y, wt, xn, xm, offs, out):
             else:
                 nc.scalar.copy(dst, src)
 
-        def quantize_g(g):
+        def quantize_g(g, c0=0, c1=N):
             nc.vector.quantize_mx(
-                out=g_codes[:, g, :].bitcast(E5M2),
-                scales=g_scales[:, g, :],
-                in_=g_bf[g][:].rearrange("p i t -> p (i t)"),
+                out=g_codes[:, g, c0:c1].bitcast(E5M2),
+                scales=g_scales[:, g, c0:c1],
+                in_=g_bf[g][:, c0:c1, :].rearrange("p i t -> p (i t)"),
             )
 
         m_bf = {}
@@ -290,47 +327,65 @@ def tile_attend_gkl_w_clip_kernel(tc, xT, wT, y, wt, xn, xm, offs, out):
                     stop=(g == PASSES - 1),
                 )
             dw[b] = tagged([P, N], F32, f"dw{b}")
-            nc.scalar.copy(dw[b][:], acc[:])
+            nc.scalar.activation(dw[b][:], acc[:], ACT.Copy, scale=-1.0)
 
         def place(b):
             nc.vector.tensor_copy(windows[b % WINDOWS][:].indirect(offsets[:]), dw[b][:])
             nc.sync.dma_start(out[b * P : (b + 1) * P, :], windows[b % WINDOWS][:])
 
-        round_x(0, 0, "w_plane3", False)
-        round_x(0, 1, "w_plane3", True)
+        round_x_part(0, 84, P, "w_plane3", False)
+        round_x_part(0, 0, 84, "w_plane3", True)
         for t in range(PACK):
             quantize_x(0, t, t + 1)
             score(0, t)
-        round_x(1, 0, "x_raw0_0", False)
-        round_x(1, 1, "x_raw0_0", False)
+        round_x(1, 0, "x_raw0", False)
+        round_x(1, 1, "x_raw0", False)
         for t in range(PACK):
             row_max(0, t)
             row_exp(0, t)
         quantize_x(1, 0, PACK)
         for t in range(PACK):
             score(1, t)
-        for t in range(PACK):
-            row_diff(0, t)
-            row_square(0, t)
+        row_diff(0, 0)
+        row_square(0, 0)
+        row_diff(0, 1)
+        row_square(0, 1)
+        row_diff(0, 2)
+        row_square_vector(0, 2)
+        row_diff(0, 3)
+        row_square(0, 3)
         square_sums(0)
         row_roots(0, 0, PACK)
-        for t in range(PACK):
-            row_max(1, t)
-            row_exp(1, t)
-        for t in range(PACK):
-            row_diff(1, t)
-            row_square(1, t)
+        row_max(1, 0)
+        row_exp(1, 0)
+        row_max(1, 1)
+        row_exp(1, 1)
+        row_max(1, 2)
+        row_exp(1, 2)
+        row_max(1, 3)
+        row_exp(1, 3)
+        row_diff(1, 0)
+        row_square(1, 0)
+        row_diff(1, 1)
+        row_square(1, 1)
+        row_diff(1, 2)
+        row_square(1, 2)
+        row_diff(1, 3)
+        row_square(1, 3)
         square_sums(1)
         row_roots(1, 0, 4)
-        scale_rows_scalar(1, 3)
-        for t in range(3):
-            scale_rows(1, t)
+        scale_rows(1, 0)
+        scale_rows(1, 1)
+        scale_rows(1, 2)
+        scale_rows(1, 3)
         weave_g(1, 0, 352, True)
         weave_g(1, 352, 512, False)
-        for t in range(PACK):
-            scale_rows(0, t)
-        weave_plain(0, 0, 255, True)
-        weave_plain(0, 255, 512, False)
+        scale_rows(0, 0)
+        scale_rows(0, 1)
+        scale_rows(0, 2)
+        scale_rows(0, 3)
+        weave_plain(0, 0, 223, True)
+        weave_plain(0, 223, 512, False)
         quantize_g(1)
         quantize_g(0)
         round_m(0, 3, False)
@@ -341,8 +396,8 @@ def tile_attend_gkl_w_clip_kernel(tc, xT, wT, y, wt, xn, xm, offs, out):
         round_m(6, 8, True)
         quantize_m(2, 3)
         quantize_m(3, 4)
-        quantize_m(6, 8)
         quantize_m(4, 6)
+        quantize_m(6, 8)
         for b in (1, 2, 3):
             multiply(b)
         for b in (1, 2, 3):

@@ -22,8 +22,17 @@ PACK = 4
 K_PASS = P * PACK
 PASSES = R // K_PASS
 D_BLOCKS = D // P
-LINE = 4
+RUN = 4
+LIST_GROUP = 16
+
 WINDOWS = 3
+WINDOWS_ON_VECTOR = 2
+
+X0_VECTOR = 84
+G1_VECTOR = 352
+G0_VECTOR = 223
+SQUARES_ON_VECTOR = (0, 2)
+M_FIRST, M_SECOND, M_THIRD = range(0, 3), range(3, 6), range(6, 8)
 
 
 def tile_attend_gkl_w_clip_kernel(tc, xT, wT, y, wt, xn, xm, offs, out):
@@ -32,51 +41,62 @@ def tile_attend_gkl_w_clip_kernel(tc, xT, wT, y, wt, xn, xm, offs, out):
         keep = ctx.enter_context(tc.tile_pool(name="keep", bufs=1))
         psum = ctx.enter_context(tc.psum_pool(name="psum", bufs=1))
 
-        def sb(shape, dtype, name):
-            return keep.tile(shape, dtype, name=name, align_bytes=64)
+        follows = {
+            "x_bf0": "w_plane3",
+            "x_bf1": "x_raw0",
+            "g_bf0": "sumsq1",
+            f"m_bf{M_FIRST.start}": "e1_3",
+            f"m_bf{M_SECOND.start}": "g_rows1",
+            f"m_bf{M_THIRD.start}": "g_bf1",
+            "dw1": "xm_raw1",
+        }
 
-        offsets = keep.tile([P, N // 16], U16, name="offsets")
+        def sb(shape, dtype, name):
+            return keep.tile(shape, dtype, name=name, tag=follows.get(name, name), align_bytes=64)
+
+        def copy(on_vector, dst, src):
+            if on_vector:
+                nc.vector.tensor_copy(dst, src)
+            else:
+                nc.scalar.copy(dst, src)
+
+        offsets = keep.tile([P, N // LIST_GROUP], U16, name="offsets")
         nc.sync.dma_start(offsets[:], offs)
+
         w_rows = wT.rearrange("(p j) c -> p j c", j=PACK)
         w_plane = []
         for j in range(PACK):
             plane = sb([P, T], F32, f"w_plane{j}")
             nc.sync.dma_start(plane[:], w_rows[:, j, :])
             w_plane.append(plane)
+
         x_rows = xT.rearrange("b (p j) r -> p (b j) r", j=PACK)
+        x_raw0 = sb([P, PACK, K_PASS], F32, "x_raw0")
+        nc.sync.dma_start(x_raw0[:], x_rows[:, :, 0:K_PASS])
+        half = K_PASS // 2
+        x_raw1 = []
+        for h in range(2):
+            raw = sb([P, PACK, half], F32, f"x_raw1_{h}")
+            nc.sync.dma_start(raw[:], x_rows[:, :, K_PASS + h * half : K_PASS + (h + 1) * half])
+            x_raw1.append(raw)
+
         y_rows = y.rearrange("b (g p t) i -> p (b g) t i", g=PASSES, t=PACK)
-        xm_rows = xm.rearrange("b (g p t) d -> p (b g) t d", g=PASSES, t=PACK)
-        HALF = K_PASS // 2
-        x_raw = {}
-        y_raw = {}
-
-        def load_x(g):
-            for h in range(2):
-                x_raw[g, h] = sb([P, PACK, HALF], F32, f"x_raw{g}_{h}")
-                c0 = g * K_PASS + h * HALF
-                nc.sync.dma_start(x_raw[g, h][:], x_rows[:, :, c0 : c0 + HALF])
-
-        xn_sb = sb([P, PASSES, PACK], F32, "xn_sb")
-        wt_sb = sb([P, PASSES, PACK], F32, "wt_sb")
-
-        def load_row_values():
-            nc.sync.dma_start(xn_sb[:], xn.rearrange("b (g p t) o -> p (b g) (t o)", g=PASSES, t=PACK))
-            nc.sync.dma_start(wt_sb[:], wt.rearrange("b (g p t) o -> p (b g) (t o)", g=PASSES, t=PACK))
-
-        def load_x_whole(g):
-            x_raw[g] = sb([P, PACK, K_PASS], F32, f"x_raw{g}")
-            nc.sync.dma_start(x_raw[g][:], x_rows[:, :, g * K_PASS : (g + 1) * K_PASS])
+        y_sb = {}
 
         def load_y(g):
-            for h in range(2):
-                y_raw[g, h] = sb([P, 2, N], F32, f"y_raw{g}_{h}")
-                nc.sync.dma_start(y_raw[g, h][:], y_rows[:, g, 2 * h : 2 * h + 2, :])
+            for t0 in range(0, PACK, 2):
+                pair = sb([P, 2, N], F32, f"y_pair{g}_{t0}")
+                nc.sync.dma_start(pair[:], y_rows[:, g, t0 : t0 + 2, :])
+                y_sb[g, t0], y_sb[g, t0 + 1] = pair[:, 0, :], pair[:, 1, :]
 
-        load_x_whole(0)
-        load_x(1)
         load_y(0)
-        load_row_values()
+        xn_sb = sb([P, PASSES, PACK], F32, "xn_sb")
+        wt_sb = sb([P, PASSES, PACK], F32, "wt_sb")
+        nc.sync.dma_start(xn_sb[:], xn.rearrange("b (g p t) o -> p (b g) (t o)", g=PASSES, t=PACK))
+        nc.sync.dma_start(wt_sb[:], wt.rearrange("b (g p t) o -> p (b g) (t o)", g=PASSES, t=PACK))
         load_y(1)
+
+        xm_rows = xm.rearrange("b (g p t) d -> p (b g) t d", g=PASSES, t=PACK)
         xm_raw = []
         for g in range(PASSES):
             raw = sb([P, PACK, D], F32, f"xm_raw{g}")
@@ -84,46 +104,39 @@ def tile_attend_gkl_w_clip_kernel(tc, xT, wT, y, wt, xn, xm, offs, out):
             xm_raw.append(raw)
 
         minus_half = sb([P, PACK], F32, "minus_half")
-        nc.gpsimd.memset(minus_half[:], -0.5)
+        ones = sb([P, PACK], F32, "ones")
+        nc.gpsimd.memset(ones[:], 1.0)
+        nc.scalar.activation(minus_half[:], ones[:], ACT.Copy, scale=-0.5)
 
         windows = []
-        for b in range(WINDOWS):
-            window = sb([P, T], F32, f"window{b}")
-            if b < 2:
-                nc.vector.memset(window[:], 0.0)
-            else:
-                nc.gpsimd.memset(window[:], 0.0)
+        for k in range(WINDOWS):
+            window = sb([P, T], F32, f"window{k}")
+            engine = nc.vector if k < WINDOWS_ON_VECTOR else nc.gpsimd
+            engine.memset(window[:], 0.0)
             windows.append(window)
-
-        def shared(shape, dtype, name, tag):
-            return keep.tile(shape, dtype, name=name, tag=tag, align_bytes=64)
 
         w_bf = sb([P, N, PACK], BF16, "w_bf")
         for j in range(PACK):
             nc.vector.tensor_copy(w_bf[:, :, j], w_plane[j][:].indirect(offsets[:]))
         w_codes = sb([P, N], U32, "w_codes")
         w_scales = sb([P, N], U8, "w_scales")
-        nc.vector.quantize_mx(out=w_codes[:].bitcast(E4M3), scales=w_scales[:], in_=w_bf[:].rearrange("p i j -> p (i j)"))
+        nc.vector.quantize_mx(
+            out=w_codes[:].bitcast(E4M3), scales=w_scales[:], in_=w_bf[:].rearrange("p i j -> p (i j)")
+        )
 
         x_codes = sb([P, PASSES, PACK, P], U32, "x_codes")
         x_scales = sb([P, PASSES, PACK, P], U8, "x_scales")
         x_bf = {}
+        scores = {}
+        e = {}
+        root = {}
+        diff = [sb([P, PACK, N], F32, f"diff{g}") for g in range(PASSES)]
+        sums = [sb([P, PACK], F32, f"sums{g}") for g in range(PASSES)]
+        sumsq = [sb([P, PACK], F32, f"sumsq{g}") for g in range(PASSES)]
 
-        def round_x(g, h, tag, on_vector):
-            if g not in x_bf:
-                x_bf[g] = shared([P, PACK, P, PACK], BF16, f"x_bf{g}", tag)
-            dst = x_bf[g][:, :, h * (P // 2) : (h + 1) * (P // 2), :].rearrange("p t m j -> p m j t")
-            src = x_raw[g, h][:].rearrange("p j (m t) -> p m j t", t=PACK)
-            if on_vector:
-                nc.vector.tensor_copy(dst, src)
-            else:
-                nc.scalar.activation(dst, src, ACT.Copy)
-
-        def round_x_part(g, m0, m1, tag, on_vector):
-            if g not in x_bf:
-                x_bf[g] = shared([P, PACK, P, PACK], BF16, f"x_bf{g}", tag)
+        def weave_x(g, m0, m1, raw, on_vector):
             dst = x_bf[g][:, :, m0:m1, :].rearrange("p t m j -> p m j t")
-            src = x_raw[g][:, :, PACK * m0 : PACK * m1].rearrange("p j (m t) -> p m j t", t=PACK)
+            src = raw.rearrange("p j (m t) -> p m j t", t=PACK)
             if on_vector:
                 nc.vector.tensor_copy(dst, src)
             else:
@@ -135,17 +148,6 @@ def tile_attend_gkl_w_clip_kernel(tc, xT, wT, y, wt, xn, xm, offs, out):
                 scales=x_scales[:, g, t0:t1, :].rearrange("p t m -> p (t m)"),
                 in_=x_bf[g][:, t0:t1, :, :].rearrange("p t m j -> p (t m j)"),
             )
-
-        diff = [sb([P, PACK, N], F32, f"diff{g}") for g in range(PASSES)]
-        sums = [sb([P, PACK], F32, f"sums{g}") for g in range(PASSES)]
-        sumsq = [shared([P, PACK], F32, f"sumsq{g}", f"sumsq{g}") for g in range(PASSES)]
-        scores = {}
-        neg_max = {}
-        e = {}
-        tags = {"e1_3": "late", "m_bf0": "late", "g_rows1": "woven", "m_bf3": "woven", "g_bf1": "coded", "m_bf6": "coded", "dw1": "xm_raw1", "g_bf0": "sumsq1"}
-
-        def tagged(shape, dtype, name):
-            return shared(shape, dtype, name, tags.get(name, name))
 
         def score(g, t):
             scores[g, t] = psum.tile([P, N], F32, name=f"scores{g}_{t}", tag=f"bank{PACK * g + t}")
@@ -159,160 +161,115 @@ def tile_attend_gkl_w_clip_kernel(tc, xT, wT, y, wt, xn, xm, offs, out):
                 stop=True,
             )
 
-        def row_max(g, t):
-            neg_max[g, t] = tagged([P, 1], F32, f"neg_max{g}_{t}")
-            nc.vector.tensor_reduce(neg_max[g, t][:], scores[g, t][:], AXIS.X, ALU.max, negate=True)
-
-        def row_exp(g, t):
-            e[g, t] = tagged([P, N], F32, f"e{g}_{t}")
-            nc.scalar.activation(
-                e[g, t][:], scores[g, t][:], ACT.Exp, bias=neg_max[g, t][:], accum_out=sums[g][:, t : t + 1]
-            )
-
-        def row_diff(g, t):
-            nc.vector.scalar_tensor_tensor(
-                diff[g][:, t, :], y_raw[g, t // 2][:, t % 2, :], sums[g][:, t : t + 1], e[g, t][:], ALU.mult, ALU.subtract
-            )
-
-        def row_square(g, t):
-            nc.scalar.activation(e[g, t][:], diff[g][:, t, :], ACT.Square, scale=1.0 / CLIP, accum_out=sumsq[g][:, t : t + 1])
-
-        def row_square_vector(g, t):
-            nc.vector.scalar_tensor_tensor(
-                e[g, t][:], diff[g][:, t, :], 1.0 / (CLIP * CLIP), diff[g][:, t, :], ALU.mult, ALU.mult,
-                accum_out=sumsq[g][:, t : t + 1],
-            )
-
-        sums_sq = {}
-        root = {}
-
-        def square_sums(g):
-            sums_sq[g] = tagged([P, PACK], F32, f"sums_sq{g}")
-            nc.vector.tensor_tensor(sums_sq[g][:], sums[g][:], sums[g][:], ALU.mult)
-
-        larger = {}
-
-        def row_larger(g, t, t0, n):
-            if (g, t0) not in larger:
-                larger[g, t0] = tagged([P, n], F32, f"larger{g}_{t0}")
-            col = slice(t, t + 1)
-            nc.vector.tensor_scalar(
-                larger[g, t0][:, t - t0 : t - t0 + 1], sumsq[g][:, col], xn_sb[:, g, col], sums_sq[g][:, col], ALU.mult, ALU.max
-            )
-
-        def row_roots_batch(g):
-            length = tagged([P, PACK], F32, f"length{g}")
-            nc.vector.tensor_tensor(length[:], sumsq[g][:], xn_sb[:, g, :], ALU.mult)
-            bound = tagged([P, PACK], F32, f"bound{g}")
-            nc.vector.tensor_tensor(bound[:], length[:], sums_sq[g][:], ALU.max)
-            tile = tagged([P, PACK], F32, f"root{g}")
-            nc.gpsimd.tensor_tensor(tile[:], bound[:], minus_half[:], ALU.pow)
+        def exponentials(g):
             for t in range(PACK):
-                root[g, t] = tile[:, t : t + 1]
+                neg_max = sb([P, 1], F32, f"neg_max{g}_{t}")
+                nc.vector.tensor_reduce(neg_max[:], scores[g, t][:], AXIS.X, ALU.max, negate=True)
+                e[g, t] = sb([P, N], F32, f"e{g}_{t}")
+                nc.scalar.activation(
+                    e[g, t][:], scores[g, t][:], ACT.Exp, bias=neg_max[:], accum_out=sums[g][:, t : t + 1]
+                )
 
-        def row_roots(g, t0, t1):
-            n = t1 - t0
-            for t in range(t0, t1):
-                row_larger(g, t, t0, n)
-            tile = tagged([P, n], F32, f"root{g}_{t0}")
-            nc.gpsimd.tensor_tensor(tile[:], larger[g, t0][:], minus_half[:, 0:n], ALU.pow)
-            for t in range(t0, t1):
-                root[g, t] = tile[:, t - t0 : t - t0 + 1]
+        def differences(g):
+            for t in range(PACK):
+                rows = diff[g][:, t, :]
+                total = sumsq[g][:, t : t + 1]
+                nc.vector.scalar_tensor_tensor(
+                    rows, y_sb[g, t], sums[g][:, t : t + 1], e[g, t][:], ALU.mult, ALU.subtract
+                )
+                if (g, t) == SQUARES_ON_VECTOR:
+                    nc.vector.scalar_tensor_tensor(
+                        e[g, t][:], rows, 1.0 / (CLIP * CLIP), rows, ALU.mult, ALU.mult, accum_out=total
+                    )
+                else:
+                    nc.scalar.activation(e[g, t][:], rows, ACT.Square, scale=1.0 / CLIP, accum_out=total)
 
-        def row_roots_sqrt(g, t0, t1):
-            n = t1 - t0
-            length = tagged([P, n], F32, f"length{g}_{t0}")
-            if n == 1:
-                nc.scalar.activation(length[:], sumsq[g][:, t0:t1], ACT.Sqrt, scale=xn_sb[:, g, t0:t1])
-            else:
-                product = tagged([P, n], F32, f"product{g}_{t0}")
-                nc.vector.tensor_tensor(product[:], sumsq[g][:, t0:t1], xn_sb[:, g, t0:t1], ALU.mult)
-                nc.scalar.activation(length[:], product[:], ACT.Sqrt)
-            bound = tagged([P, n], F32, f"bound{g}_{t0}")
-            nc.vector.tensor_tensor(bound[:], length[:], sums[g][:, t0:t1], ALU.max)
-            tile = tagged([P, n], F32, f"root{g}_{t0}")
-            nc.vector.reciprocal(tile[:], bound[:])
-            for t in range(t0, t1):
-                root[g, t] = tile[:, t - t0 : t - t0 + 1]
+        def row_roots(g):
+            sums_sq = sb([P, PACK], F32, f"sums_sq{g}")
+            nc.vector.tensor_tensor(sums_sq[:], sums[g][:], sums[g][:], ALU.mult)
+            larger = sb([P, PACK], F32, f"larger{g}")
+            for t in range(PACK):
+                col = slice(t, t + 1)
+                nc.vector.tensor_scalar(
+                    larger[:, col], sumsq[g][:, col], xn_sb[:, g, col], sums_sq[:, col], ALU.mult, ALU.max
+                )
+            root[g] = sb([P, PACK], F32, f"root{g}")
+            nc.gpsimd.tensor_tensor(root[g][:], larger[:], minus_half[:], ALU.pow)
+
+        x_bf[0] = sb([P, PACK, P, PACK], BF16, "x_bf0")
+        weave_x(0, X0_VECTOR, P, x_raw0[:, :, PACK * X0_VECTOR :], False)
+        weave_x(0, 0, X0_VECTOR, x_raw0[:, :, 0 : PACK * X0_VECTOR], True)
+        for t in range(PACK):
+            quantize_x(0, t, t + 1)
+            score(0, t)
+        x_bf[1] = sb([P, PACK, P, PACK], BF16, "x_bf1")
+        for h in range(2):
+            weave_x(1, h * (P // 2), (h + 1) * (P // 2), x_raw1[h][:], False)
+        exponentials(0)
+        quantize_x(1, 0, PACK)
+        for t in range(PACK):
+            score(1, t)
+        differences(0)
+        row_roots(0)
+        exponentials(1)
+        differences(1)
+        row_roots(1)
 
         g_codes = sb([P, PASSES, N], U32, "g_codes")
         g_scales = sb([P, PASSES, N], U8, "g_scales")
         g_rows = {}
         g_bf = {}
 
-        def scale_rows(g, t, c0=0, c1=N):
-            if g not in g_rows:
-                g_rows[g] = tagged([P, PACK, N], BF16, f"g_rows{g}")
-            nc.vector.tensor_scalar(
-                g_rows[g][:, t, c0:c1], diff[g][:, t, c0:c1], root[g, t], wt_sb[:, g, t : t + 1], ALU.mult, ALU.mult
+        def scale_rows(g):
+            g_rows[g] = sb([P, PACK, N], BF16, f"g_rows{g}")
+            for t in range(PACK):
+                col = slice(t, t + 1)
+                nc.vector.tensor_scalar(
+                    g_rows[g][:, t, :], diff[g][:, t, :], root[g][:, col], wt_sb[:, g, col], ALU.mult, ALU.mult
+                )
+            g_bf[g] = sb([P, N, PACK], BF16, f"g_bf{g}")
+
+        scale_rows(1)
+        for slots, on_vector in ((slice(0, G1_VECTOR), True), (slice(G1_VECTOR, N), False)):
+            copy(
+                on_vector,
+                g_bf[1][:, slots, :].rearrange("p (c i) t -> p c t i", i=RUN),
+                g_rows[1][:, :, slots].rearrange("p t (c i) -> p c t i", i=RUN),
             )
-
-        def scale_rows_scalar(g, t):
-            if g not in g_rows:
-                g_rows[g] = tagged([P, PACK, N], BF16, f"g_rows{g}")
-            factor = tagged([P, 1], F32, f"factor{g}_{t}")
-            nc.scalar.activation(factor[:], root[g, t], ACT.Copy, scale=wt_sb[:, g, t : t + 1])
-            nc.scalar.activation(g_rows[g][:, t, :], diff[g][:, t, :], ACT.Copy, scale=factor[:])
-
-        def scale_rows_shared(g, t):
-            if g not in g_rows:
-                g_rows[g] = tagged([P, PACK, N], BF16, f"g_rows{g}")
-            factor = tagged([P, 1], F32, f"factor{g}_{t}")
-            nc.vector.tensor_tensor(factor[:], root[g, t], wt_sb[:, g, t : t + 1], ALU.mult)
-            nc.scalar.activation(g_rows[g][:, t, :], diff[g][:, t, :], ACT.Copy, scale=factor[:])
-
-        def weave_g(g, c0, c1, on_vector):
-            if g not in g_bf:
-                g_bf[g] = tagged([P, N, PACK], BF16, f"g_bf{g}")
-            dst = g_bf[g][:, c0:c1, :].rearrange("p (c i) t -> p c t i", i=LINE)
-            src = g_rows[g][:, :, c0:c1].rearrange("p t (c i) -> p c t i", i=LINE)
-            if on_vector:
-                nc.vector.tensor_copy(dst, src)
-            else:
-                nc.scalar.copy(dst, src)
-
-        def weave_plain(g, c0, c1, on_vector):
-            if g not in g_bf:
-                g_bf[g] = tagged([P, N, PACK], BF16, f"g_bf{g}")
-            dst = g_bf[g][:, c0:c1, :]
-            src = g_rows[g][:, :, c0:c1].rearrange("p t i -> p i t")
-            if on_vector:
-                nc.vector.tensor_copy(dst, src)
-            else:
-                nc.scalar.copy(dst, src)
-
-        def quantize_g(g, c0=0, c1=N):
+        scale_rows(0)
+        for slots, on_vector in ((slice(0, G0_VECTOR), True), (slice(G0_VECTOR, N), False)):
+            copy(on_vector, g_bf[0][:, slots, :], g_rows[0][:, :, slots].rearrange("p t i -> p i t"))
+        for g in (1, 0):
             nc.vector.quantize_mx(
-                out=g_codes[:, g, c0:c1].bitcast(E5M2),
-                scales=g_scales[:, g, c0:c1],
-                in_=g_bf[g][:, c0:c1, :].rearrange("p i t -> p (i t)"),
+                out=g_codes[:, g, :].bitcast(E5M2),
+                scales=g_scales[:, g, :],
+                in_=g_bf[g][:].rearrange("p i t -> p (i t)"),
             )
 
-        m_bf = {}
         m_codes = sb([P, D_BLOCKS * PASSES, P], U32, "m_codes")
         m_scales = sb([P, D_BLOCKS * PASSES, P], U8, "m_scales")
-
-        def round_m(u0, u1, on_vector):
-            tile = tagged([P, u1 - u0, P, PACK], BF16, f"m_bf{u0}")
-            for u in range(u0, u1):
-                b, g = divmod(u, PASSES)
-                m_bf[u] = (tile, u - u0)
-                dst = tile[:, u - u0, :, :].rearrange("p (c i) t -> p c t i", i=LINE)
-                src = xm_raw[g][:, :, b * P : (b + 1) * P].rearrange("p t (c i) -> p c t i", i=LINE)
-                if on_vector:
-                    nc.vector.tensor_copy(dst, src)
-                else:
-                    nc.scalar.copy(dst, src)
-
-        def quantize_m(u0, u1):
-            tile, k = m_bf[u0]
-            nc.vector.quantize_mx(
-                out=m_codes[:, u0:u1, :].rearrange("p u m -> p (u m)").bitcast(E4M3),
-                scales=m_scales[:, u0:u1, :].rearrange("p u m -> p (u m)"),
-                in_=tile[:, k : k + u1 - u0, :, :].rearrange("p u m t -> p (u m t)"),
-            )
-
+        m_bf = {}
         dw = {}
+
+        def weave_m(units, on_vector):
+            m_bf[units] = sb([P, len(units), P, PACK], BF16, f"m_bf{units.start}")
+            for u in units:
+                b, g = divmod(u, PASSES)
+                copy(
+                    on_vector,
+                    m_bf[units][:, u - units.start, :, :].rearrange("p (c i) t -> p c t i", i=RUN),
+                    xm_raw[g][:, :, b * P : (b + 1) * P].rearrange("p t (c i) -> p c t i", i=RUN),
+                )
+
+        def quantize_m(b):
+            for units in (M_FIRST, M_SECOND, M_THIRD):
+                u0, u1 = max(units.start, PASSES * b), min(units.stop, PASSES * (b + 1))
+                if u0 < u1:
+                    nc.vector.quantize_mx(
+                        out=m_codes[:, u0:u1, :].rearrange("p u m -> p (u m)").bitcast(E4M3),
+                        scales=m_scales[:, u0:u1, :].rearrange("p u m -> p (u m)"),
+                        in_=m_bf[units][:, u0 - units.start : u1 - units.start, :, :].rearrange("p u m t -> p (u m t)"),
+                    )
 
         def multiply(b):
             acc = psum.tile([P, N], F32, name=f"acc{b}", tag=f"bank{b}")
@@ -326,79 +283,20 @@ def tile_attend_gkl_w_clip_kernel(tc, xT, wT, y, wt, xn, xm, offs, out):
                     start=(g == 0),
                     stop=(g == PASSES - 1),
                 )
-            dw[b] = tagged([P, N], F32, f"dw{b}")
+            dw[b] = sb([P, N], F32, f"dw{b}")
             nc.scalar.activation(dw[b][:], acc[:], ACT.Copy, scale=-1.0)
 
         def place(b):
-            nc.vector.tensor_copy(windows[b % WINDOWS][:].indirect(offsets[:]), dw[b][:])
-            nc.sync.dma_start(out[b * P : (b + 1) * P, :], windows[b % WINDOWS][:])
+            window = windows[b % WINDOWS]
+            nc.vector.tensor_copy(window[:].indirect(offsets[:]), dw[b][:])
+            nc.sync.dma_start(out[b * P : (b + 1) * P, :], window[:])
 
-        round_x_part(0, 84, P, "w_plane3", False)
-        round_x_part(0, 0, 84, "w_plane3", True)
-        for t in range(PACK):
-            quantize_x(0, t, t + 1)
-            score(0, t)
-        round_x(1, 0, "x_raw0", False)
-        round_x(1, 1, "x_raw0", False)
-        for t in range(PACK):
-            row_max(0, t)
-            row_exp(0, t)
-        quantize_x(1, 0, PACK)
-        for t in range(PACK):
-            score(1, t)
-        row_diff(0, 0)
-        row_square(0, 0)
-        row_diff(0, 1)
-        row_square(0, 1)
-        row_diff(0, 2)
-        row_square_vector(0, 2)
-        row_diff(0, 3)
-        row_square(0, 3)
-        square_sums(0)
-        row_roots(0, 0, PACK)
-        row_max(1, 0)
-        row_exp(1, 0)
-        row_max(1, 1)
-        row_exp(1, 1)
-        row_max(1, 2)
-        row_exp(1, 2)
-        row_max(1, 3)
-        row_exp(1, 3)
-        row_diff(1, 0)
-        row_square(1, 0)
-        row_diff(1, 1)
-        row_square(1, 1)
-        row_diff(1, 2)
-        row_square(1, 2)
-        row_diff(1, 3)
-        row_square(1, 3)
-        square_sums(1)
-        row_roots(1, 0, 4)
-        scale_rows(1, 0)
-        scale_rows(1, 1)
-        scale_rows(1, 2)
-        scale_rows(1, 3)
-        weave_g(1, 0, 352, True)
-        weave_g(1, 352, 512, False)
-        scale_rows(0, 0)
-        scale_rows(0, 1)
-        scale_rows(0, 2)
-        scale_rows(0, 3)
-        weave_plain(0, 0, 223, True)
-        weave_plain(0, 223, 512, False)
-        quantize_g(1)
-        quantize_g(0)
-        round_m(0, 3, False)
-        quantize_m(0, 2)
+        weave_m(M_FIRST, False)
+        quantize_m(0)
         multiply(0)
         place(0)
-        round_m(3, 6, False)
-        round_m(6, 8, True)
-        quantize_m(2, 3)
-        quantize_m(3, 4)
-        quantize_m(4, 6)
-        quantize_m(6, 8)
-        for b in (1, 2, 3):
-            multiply(b)
-        for b in (1, 2, 3):
-            place(b)
+        weave_m(M_SECOND, False)
+        weave_m(M_THIRD, True)
+        for step in (quantize_m, multiply, place):
+            for b in range(1, D_BLOCKS):
+                step(b)

@@ -28,7 +28,8 @@ LIST_GROUP = 16
 WINDOWS = 3
 WINDOWS_ON_VECTOR = 2
 
-X0_VECTOR = 84
+W_VECTOR = 352
+X0_VECTOR = 70
 G1_VECTOR = 352
 G0_VECTOR = 223
 SQUARES_ON_VECTOR = (0, 2)
@@ -42,7 +43,7 @@ def tile_attend_gkl_w_clip_kernel(tc, xT, wT, y, wt, xn, xm, offs, out):
         psum = ctx.enter_context(tc.psum_pool(name="psum", bufs=1))
 
         follows = {
-            "x_bf0": "w_plane3",
+            "x_bf0": "w_picked",
             "x_bf1": "x_raw0",
             "g_bf0": "sumsq1",
             f"m_bf{M_FIRST.start}": "e1_3",
@@ -115,9 +116,16 @@ def tile_attend_gkl_w_clip_kernel(tc, xT, wT, y, wt, xn, xm, offs, out):
             engine.memset(window[:], 0.0)
             windows.append(window)
 
-        w_bf = sb([P, N, PACK], BF16, "w_bf")
+        w_picked = sb([P, PACK, N], F32, "w_picked")
         for j in range(PACK):
-            nc.vector.tensor_copy(w_bf[:, :, j], w_plane[j][:].indirect(offsets[:]))
+            nc.vector.tensor_copy(w_picked[:, j, :], w_plane[j][:].indirect(offsets[:]))
+        w_bf = sb([P, N, PACK], BF16, "w_bf")
+        for slots, on_vector in ((slice(0, W_VECTOR), True), (slice(W_VECTOR, N), False)):
+            copy(
+                on_vector,
+                w_bf[:, slots, :].rearrange("p (c i) j -> p c j i", i=RUN),
+                w_picked[:, :, slots].rearrange("p j (c i) -> p c j i", i=RUN),
+            )
         w_codes = sb([P, N], U32, "w_codes")
         w_scales = sb([P, N], U8, "w_scales")
         nc.vector.quantize_mx(
@@ -135,12 +143,16 @@ def tile_attend_gkl_w_clip_kernel(tc, xT, wT, y, wt, xn, xm, offs, out):
         sumsq = [sb([P, PACK], F32, f"sumsq{g}") for g in range(PASSES)]
 
         def weave_x(g, m0, m1, raw, on_vector):
-            dst = x_bf[g][:, :, m0:m1, :].rearrange("p t m j -> p m j t")
-            src = raw.rearrange("p j (m t) -> p m j t", t=PACK)
+            dst = x_bf[g][:, :, m0:m1, :]
             if on_vector:
-                nc.vector.tensor_copy(dst, src)
+                nc.vector.tensor_copy(
+                    dst.rearrange("p (u t) m j -> p u m j t", u=2),
+                    raw.rearrange("p j (m u t) -> p u m j t", u=2, t=2),
+                )
             else:
-                nc.scalar.activation(dst, src, ACT.Copy)
+                nc.scalar.activation(
+                    dst.rearrange("p t m j -> p m j t"), raw.rearrange("p j (m t) -> p m j t", t=PACK), ACT.Copy
+                )
 
         def quantize_x(g, t0, t1):
             nc.vector.quantize_mx(

@@ -26,14 +26,7 @@ RUN = 4
 LIST_GROUP = 16
 
 WINDOWS = 3
-WINDOWS_ON_VECTOR = 2
-
-W_VECTOR = 352
-X0_VECTOR = 70
-G1_VECTOR = 352
-G0_VECTOR = 223
-SQUARES_ON_VECTOR = (0, 2)
-M_FIRST, M_SECOND, M_THIRD = range(0, 3), range(3, 6), range(6, 8)
+TILES = PASSES * PACK
 
 
 def tile_attend_gkl_w_clip_kernel(tc, xT, wT, y, wt, xn, xm, offs, out):
@@ -43,59 +36,47 @@ def tile_attend_gkl_w_clip_kernel(tc, xT, wT, y, wt, xn, xm, offs, out):
         psum = ctx.enter_context(tc.psum_pool(name="psum", bufs=1))
 
         follows = {
-            "x_bf0": "w_picked",
-            "x_bf1": "x_raw0",
-            "g_bf0": "sumsq1",
-            f"m_bf{M_FIRST.start}": "e1_3",
-            f"m_bf{M_SECOND.start}": "g_rows1",
-            f"m_bf{M_THIRD.start}": "g_bf1",
+            "x_bf0_1": "w_bf",
+            "x_bf1": "x_raw0_1",
+            "g_rows": "y_pair1_2",
+            "m_bf": f"e{TILES - 1}",
             "dw1": "xm_raw1",
         }
 
         def sb(shape, dtype, name):
             return keep.tile(shape, dtype, name=name, tag=follows.get(name, name), align_bytes=64)
 
-        def copy(on_vector, dst, src):
-            if on_vector:
-                nc.vector.tensor_copy(dst, src)
-            else:
-                nc.scalar.copy(dst, src)
+        xn_sb = sb([P, PASSES, PACK], F32, "xn_sb")
+        wt_sb = sb([P, PASSES, PACK], F32, "wt_sb")
+        nc.scalar.dma_start(xn_sb[:], xn.rearrange("b (g p t) o -> p (b g) (t o)", g=PASSES, t=PACK))
+        nc.scalar.dma_start(wt_sb[:], wt.rearrange("b (g p t) o -> p (b g) (t o)", g=PASSES, t=PACK))
 
         offsets = keep.tile([P, N // LIST_GROUP], U16, name="offsets")
-        nc.sync.dma_start(offsets[:], offs)
-
         w_rows = wT.rearrange("(p j) c -> p j c", j=PACK)
         w_plane = []
         for j in range(PACK):
             plane = sb([P, T], F32, f"w_plane{j}")
             nc.sync.dma_start(plane[:], w_rows[:, j, :])
             w_plane.append(plane)
+            if j == 0:
+                nc.sync.dma_start(offsets[:], offs)
 
         x_rows = xT.rearrange("b (p j) r -> p (b j) r", j=PACK)
-        x_raw0 = sb([P, PACK, K_PASS], F32, "x_raw0")
-        nc.sync.dma_start(x_raw0[:], x_rows[:, :, 0:K_PASS])
         half = K_PASS // 2
-        x_raw1 = []
-        for h in range(2):
-            raw = sb([P, PACK, half], F32, f"x_raw1_{h}")
-            nc.sync.dma_start(raw[:], x_rows[:, :, K_PASS + h * half : K_PASS + (h + 1) * half])
-            x_raw1.append(raw)
+        x_raw = {}
+        for g in range(PASSES):
+            for h in range(2):
+                x_raw[g, h] = sb([P, PACK, half], F32, f"x_raw{g}_{h}")
+                c0 = g * K_PASS + h * half
+                nc.sync.dma_start(x_raw[g, h][:], x_rows[:, :, c0 : c0 + half])
 
         y_rows = y.rearrange("b (g p t) i -> p (b g) t i", g=PASSES, t=PACK)
-        y_sb = {}
-
-        def load_y(g):
+        y_sb = []
+        for g in range(PASSES):
             for t0 in range(0, PACK, 2):
                 pair = sb([P, 2, N], F32, f"y_pair{g}_{t0}")
                 nc.sync.dma_start(pair[:], y_rows[:, g, t0 : t0 + 2, :])
-                y_sb[g, t0], y_sb[g, t0 + 1] = pair[:, 0, :], pair[:, 1, :]
-
-        load_y(0)
-        xn_sb = sb([P, PASSES, PACK], F32, "xn_sb")
-        wt_sb = sb([P, PASSES, PACK], F32, "wt_sb")
-        nc.sync.dma_start(xn_sb[:], xn.rearrange("b (g p t) o -> p (b g) (t o)", g=PASSES, t=PACK))
-        nc.sync.dma_start(wt_sb[:], wt.rearrange("b (g p t) o -> p (b g) (t o)", g=PASSES, t=PACK))
-        load_y(1)
+                y_sb.extend([pair[:, 0, :], pair[:, 1, :]])
 
         xm_rows = xm.rearrange("b (g p t) d -> p (b g) t d", g=PASSES, t=PACK)
         xm_raw = []
@@ -104,211 +85,226 @@ def tile_attend_gkl_w_clip_kernel(tc, xT, wT, y, wt, xn, xm, offs, out):
             nc.sync.dma_start(raw[:], xm_rows[:, g, :, :])
             xm_raw.append(raw)
 
-        minus_half = sb([P, PACK], F32, "minus_half")
-        ones = sb([P, PACK], F32, "ones")
-        nc.gpsimd.memset(ones[:], 1.0)
-        nc.scalar.activation(minus_half[:], ones[:], ACT.Copy, scale=-0.5)
+        minus_half = sb([P, 1], F32, "minus_half")
+        plus_half = sb([P, TILES], F32, "plus_half")
+        nc.gpsimd.memset(plus_half[:], 0.5)
+        nc.scalar.activation(minus_half[:], plus_half[:, 0:1], ACT.Copy, scale=-1.0)
 
         windows = []
         for k in range(WINDOWS):
             window = sb([P, T], F32, f"window{k}")
-            engine = nc.vector if k < WINDOWS_ON_VECTOR else nc.gpsimd
-            engine.memset(window[:], 0.0)
+            nc.vector.memset(window[:], 0.0)
             windows.append(window)
 
-        w_picked = sb([P, PACK, N], F32, "w_picked")
-        for j in range(PACK):
-            nc.vector.tensor_copy(w_picked[:, j, :], w_plane[j][:].indirect(offsets[:]))
+        xn_cut = sb([P, TILES], F32, "xn_cut")
+        nc.gpsimd.tensor_scalar(
+            xn_cut[:], xn_sb[:].rearrange("p g t -> p (g t)"), 1.0 / (CLIP * CLIP), 0.0, ALU.mult, ALU.add
+        )
+        length = sb([P, TILES], F32, "length")
+        nc.gpsimd.tensor_tensor(length[:], xn_cut[:], plus_half[:], ALU.pow)
+
         w_bf = sb([P, N, PACK], BF16, "w_bf")
-        for slots, on_vector in ((slice(0, W_VECTOR), True), (slice(W_VECTOR, N), False)):
-            copy(
-                on_vector,
-                w_bf[:, slots, :].rearrange("p (c i) j -> p c j i", i=RUN),
-                w_picked[:, :, slots].rearrange("p j (c i) -> p c j i", i=RUN),
-            )
+        for j in range(PACK):
+            nc.vector.tensor_copy(w_bf[:, :, j], w_plane[j][:].indirect(offsets[:]))
         w_codes = sb([P, N], U32, "w_codes")
         w_scales = sb([P, N], U8, "w_scales")
         nc.vector.quantize_mx(
             out=w_codes[:].bitcast(E4M3), scales=w_scales[:], in_=w_bf[:].rearrange("p i j -> p (i j)")
         )
 
-        x_codes = sb([P, PASSES, PACK, P], U32, "x_codes")
-        x_scales = sb([P, PASSES, PACK, P], U8, "x_scales")
-        x_bf = {}
+        x_codes = sb([P, TILES, P], U32, "x_codes")
+        x_scales = sb([P, TILES, P], U8, "x_scales")
         scores = {}
-        e = {}
-        root = {}
-        diff = [sb([P, PACK, N], F32, f"diff{g}") for g in range(PASSES)]
-        sums = [sb([P, PACK], F32, f"sums{g}") for g in range(PASSES)]
-        sumsq = [sb([P, PACK], F32, f"sumsq{g}") for g in range(PASSES)]
 
-        def weave_x(g, m0, m1, raw, on_vector):
-            dst = x_bf[g][:, :, m0:m1, :]
-            if on_vector:
-                nc.vector.tensor_copy(
-                    dst.rearrange("p (u t) m j -> p u m j t", u=2),
-                    raw.rearrange("p j (m u t) -> p u m j t", u=2, t=2),
-                )
-            else:
-                nc.scalar.activation(
-                    dst.rearrange("p t m j -> p m j t"), raw.rearrange("p j (m t) -> p m j t", t=PACK), ACT.Copy
-                )
-
-        def quantize_x(g, t0, t1):
+        def quantize_x(k0, k1, woven):
             nc.vector.quantize_mx(
-                out=x_codes[:, g, t0:t1, :].rearrange("p t m -> p (t m)").bitcast(E4M3),
-                scales=x_scales[:, g, t0:t1, :].rearrange("p t m -> p (t m)"),
-                in_=x_bf[g][:, t0:t1, :, :].rearrange("p t m j -> p (t m j)"),
+                out=x_codes[:, k0:k1, :].rearrange("p t m -> p (t m)").bitcast(E4M3),
+                scales=x_scales[:, k0:k1, :].rearrange("p t m -> p (t m)"),
+                in_=woven.rearrange("p t m j -> p (t m j)"),
             )
 
-        def score(g, t):
-            scores[g, t] = psum.tile([P, N], F32, name=f"scores{g}_{t}", tag=f"bank{PACK * g + t}")
+        def score(k):
+            scores[k] = psum.tile([P, N], F32, name=f"scores{k}", tag=f"bank{k}")
             nc.tensor.matmul_mx(
-                out=scores[g, t][:],
-                lhsT=x_codes[:, g, t, :].bitcast(E4M3),
-                lhsT_scale=x_scales[:, g, t, :],
+                out=scores[k][:],
+                lhsT=x_codes[:, k, :].bitcast(E4M3),
+                lhsT_scale=x_scales[:, k, :],
                 rhs=w_codes[:].bitcast(E4M3),
                 rhs_scale=w_scales[:],
                 start=True,
                 stop=True,
             )
 
-        def exponentials(g):
-            for t in range(PACK):
-                neg_max = sb([P, 1], F32, f"neg_max{g}_{t}")
-                nc.vector.tensor_reduce(neg_max[:], scores[g, t][:], AXIS.X, ALU.max, negate=True)
-                e[g, t] = sb([P, N], F32, f"e{g}_{t}")
-                nc.scalar.activation(
-                    e[g, t][:], scores[g, t][:], ACT.Exp, bias=neg_max[:], accum_out=sums[g][:, t : t + 1]
-                )
-
-        def differences(g):
-            for t in range(PACK):
-                rows = diff[g][:, t, :]
-                total = sumsq[g][:, t : t + 1]
-                nc.vector.scalar_tensor_tensor(
-                    rows, y_sb[g, t], sums[g][:, t : t + 1], e[g, t][:], ALU.mult, ALU.subtract
-                )
-                if (g, t) == SQUARES_ON_VECTOR:
-                    nc.vector.scalar_tensor_tensor(
-                        e[g, t][:], rows, 1.0 / (CLIP * CLIP), rows, ALU.mult, ALU.mult, accum_out=total
-                    )
+        cols = P // 2
+        x_bf0 = []
+        for u in range(2):
+            woven = sb([P, 2, P, PACK], BF16, f"x_bf0_{u}")
+            x_bf0.append(woven)
+            for h in range(2):
+                dst = woven[:, :, h * cols : (h + 1) * cols, :].rearrange("p t m j -> p m j t")
+                raw = x_raw[0, h][:].rearrange("p j (m t) -> p m j t", t=PACK)[:, :, :, 2 * u : 2 * u + 2]
+                if u == 0:
+                    nc.scalar.activation(dst, raw, ACT.Copy)
                 else:
-                    nc.scalar.activation(e[g, t][:], rows, ACT.Square, scale=1.0 / CLIP, accum_out=total)
-
-        def row_roots(g):
-            sums_sq = sb([P, PACK], F32, f"sums_sq{g}")
-            nc.vector.tensor_tensor(sums_sq[:], sums[g][:], sums[g][:], ALU.mult)
-            larger = sb([P, PACK], F32, f"larger{g}")
-            for t in range(PACK):
-                col = slice(t, t + 1)
-                nc.vector.tensor_scalar(
-                    larger[:, col], sumsq[g][:, col], xn_sb[:, g, col], sums_sq[:, col], ALU.mult, ALU.max
-                )
-            root[g] = sb([P, PACK], F32, f"root{g}")
-            nc.gpsimd.tensor_tensor(root[g][:], larger[:], minus_half[:], ALU.pow)
-
-        x_bf[0] = sb([P, PACK, P, PACK], BF16, "x_bf0")
-        weave_x(0, X0_VECTOR, P, x_raw0[:, :, PACK * X0_VECTOR :], False)
-        weave_x(0, 0, X0_VECTOR, x_raw0[:, :, 0 : PACK * X0_VECTOR], True)
-        for t in range(PACK):
-            quantize_x(0, t, t + 1)
-            score(0, t)
-        x_bf[1] = sb([P, PACK, P, PACK], BF16, "x_bf1")
+                    nc.vector.tensor_copy(dst, raw)
+        quantize_x(0, 1, x_bf0[0][:, 0:1, :, :])
+        score(0)
+        quantize_x(1, 2, x_bf0[0][:, 1:2, :, :])
+        score(1)
+        quantize_x(2, 4, x_bf0[1][:])
+        score(2)
+        score(3)
+        x_bf1 = sb([P, PACK, P, PACK], BF16, "x_bf1")
         for h in range(2):
-            weave_x(1, h * (P // 2), (h + 1) * (P // 2), x_raw1[h][:], False)
-        exponentials(0)
-        quantize_x(1, 0, PACK)
-        for t in range(PACK):
-            score(1, t)
-        differences(0)
-        row_roots(0)
-        exponentials(1)
-        differences(1)
-        row_roots(1)
-
-        g_codes = sb([P, PASSES, N], U32, "g_codes")
-        g_scales = sb([P, PASSES, N], U8, "g_scales")
-        g_rows = {}
-        g_bf = {}
-
-        def scale_rows(g):
-            g_rows[g] = sb([P, PACK, N], BF16, f"g_rows{g}")
-            for t in range(PACK):
-                col = slice(t, t + 1)
-                nc.vector.tensor_scalar(
-                    g_rows[g][:, t, :], diff[g][:, t, :], root[g][:, col], wt_sb[:, g, col], ALU.mult, ALU.mult
-                )
-            g_bf[g] = sb([P, N, PACK], BF16, f"g_bf{g}")
-
-        scale_rows(1)
-        for slots, on_vector in ((slice(0, G1_VECTOR), True), (slice(G1_VECTOR, N), False)):
-            copy(
-                on_vector,
-                g_bf[1][:, slots, :].rearrange("p (c i) t -> p c t i", i=RUN),
-                g_rows[1][:, :, slots].rearrange("p t (c i) -> p c t i", i=RUN),
+            nc.scalar.activation(
+                x_bf1[:, :, h * cols : (h + 1) * cols, :].rearrange("p t m j -> p m j t"),
+                x_raw[1, h][:].rearrange("p j (m t) -> p m j t", t=PACK),
+                ACT.Copy,
             )
-        scale_rows(0)
-        for slots, on_vector in ((slice(0, G0_VECTOR), True), (slice(G0_VECTOR, N), False)):
-            copy(on_vector, g_bf[0][:, slots, :], g_rows[0][:, :, slots].rearrange("p t i -> p i t"))
-        for g in (1, 0):
+
+        diff = [sb([P, N], F32, f"diff{k}") for k in range(TILES)]
+        e = [sb([P, N], F32, f"e{k}") for k in range(TILES)]
+        sums = sb([P, TILES], F32, "sums")
+        sumsq = sb([P, TILES], F32, "sumsq")
+        larger = sb([P, TILES], F32, "larger")
+        root = sb([P, TILES], F32, "root")
+        wt_cols = wt_sb[:].rearrange("p g t -> p (g t)")
+
+        def exponential(k):
+            neg_max = sb([P, 1], F32, f"neg_max{k}")
+            nc.vector.tensor_reduce(neg_max[:], scores[k][:], AXIS.X, ALU.max, negate=True)
+            nc.scalar.activation(e[k][:], scores[k][:], ACT.Exp, bias=neg_max[:], accum_out=sums[:, k : k + 1])
+
+        def difference(k):
+            col = slice(k, k + 1)
+            nc.vector.scalar_tensor_tensor(diff[k][:], y_sb[k], sums[:, col], e[k][:], ALU.mult, ALU.subtract)
+            nc.scalar.activation(e[k][:], diff[k][:], ACT.Square, scale=length[:, col], accum_out=sumsq[:, col])
+
+        def row_root(k0, k1):
+            for k in range(k0, k1):
+                col = slice(k, k + 1)
+                nc.vector.tensor_scalar(
+                    larger[:, col], sums[:, col], sums[:, col], sumsq[:, col], ALU.mult, ALU.max
+                )
+            nc.gpsimd.tensor_tensor(
+                root[:, k0:k1], larger[:, k0:k1], minus_half[:, 0 : k1 - k0], ALU.pow
+            )
+
+        exponential(0)
+        exponential(1)
+        for k in range(TILES):
+            difference(k)
+            if k == 0:
+                quantize_x(PACK, TILES, x_bf1[:])
+                for k1 in range(PACK, TILES):
+                    score(k1)
+            if k + 2 < TILES:
+                exponential(k + 2)
+            row_root(k, k + 1)
+
+        HALF = N // 2
+        G0_VECTOR = 128
+        halves = (slice(0, HALF), slice(HALF, N))
+        g_codes = [sb([P, N], U32, f"g_codes{g}") for g in range(PASSES)]
+        g_scales = [sb([P, N], U8, f"g_scales{g}") for g in range(PASSES)]
+        nc.vector.memset(g_codes[1][:, halves[1]], 0)
+        nc.vector.memset(g_scales[1][:, halves[1]], 0)
+        g_rows = sb([P, PASSES, PACK, N], BF16, "g_rows")
+        g_bf = [sb([P, N, PACK], BF16, f"g_bf{g}") for g in range(PASSES)]
+
+        def scale_rows(g, slots):
+            for t in range(PACK):
+                k = PACK * g + t
+                col = slice(k, k + 1)
+                nc.vector.tensor_scalar(
+                    g_rows[:, g, t, slots], diff[k][:, slots], root[:, col], wt_cols[:, col], ALU.mult, ALU.mult
+                )
+
+        def weave_g(g, slots, on_vector):
+            dst = g_bf[g][:, slots, :].rearrange("p (c i) t -> p c t i", i=RUN)
+            rows = g_rows[:, g, :, slots].rearrange("p t (c i) -> p c t i", i=RUN)
+            if on_vector:
+                nc.vector.tensor_copy(dst, rows)
+            else:
+                nc.scalar.copy(dst, rows)
+
+        def quantize_g(g, slots):
             nc.vector.quantize_mx(
-                out=g_codes[:, g, :].bitcast(E5M2),
-                scales=g_scales[:, g, :],
-                in_=g_bf[g][:].rearrange("p i t -> p (i t)"),
+                out=g_codes[g][:, slots].bitcast(E5M2),
+                scales=g_scales[g][:, slots],
+                in_=g_bf[g][:, slots, :].rearrange("p i t -> p (i t)"),
             )
 
         m_codes = sb([P, D_BLOCKS * PASSES, P], U32, "m_codes")
         m_scales = sb([P, D_BLOCKS * PASSES, P], U8, "m_scales")
-        m_bf = {}
-        dw = {}
+        m_bf = sb([P, D_BLOCKS * PASSES, P, PACK], BF16, "m_bf")
 
-        def weave_m(units, on_vector):
-            m_bf[units] = sb([P, len(units), P, PACK], BF16, f"m_bf{units.start}")
-            for u in units:
-                b, g = divmod(u, PASSES)
-                copy(
-                    on_vector,
-                    m_bf[units][:, u - units.start, :, :].rearrange("p (c i) t -> p c t i", i=RUN),
+        def weave_m(b):
+            for g in range(PASSES):
+                nc.scalar.copy(
+                    m_bf[:, PASSES * b + g, :, :].rearrange("p (c i) t -> p c t i", i=RUN),
                     xm_raw[g][:, :, b * P : (b + 1) * P].rearrange("p t (c i) -> p c t i", i=RUN),
                 )
 
-        def quantize_m(b):
-            for units in (M_FIRST, M_SECOND, M_THIRD):
-                u0, u1 = max(units.start, PASSES * b), min(units.stop, PASSES * (b + 1))
-                if u0 < u1:
-                    nc.vector.quantize_mx(
-                        out=m_codes[:, u0:u1, :].rearrange("p u m -> p (u m)").bitcast(E4M3),
-                        scales=m_scales[:, u0:u1, :].rearrange("p u m -> p (u m)"),
-                        in_=m_bf[units][:, u0 - units.start : u1 - units.start, :, :].rearrange("p u m t -> p (u m t)"),
-                    )
+        def quantize_m(b0, b1):
+            u0, u1 = PASSES * b0, PASSES * b1
+            nc.vector.quantize_mx(
+                out=m_codes[:, u0:u1, :].rearrange("p u m -> p (u m)").bitcast(E4M3),
+                scales=m_scales[:, u0:u1, :].rearrange("p u m -> p (u m)"),
+                in_=m_bf[:, u0:u1, :, :].rearrange("p u m t -> p (u m t)"),
+            )
 
-        def multiply(b):
-            acc = psum.tile([P, N], F32, name=f"acc{b}", tag=f"bank{b}")
+        def multiply(b, slots, bank, name):
+            acc = psum.tile([P, N], F32, name=f"acc_{name}", tag=f"bank{bank}")
             for g in range(PASSES):
                 nc.tensor.matmul_mx(
                     out=acc[:],
                     lhsT=m_codes[:, PASSES * b + g, :].bitcast(E4M3),
                     lhsT_scale=m_scales[:, PASSES * b + g, :],
-                    rhs=g_codes[:, g, :].bitcast(E5M2),
-                    rhs_scale=g_scales[:, g, :],
+                    rhs=g_codes[g][:].bitcast(E5M2),
+                    rhs_scale=g_scales[g][:],
                     start=(g == 0),
                     stop=(g == PASSES - 1),
                 )
-            dw[b] = sb([P, N], F32, f"dw{b}")
-            nc.scalar.activation(dw[b][:], acc[:], ACT.Copy, scale=-1.0)
+            sums_out = sb([P, slots.stop - slots.start], F32, name)
+            nc.scalar.activation(sums_out[:], acc[:, slots], ACT.Copy, scale=-1.0)
+            return sums_out
 
-        def place(b):
-            window = windows[b % WINDOWS]
-            nc.vector.tensor_copy(window[:].indirect(offsets[:]), dw[b][:])
-            nc.sync.dma_start(out[b * P : (b + 1) * P, :], window[:])
+        def scatter(b, slots, values):
+            listed = offsets[:, slots.start // LIST_GROUP : slots.stop // LIST_GROUP]
+            nc.vector.tensor_copy(windows[b % WINDOWS][:].indirect(listed), values[:])
 
-        weave_m(M_FIRST, False)
-        quantize_m(0)
-        multiply(0)
-        place(0)
-        weave_m(M_SECOND, False)
-        weave_m(M_THIRD, True)
-        for step in (quantize_m, multiply, place):
-            for b in range(1, D_BLOCKS):
-                step(b)
+        def store(b):
+            nc.sync.dma_start(out[b * P : (b + 1) * P, :], windows[b % WINDOWS][:])
+
+        whole = slice(0, N)
+        scale_rows(0, whole)
+        scale_rows(1, halves[0])
+        weave_m(0)
+        weave_g(0, slice(G0_VECTOR, N), False)
+        weave_g(1, halves[0], True)
+        weave_g(0, slice(0, G0_VECTOR), True)
+        quantize_m(0, 1)
+        quantize_g(0, whole)
+        quantize_g(1, halves[0])
+        early = multiply(0, halves[0], 0, "dw_early")
+        weave_m(1)
+        scale_rows(1, halves[1])
+        weave_g(1, halves[1], True)
+        quantize_g(1, halves[1])
+        late = multiply(0, halves[1], 1, "dw0")
+        quantize_m(1, 2)
+        scatter(0, halves[0], early)
+        scatter(0, halves[1], late)
+        store(0)
+        weave_m(2)
+        weave_m(3)
+        dw = {1: multiply(1, whole, 2, "dw1")}
+        quantize_m(2, 4)
+        scatter(1, whole, dw[1])
+        store(1)
+        for b in (2, 3):
+            dw[b] = multiply(b, whole, b + 1, f"dw{b}")
+        for b in (2, 3):
+            scatter(b, whole, dw[b])
+            store(b)

@@ -38,9 +38,13 @@ def tile_attend_gkl_w_clip_kernel(tc, xT, wT, y, wt, xn, xm, offs, out):
         follows = {
             "x_bf0_1": "w_bf",
             "x_bf1": "x_raw0_1",
+            "neg_max6": "sumsq0",
+            "neg_max7": "sums_sq0",
             "g_rows": "y_pair1_2",
+            "g_bf0": "sumsq1",
             "m_bf": f"e{TILES - 1}",
-            "dw1": "xm_raw1",
+            "early1": "y_pair1_2",
+            "dw2": "xm_raw1",
         }
 
         def sb(shape, dtype, name):
@@ -48,8 +52,6 @@ def tile_attend_gkl_w_clip_kernel(tc, xT, wT, y, wt, xn, xm, offs, out):
 
         xn_sb = sb([P, PASSES, PACK], F32, "xn_sb")
         wt_sb = sb([P, PASSES, PACK], F32, "wt_sb")
-        nc.scalar.dma_start(xn_sb[:], xn.rearrange("b (g p t) o -> p (b g) (t o)", g=PASSES, t=PACK))
-        nc.scalar.dma_start(wt_sb[:], wt.rearrange("b (g p t) o -> p (b g) (t o)", g=PASSES, t=PACK))
 
         offsets = keep.tile([P, N // LIST_GROUP], U16, name="offsets")
         w_rows = wT.rearrange("(p j) c -> p j c", j=PACK)
@@ -77,6 +79,9 @@ def tile_attend_gkl_w_clip_kernel(tc, xT, wT, y, wt, xn, xm, offs, out):
                 pair = sb([P, 2, N], F32, f"y_pair{g}_{t0}")
                 nc.sync.dma_start(pair[:], y_rows[:, g, t0 : t0 + 2, :])
                 y_sb.extend([pair[:, 0, :], pair[:, 1, :]])
+            if g == 0:
+                nc.sync.dma_start(xn_sb[:], xn.rearrange("b (g p t) o -> p (b g) (t o)", g=PASSES, t=PACK))
+                nc.sync.dma_start(wt_sb[:], wt.rearrange("b (g p t) o -> p (b g) (t o)", g=PASSES, t=PACK))
 
         xm_rows = xm.rearrange("b (g p t) d -> p (b g) t d", g=PASSES, t=PACK)
         xm_raw = []
@@ -85,23 +90,17 @@ def tile_attend_gkl_w_clip_kernel(tc, xT, wT, y, wt, xn, xm, offs, out):
             nc.sync.dma_start(raw[:], xm_rows[:, g, :, :])
             xm_raw.append(raw)
 
-        minus_half = sb([P, 1], F32, "minus_half")
-        plus_half = sb([P, TILES], F32, "plus_half")
-        nc.gpsimd.memset(plus_half[:], 0.5)
-        nc.scalar.activation(minus_half[:], plus_half[:, 0:1], ACT.Copy, scale=-1.0)
+        minus_half = sb([P, PACK], F32, "minus_half")
+        ones = sb([P, PACK], F32, "ones")
+        nc.gpsimd.memset(ones[:], 1.0)
+        nc.scalar.activation(minus_half[:], ones[:], ACT.Copy, scale=-0.5)
 
         windows = []
         for k in range(WINDOWS):
             window = sb([P, T], F32, f"window{k}")
-            nc.vector.memset(window[:], 0.0)
+            engine = nc.vector if k < 2 else nc.gpsimd
+            engine.memset(window[:], 0.0)
             windows.append(window)
-
-        xn_cut = sb([P, TILES], F32, "xn_cut")
-        nc.gpsimd.tensor_scalar(
-            xn_cut[:], xn_sb[:].rearrange("p g t -> p (g t)"), 1.0 / (CLIP * CLIP), 0.0, ALU.mult, ALU.add
-        )
-        length = sb([P, TILES], F32, "length")
-        nc.gpsimd.tensor_tensor(length[:], xn_cut[:], plus_half[:], ALU.pow)
 
         w_bf = sb([P, N, PACK], BF16, "w_bf")
         for j in range(PACK):
@@ -164,31 +163,32 @@ def tile_attend_gkl_w_clip_kernel(tc, xT, wT, y, wt, xn, xm, offs, out):
 
         diff = [sb([P, N], F32, f"diff{k}") for k in range(TILES)]
         e = [sb([P, N], F32, f"e{k}") for k in range(TILES)]
-        sums = sb([P, TILES], F32, "sums")
-        sumsq = sb([P, TILES], F32, "sumsq")
-        larger = sb([P, TILES], F32, "larger")
-        root = sb([P, TILES], F32, "root")
-        wt_cols = wt_sb[:].rearrange("p g t -> p (g t)")
+        sums = [sb([P, PACK], F32, f"sums{g}") for g in range(PASSES)]
+        sumsq = [sb([P, PACK], F32, f"sumsq{g}") for g in range(PASSES)]
+        root = [sb([P, PACK], F32, f"root{g}") for g in range(PASSES)]
 
         def exponential(k):
+            g, t = divmod(k, PACK)
             neg_max = sb([P, 1], F32, f"neg_max{k}")
             nc.vector.tensor_reduce(neg_max[:], scores[k][:], AXIS.X, ALU.max, negate=True)
-            nc.scalar.activation(e[k][:], scores[k][:], ACT.Exp, bias=neg_max[:], accum_out=sums[:, k : k + 1])
+            nc.scalar.activation(e[k][:], scores[k][:], ACT.Exp, bias=neg_max[:], accum_out=sums[g][:, t : t + 1])
 
         def difference(k):
-            col = slice(k, k + 1)
-            nc.vector.scalar_tensor_tensor(diff[k][:], y_sb[k], sums[:, col], e[k][:], ALU.mult, ALU.subtract)
-            nc.scalar.activation(e[k][:], diff[k][:], ACT.Square, scale=length[:, col], accum_out=sumsq[:, col])
+            g, t = divmod(k, PACK)
+            col = slice(t, t + 1)
+            nc.vector.scalar_tensor_tensor(diff[k][:], y_sb[k], sums[g][:, col], e[k][:], ALU.mult, ALU.subtract)
+            nc.scalar.activation(e[k][:], diff[k][:], ACT.Square, scale=1.0 / CLIP, accum_out=sumsq[g][:, col])
 
-        def row_root(k0, k1):
-            for k in range(k0, k1):
-                col = slice(k, k + 1)
+        def row_roots(g):
+            sums_sq = sb([P, PACK], F32, f"sums_sq{g}")
+            nc.vector.tensor_tensor(sums_sq[:], sums[g][:], sums[g][:], ALU.mult)
+            larger = sb([P, PACK], F32, f"larger{g}")
+            for t in range(PACK):
+                col = slice(t, t + 1)
                 nc.vector.tensor_scalar(
-                    larger[:, col], sums[:, col], sums[:, col], sumsq[:, col], ALU.mult, ALU.max
+                    larger[:, col], sumsq[g][:, col], xn_sb[:, g, col], sums_sq[:, col], ALU.mult, ALU.max
                 )
-            nc.gpsimd.tensor_tensor(
-                root[:, k0:k1], larger[:, k0:k1], minus_half[:, 0 : k1 - k0], ALU.pow
-            )
+            nc.gpsimd.tensor_tensor(root[g][:], larger[:], minus_half[:], ALU.pow)
 
         exponential(0)
         exponential(1)
@@ -198,26 +198,27 @@ def tile_attend_gkl_w_clip_kernel(tc, xT, wT, y, wt, xn, xm, offs, out):
                 quantize_x(PACK, TILES, x_bf1[:])
                 for k1 in range(PACK, TILES):
                     score(k1)
+            if k % PACK == PACK - 1:
+                row_roots(k // PACK)
             if k + 2 < TILES:
                 exponential(k + 2)
-            row_root(k, k + 1)
 
         HALF = N // 2
-        G0_VECTOR = 128
         halves = (slice(0, HALF), slice(HALF, N))
         g_codes = [sb([P, N], U32, f"g_codes{g}") for g in range(PASSES)]
         g_scales = [sb([P, N], U8, f"g_scales{g}") for g in range(PASSES)]
-        nc.vector.memset(g_codes[1][:, halves[1]], 0)
-        nc.vector.memset(g_scales[1][:, halves[1]], 0)
+        for g in range(PASSES):
+            nc.vector.memset(g_codes[g][:, halves[1]], 0)
+            nc.vector.memset(g_scales[g][:, halves[1]], 0)
         g_rows = sb([P, PASSES, PACK, N], BF16, "g_rows")
         g_bf = [sb([P, N, PACK], BF16, f"g_bf{g}") for g in range(PASSES)]
 
         def scale_rows(g, slots):
             for t in range(PACK):
                 k = PACK * g + t
-                col = slice(k, k + 1)
+                col = slice(t, t + 1)
                 nc.vector.tensor_scalar(
-                    g_rows[:, g, t, slots], diff[k][:, slots], root[:, col], wt_cols[:, col], ALU.mult, ALU.mult
+                    g_rows[:, g, t, slots], diff[k][:, slots], root[g][:, col], wt_sb[:, g, col], ALU.mult, ALU.mult
                 )
 
         def weave_g(g, slots, on_vector):
@@ -278,33 +279,39 @@ def tile_attend_gkl_w_clip_kernel(tc, xT, wT, y, wt, xn, xm, offs, out):
             nc.sync.dma_start(out[b * P : (b + 1) * P, :], windows[b % WINDOWS][:])
 
         whole = slice(0, N)
-        scale_rows(0, whole)
-        scale_rows(1, halves[0])
+        first, second = halves
+        for g in range(PASSES):
+            scale_rows(g, first)
         weave_m(0)
-        weave_g(0, slice(G0_VECTOR, N), False)
-        weave_g(1, halves[0], True)
-        weave_g(0, slice(0, G0_VECTOR), True)
+        one_port = slice(0, 223)
+        nc.vector.tensor_copy(g_bf[0][:, one_port, :], g_rows[:, 0, :, one_port].rearrange("p t i -> p i t"))
+        rest = slice(223, HALF)
+        nc.scalar.copy(g_bf[0][:, rest, :], g_rows[:, 0, :, rest].rearrange("p t i -> p i t"))
         quantize_m(0, 1)
-        quantize_g(0, whole)
-        quantize_g(1, halves[0])
-        early = multiply(0, halves[0], 0, "dw_early")
+        weave_g(1, first, True)
+        for g in range(PASSES):
+            quantize_g(g, first)
         weave_m(1)
-        scale_rows(1, halves[1])
-        weave_g(1, halves[1], True)
-        quantize_g(1, halves[1])
-        late = multiply(0, halves[1], 1, "dw0")
+        early = [multiply(0, first, 0, "early0")]
+        for g in range(PASSES):
+            scale_rows(g, second)
         quantize_m(1, 2)
-        scatter(0, halves[0], early)
-        scatter(0, halves[1], late)
-        store(0)
-        weave_m(2)
-        weave_m(3)
-        dw = {1: multiply(1, whole, 2, "dw1")}
-        quantize_m(2, 4)
-        scatter(1, whole, dw[1])
-        store(1)
+        weave_g(0, second, False)
+        quantize_g(0, second)
+        weave_g(1, second, False)
+        early.append(multiply(1, first, 1, "early1"))
+        scatter(0, first, early[0])
+        quantize_g(1, second)
+        scatter(1, first, early[1])
+        late = [multiply(b, second, 2 + b, f"late{b}") for b in range(2)]
+        for b in range(2):
+            weave_m(2 + b)
+            quantize_m(2 + b, 3 + b)
+            scatter(b, second, late[b])
+            store(b)
+        dw = {}
         for b in (2, 3):
-            dw[b] = multiply(b, whole, b + 1, f"dw{b}")
+            dw[b] = multiply(b, whole, b + 2, f"dw{b}")
         for b in (2, 3):
             scatter(b, whole, dw[b])
             store(b)

@@ -36,22 +36,33 @@ def tile_attend_gkl_w_clip_kernel(tc, xT, wT, y, wt, xn, xm, offs, out):
         psum = ctx.enter_context(tc.psum_pool(name="psum", bufs=1))
 
         follows = {
-            "x_bf0_1": "w_bf",
-            "x_bf1": "x_raw0_1",
+            "x_raw0_1": "w_plane0",
+            "x_raw1_0": "w_plane1",
+            "x_raw1_1": "w_bf",
+            "y_pair0_0": "x_raw0_1",
+            "y_pair0_2": "x_bf0_0",
+            "xn_sb": "x_bf0_1",
+            "y_pair1_0": "neg_max0",
+            "y_pair1_2": "neg_max1",
+            "wt_sb": "neg_max2",
+            "xm_raw0": "neg_max3",
+            "xm_raw1": "y_pair0_2",
+            "m_bf3": "g_bf1",
             "neg_max6": "sumsq0",
             "neg_max7": "sums_sq0",
             "g_rows": "y_pair1_2",
             "g_bf0": "sumsq1",
-            "m_bf": f"e{TILES - 1}",
-            "early1": "y_pair1_2",
-            "dw2": "xm_raw1",
+            "m_bf0": f"e{TILES - 1}",
+            "dw1": "xm_raw1",
+            "dw2": "m_bf3",
         }
 
-        def sb(shape, dtype, name):
-            return keep.tile(shape, dtype, name=name, tag=follows.get(name, name), align_bytes=64)
+        def slot_of(name):
+            return slot_of(follows[name]) if name in follows else name
 
-        xn_sb = sb([P, PASSES, PACK], F32, "xn_sb")
-        wt_sb = sb([P, PASSES, PACK], F32, "wt_sb")
+        def sb(shape, dtype, name):
+            return keep.tile(shape, dtype, name=name, tag=slot_of(name), align_bytes=64)
+
 
         offsets = keep.tile([P, N // LIST_GROUP], U16, name="offsets")
         w_rows = wT.rearrange("(p j) c -> p j c", j=PACK)
@@ -66,29 +77,35 @@ def tile_attend_gkl_w_clip_kernel(tc, xT, wT, y, wt, xn, xm, offs, out):
         x_rows = xT.rearrange("b (p j) r -> p (b j) r", j=PACK)
         half = K_PASS // 2
         x_raw = {}
-        for g in range(PASSES):
-            for h in range(2):
-                x_raw[g, h] = sb([P, PACK, half], F32, f"x_raw{g}_{h}")
-                c0 = g * K_PASS + h * half
-                nc.sync.dma_start(x_raw[g, h][:], x_rows[:, :, c0 : c0 + half])
-
         y_rows = y.rearrange("b (g p t) i -> p (b g) t i", g=PASSES, t=PACK)
         y_sb = []
-        for g in range(PASSES):
-            for t0 in range(0, PACK, 2):
-                pair = sb([P, 2, N], F32, f"y_pair{g}_{t0}")
-                nc.sync.dma_start(pair[:], y_rows[:, g, t0 : t0 + 2, :])
-                y_sb.extend([pair[:, 0, :], pair[:, 1, :]])
-            if g == 0:
-                nc.sync.dma_start(xn_sb[:], xn.rearrange("b (g p t) o -> p (b g) (t o)", g=PASSES, t=PACK))
-                nc.sync.dma_start(wt_sb[:], wt.rearrange("b (g p t) o -> p (b g) (t o)", g=PASSES, t=PACK))
+        cols = P // 2
+        x_bf = {}
+
+        def load_x(g, h):
+            x_raw[g, h] = sb([P, PACK, half], F32, f"x_raw{g}_{h}")
+            c0 = g * K_PASS + h * half
+            nc.sync.dma_start(x_raw[g, h][:], x_rows[:, :, c0 : c0 + half])
+
+        def load_y(g, t0):
+            pair = sb([P, 2, N], F32, f"y_pair{g}_{t0}")
+            nc.sync.dma_start(pair[:], y_rows[:, g, t0 : t0 + 2, :])
+            y_sb.extend([pair[:, 0, :], pair[:, 1, :]])
 
         xm_rows = xm.rearrange("b (g p t) d -> p (b g) t d", g=PASSES, t=PACK)
         xm_raw = []
-        for g in range(PASSES):
+
+        def load_column(name, values):
+            tile_sb = sb([P, PASSES, PACK], F32, name)
+            nc.sync.dma_start(tile_sb[:], values.rearrange("b (g p t) o -> p (b g) (t o)", g=PASSES, t=PACK))
+            return tile_sb
+
+        def load_xm(g):
             raw = sb([P, PACK, D], F32, f"xm_raw{g}")
             nc.sync.dma_start(raw[:], xm_rows[:, g, :, :])
             xm_raw.append(raw)
+
+        load_x(0, 0)
 
         minus_half = sb([P, PACK], F32, "minus_half")
         ones = sb([P, PACK], F32, "ones")
@@ -134,32 +151,35 @@ def tile_attend_gkl_w_clip_kernel(tc, xT, wT, y, wt, xn, xm, offs, out):
                 stop=True,
             )
 
-        cols = P // 2
-        x_bf0 = []
-        for u in range(2):
-            woven = sb([P, 2, P, PACK], BF16, f"x_bf0_{u}")
-            x_bf0.append(woven)
-            for h in range(2):
-                dst = woven[:, :, h * cols : (h + 1) * cols, :].rearrange("p t m j -> p m j t")
-                raw = x_raw[0, h][:].rearrange("p j (m t) -> p m j t", t=PACK)[:, :, :, 2 * u : 2 * u + 2]
-                if u == 0:
-                    nc.scalar.activation(dst, raw, ACT.Copy)
-                else:
-                    nc.vector.tensor_copy(dst, raw)
-        quantize_x(0, 1, x_bf0[0][:, 0:1, :, :])
+        def weave_x(g, u, h, on_vector):
+            if (g, u) not in x_bf:
+                x_bf[g, u] = sb([P, 2, P, PACK], BF16, f"x_bf{g}_{u}")
+            dst = x_bf[g, u][:, :, h * cols : (h + 1) * cols, :].rearrange("p t m j -> p m j t")
+            raw = x_raw[g, h][:].rearrange("p j (m t) -> p m j t", t=PACK)[:, :, :, 2 * u : 2 * u + 2]
+            if on_vector:
+                nc.vector.tensor_copy(dst, raw)
+            else:
+                nc.scalar.activation(dst, raw, ACT.Copy)
+
+        load_x(0, 1)
+        load_x(1, 0)
+        load_x(1, 1)
+        weave_x(0, 0, 0, False)
+        weave_x(0, 1, 0, False)
+        weave_x(0, 0, 1, False)
+        weave_x(0, 1, 1, True)
+        quantize_x(0, 1, x_bf[0, 0][:, 0:1, :, :])
         score(0)
-        quantize_x(1, 2, x_bf0[0][:, 1:2, :, :])
+        quantize_x(1, 2, x_bf[0, 0][:, 1:2, :, :])
         score(1)
-        quantize_x(2, 4, x_bf0[1][:])
+        quantize_x(2, 4, x_bf[0, 1][:])
         score(2)
         score(3)
-        x_bf1 = sb([P, PACK, P, PACK], BF16, "x_bf1")
-        for h in range(2):
-            nc.scalar.activation(
-                x_bf1[:, :, h * cols : (h + 1) * cols, :].rearrange("p t m j -> p m j t"),
-                x_raw[1, h][:].rearrange("p j (m t) -> p m j t", t=PACK),
-                ACT.Copy,
-            )
+        load_y(0, 0)
+        load_y(0, 2)
+        xn_sb = load_column("xn_sb", xn)
+        weave_x(1, 0, 0, False)
+        weave_x(1, 1, 0, False)
 
         diff = [sb([P, N], F32, f"diff{k}") for k in range(TILES)]
         e = [sb([P, N], F32, f"e{k}") for k in range(TILES)]
@@ -191,17 +211,33 @@ def tile_attend_gkl_w_clip_kernel(tc, xT, wT, y, wt, xn, xm, offs, out):
             nc.gpsimd.tensor_tensor(root[g][:], larger[:], minus_half[:], ALU.pow)
 
         exponential(0)
+        load_y(1, 0)
         exponential(1)
-        for k in range(TILES):
+        load_y(1, 2)
+        weave_x(1, 0, 1, False)
+        weave_x(1, 1, 1, True)
+        exponential(2)
+        wt_sb = load_column("wt_sb", wt)
+        difference(0)
+        for u in range(2):
+            quantize_x(PACK + 2 * u, PACK + 2 * u + 2, x_bf[1, u][:])
+            score(PACK + 2 * u)
+            score(PACK + 2 * u + 1)
+        exponential(3)
+        load_xm(0)
+        difference(1)
+        difference(2)
+        exponential(4)
+        difference(3)
+        load_xm(1)
+        row_roots(0)
+        exponential(5)
+        difference(4)
+        exponential(6)
+        exponential(7)
+        for k in range(5, TILES):
             difference(k)
-            if k == 0:
-                quantize_x(PACK, TILES, x_bf1[:])
-                for k1 in range(PACK, TILES):
-                    score(k1)
-            if k % PACK == PACK - 1:
-                row_roots(k // PACK)
-            if k + 2 < TILES:
-                exponential(k + 2)
+        row_roots(1)
 
         HALF = N // 2
         halves = (slice(0, HALF), slice(HALF, N))
@@ -238,12 +274,15 @@ def tile_attend_gkl_w_clip_kernel(tc, xT, wT, y, wt, xn, xm, offs, out):
 
         m_codes = sb([P, D_BLOCKS * PASSES, P], U32, "m_codes")
         m_scales = sb([P, D_BLOCKS * PASSES, P], U8, "m_scales")
-        m_bf = sb([P, D_BLOCKS * PASSES, P, PACK], BF16, "m_bf")
+        m_first = sb([P, D_BLOCKS - 1, PASSES, P, PACK], BF16, "m_bf0")
+        m_bf = {b: m_first[:, b, :, :, :] for b in range(D_BLOCKS - 1)}
 
         def weave_m(b):
+            if b not in m_bf:
+                m_bf[b] = sb([P, PASSES, P, PACK], BF16, f"m_bf{b}")[:]
             for g in range(PASSES):
                 nc.scalar.copy(
-                    m_bf[:, PASSES * b + g, :, :].rearrange("p (c i) t -> p c t i", i=RUN),
+                    m_bf[b][:, g, :, :].rearrange("p (c i) t -> p c t i", i=RUN),
                     xm_raw[g][:, :, b * P : (b + 1) * P].rearrange("p t (c i) -> p c t i", i=RUN),
                 )
 
@@ -252,7 +291,7 @@ def tile_attend_gkl_w_clip_kernel(tc, xT, wT, y, wt, xn, xm, offs, out):
             nc.vector.quantize_mx(
                 out=m_codes[:, u0:u1, :].rearrange("p u m -> p (u m)").bitcast(E4M3),
                 scales=m_scales[:, u0:u1, :].rearrange("p u m -> p (u m)"),
-                in_=m_bf[:, u0:u1, :, :].rearrange("p u m t -> p (u m t)"),
+                in_=m_bf[b0].rearrange("p u m t -> p (u m t)"),
             )
 
         def multiply(b, slots, bank, name):
@@ -292,26 +331,23 @@ def tile_attend_gkl_w_clip_kernel(tc, xT, wT, y, wt, xn, xm, offs, out):
         for g in range(PASSES):
             quantize_g(g, first)
         weave_m(1)
-        early = [multiply(0, first, 0, "early0")]
-        for g in range(PASSES):
-            scale_rows(g, second)
-        quantize_m(1, 2)
+        scale_rows(1, second)
+        early = multiply(0, first, 0, "early")
+        scale_rows(0, second)
         weave_g(0, second, False)
-        quantize_g(0, second)
         weave_g(1, second, False)
-        early.append(multiply(1, first, 1, "early1"))
-        scatter(0, first, early[0])
+        quantize_m(1, 2)
+        weave_m(2)
+        quantize_g(0, second)
+        quantize_m(2, 3)
         quantize_g(1, second)
-        scatter(1, first, early[1])
-        late = [multiply(b, second, 2 + b, f"late{b}") for b in range(2)]
-        for b in range(2):
-            weave_m(2 + b)
-            quantize_m(2 + b, 3 + b)
-            scatter(b, second, late[b])
-            store(b)
-        dw = {}
-        for b in (2, 3):
-            dw[b] = multiply(b, whole, b + 2, f"dw{b}")
-        for b in (2, 3):
-            scatter(b, whole, dw[b])
+        scatter(0, first, early)
+        late = multiply(0, second, 1, "late")
+        weave_m(3)
+        quantize_m(3, 4)
+        scatter(0, second, late)
+        store(0)
+        for b in range(1, D_BLOCKS):
+            values = multiply(b, whole, b + 1, f"dw{b}")
+            scatter(b, whole, values)
             store(b)

@@ -36,25 +36,25 @@ def tile_attend_gkl_w_clip_kernel(tc, xT, wT, y, wt, xn, xm, offs, out):
         psum = ctx.enter_context(tc.psum_pool(name="psum", bufs=1))
 
         follows = {
-            "x_raw0_1": "w_plane0",
-            "x_raw1_0": "w_plane1",
-            "x_raw1_1": "w_bf",
-            "y_pair0_0": "x_raw0_1",
+            "x_raw0": "w_plane0",
+            "x_raw1": "w_plane2",
+            "y_pair0_0": "w_bf",
             "y_pair0_2": "x_bf0_0",
-            "xn_sb": "x_bf0_1",
-            "y_pair1_0": "neg_max0",
-            "y_pair1_2": "neg_max1",
-            "wt_sb": "neg_max2",
+            "xn_sb": "x_raw0",
+            "x_bf1_1": "x_bf0_1",
+            "x_bf1_0": "neg_max0",
+            "y_pair1_0": "neg_max1",
+            "y_pair1_2": "neg_max2",
+            "wt_sb": "x_raw1",
             "xm_raw0": "neg_max3",
             "xm_raw1": "y_pair0_2",
-            "m_bf3": "g_bf1",
             "neg_max6": "sumsq0",
             "neg_max7": "sums_sq0",
             "g_rows": "y_pair1_2",
             "g_bf0": "sumsq1",
             "m_bf0": f"e{TILES - 1}",
-            "dw1": "xm_raw1",
-            "dw2": "m_bf3",
+            "m_bf2": "g_bf1",
+            "early1": "g_rows",
         }
 
         def slot_of(name):
@@ -82,10 +82,9 @@ def tile_attend_gkl_w_clip_kernel(tc, xT, wT, y, wt, xn, xm, offs, out):
         cols = P // 2
         x_bf = {}
 
-        def load_x(g, h):
-            x_raw[g, h] = sb([P, PACK, half], F32, f"x_raw{g}_{h}")
-            c0 = g * K_PASS + h * half
-            nc.sync.dma_start(x_raw[g, h][:], x_rows[:, :, c0 : c0 + half])
+        def load_x(g):
+            x_raw[g] = sb([P, PACK, K_PASS], F32, f"x_raw{g}")
+            nc.sync.dma_start(x_raw[g][:], x_rows[:, :, g * K_PASS : (g + 1) * K_PASS])
 
         def load_y(g, t0):
             pair = sb([P, 2, N], F32, f"y_pair{g}_{t0}")
@@ -105,7 +104,6 @@ def tile_attend_gkl_w_clip_kernel(tc, xT, wT, y, wt, xn, xm, offs, out):
             nc.sync.dma_start(raw[:], xm_rows[:, g, :, :])
             xm_raw.append(raw)
 
-        load_x(0, 0)
 
         minus_half = sb([P, PACK], F32, "minus_half")
         ones = sb([P, PACK], F32, "ones")
@@ -151,35 +149,29 @@ def tile_attend_gkl_w_clip_kernel(tc, xT, wT, y, wt, xn, xm, offs, out):
                 stop=True,
             )
 
-        def weave_x(g, u, h, on_vector):
+        def weave_x(g, u, ms, on_vector):
             if (g, u) not in x_bf:
                 x_bf[g, u] = sb([P, 2, P, PACK], BF16, f"x_bf{g}_{u}")
-            dst = x_bf[g, u][:, :, h * cols : (h + 1) * cols, :].rearrange("p t m j -> p m j t")
-            raw = x_raw[g, h][:].rearrange("p j (m t) -> p m j t", t=PACK)[:, :, :, 2 * u : 2 * u + 2]
+            dst = x_bf[g, u][:, :, ms, :].rearrange("p t m j -> p m j t")
+            raw = x_raw[g][:].rearrange("p j (m t) -> p m j t", t=PACK)[:, ms, :, 2 * u : 2 * u + 2]
             if on_vector:
                 nc.vector.tensor_copy(dst, raw)
             else:
                 nc.scalar.activation(dst, raw, ACT.Copy)
 
-        load_x(0, 1)
-        load_x(1, 0)
-        load_x(1, 1)
-        weave_x(0, 0, 0, False)
-        weave_x(0, 1, 0, False)
-        weave_x(0, 0, 1, False)
-        weave_x(0, 1, 1, True)
+        X0_VECTOR = 84
+        load_x(0)
+        load_x(1)
+        load_y(0, 0)
+        weave_x(0, 0, slice(X0_VECTOR, P), False)
+        weave_x(0, 0, slice(0, X0_VECTOR), True)
+        weave_x(0, 1, slice(0, P), False)
         quantize_x(0, 1, x_bf[0, 0][:, 0:1, :, :])
         score(0)
         quantize_x(1, 2, x_bf[0, 0][:, 1:2, :, :])
         score(1)
-        quantize_x(2, 4, x_bf[0, 1][:])
-        score(2)
-        score(3)
-        load_y(0, 0)
         load_y(0, 2)
         xn_sb = load_column("xn_sb", xn)
-        weave_x(1, 0, 0, False)
-        weave_x(1, 1, 0, False)
 
         diff = [sb([P, N], F32, f"diff{k}") for k in range(TILES)]
         e = [sb([P, N], F32, f"e{k}") for k in range(TILES)]
@@ -211,12 +203,15 @@ def tile_attend_gkl_w_clip_kernel(tc, xT, wT, y, wt, xn, xm, offs, out):
             nc.gpsimd.tensor_tensor(root[g][:], larger[:], minus_half[:], ALU.pow)
 
         exponential(0)
-        load_y(1, 0)
+        quantize_x(2, 4, x_bf[0, 1][:])
+        score(2)
+        score(3)
         exponential(1)
-        load_y(1, 2)
-        weave_x(1, 0, 1, False)
-        weave_x(1, 1, 1, True)
+        load_y(1, 0)
+        weave_x(1, 0, slice(0, P), False)
+        weave_x(1, 1, slice(0, P), True)
         exponential(2)
+        load_y(1, 2)
         wt_sb = load_column("wt_sb", wt)
         difference(0)
         for u in range(2):
@@ -274,12 +269,12 @@ def tile_attend_gkl_w_clip_kernel(tc, xT, wT, y, wt, xn, xm, offs, out):
 
         m_codes = sb([P, D_BLOCKS * PASSES, P], U32, "m_codes")
         m_scales = sb([P, D_BLOCKS * PASSES, P], U8, "m_scales")
-        m_first = sb([P, D_BLOCKS - 1, PASSES, P, PACK], BF16, "m_bf0")
-        m_bf = {b: m_first[:, b, :, :, :] for b in range(D_BLOCKS - 1)}
+        m_bf = {}
 
         def weave_m(b):
             if b not in m_bf:
-                m_bf[b] = sb([P, PASSES, P, PACK], BF16, f"m_bf{b}")[:]
+                pair = sb([P, 2, PASSES, P, PACK], BF16, f"m_bf{b}")
+                m_bf[b], m_bf[b + 1] = pair[:, 0, :, :, :], pair[:, 1, :, :, :]
             for g in range(PASSES):
                 nc.scalar.copy(
                     m_bf[b][:, g, :, :].rearrange("p (c i) t -> p c t i", i=RUN),
@@ -331,23 +326,24 @@ def tile_attend_gkl_w_clip_kernel(tc, xT, wT, y, wt, xn, xm, offs, out):
         for g in range(PASSES):
             quantize_g(g, first)
         weave_m(1)
-        scale_rows(1, second)
-        early = multiply(0, first, 0, "early")
+        early = [multiply(0, first, 0, "early0")]
         scale_rows(0, second)
+        scale_rows(1, second)
         weave_g(0, second, False)
-        weave_g(1, second, False)
         quantize_m(1, 2)
-        weave_m(2)
         quantize_g(0, second)
-        quantize_m(2, 3)
+        weave_g(1, second, False)
+        early.append(multiply(1, first, 1, "early1"))
+        scatter(0, first, early[0])
         quantize_g(1, second)
-        scatter(0, first, early)
-        late = multiply(0, second, 1, "late")
-        weave_m(3)
-        quantize_m(3, 4)
-        scatter(0, second, late)
-        store(0)
-        for b in range(1, D_BLOCKS):
-            values = multiply(b, whole, b + 1, f"dw{b}")
+        scatter(1, first, early[1])
+        for b in range(2):
+            weave_m(2 + b)
+            late = multiply(b, second, 2 + b, f"late{b}")
+            quantize_m(2 + b, 3 + b)
+            scatter(b, second, late)
+            store(b)
+        for b in range(2, D_BLOCKS):
+            values = multiply(b, whole, b + 2, f"dw{b}")
             scatter(b, whole, values)
             store(b)

@@ -37,16 +37,15 @@ def tile_attend_gkl_w_clip_kernel(tc, xT, wT, y, wt, xn, xm, offs, out):
 
         follows = {
             "x_raw0": "w_plane0",
-            "x_raw1": "w_plane2",
-            "y_pair0_0": "w_bf",
-            "y_pair0_2": "x_bf0_0",
+            "x_raw1_0": "w_plane2",
+            "x_raw1_1": "w_bf",
+            "y_pair0_0": "w_plane3",
             "xn_sb": "x_raw0",
-            "x_bf1_1": "x_bf0_1",
-            "x_bf1_0": "neg_max0",
-            "y_pair1_0": "neg_max1",
-            "y_pair1_2": "neg_max2",
-            "wt_sb": "x_raw1",
-            "xm_raw0": "neg_max3",
+            "y_pair0_2": "x_bf0_0",
+            "y_pair1_0": "x_bf0_1",
+            "y_pair1_2": "neg_max0",
+            "wt_sb": "neg_max1",
+            "xm_raw0": "neg_max2",
             "xm_raw1": "y_pair0_2",
             "neg_max6": "sumsq0",
             "neg_max7": "sums_sq0",
@@ -82,9 +81,10 @@ def tile_attend_gkl_w_clip_kernel(tc, xT, wT, y, wt, xn, xm, offs, out):
         cols = P // 2
         x_bf = {}
 
-        def load_x(g):
-            x_raw[g] = sb([P, PACK, K_PASS], F32, f"x_raw{g}")
-            nc.sync.dma_start(x_raw[g][:], x_rows[:, :, g * K_PASS : (g + 1) * K_PASS])
+        def load_x(name, c0, c1):
+            raw = sb([P, PACK, c1 - c0], F32, name)
+            nc.sync.dma_start(raw[:], x_rows[:, :, c0:c1])
+            return raw[:].rearrange("p j (m t) -> p m j t", t=PACK)
 
         def load_y(g, t0):
             pair = sb([P, 2, N], F32, f"y_pair{g}_{t0}")
@@ -149,29 +149,36 @@ def tile_attend_gkl_w_clip_kernel(tc, xT, wT, y, wt, xn, xm, offs, out):
                 stop=True,
             )
 
-        def weave_x(g, u, ms, on_vector):
-            if (g, u) not in x_bf:
-                x_bf[g, u] = sb([P, 2, P, PACK], BF16, f"x_bf{g}_{u}")
-            dst = x_bf[g, u][:, :, ms, :].rearrange("p t m j -> p m j t")
-            raw = x_raw[g][:].rearrange("p j (m t) -> p m j t", t=PACK)[:, ms, :, 2 * u : 2 * u + 2]
+        def weave_x(woven, raw, on_vector):
+            dst = woven.rearrange("p t m j -> p m j t")
             if on_vector:
                 nc.vector.tensor_copy(dst, raw)
             else:
                 nc.scalar.activation(dst, raw, ACT.Copy)
 
-        X0_VECTOR = 84
-        load_x(0)
-        load_x(1)
-        load_y(0, 0)
-        weave_x(0, 0, slice(X0_VECTOR, P), False)
-        weave_x(0, 0, slice(0, X0_VECTOR), True)
-        weave_x(0, 1, slice(0, P), False)
-        quantize_x(0, 1, x_bf[0, 0][:, 0:1, :, :])
+        x_raw0 = load_x("x_raw0", 0, K_PASS)
+        x_raw1 = [load_x(f"x_raw1_{h}", K_PASS + h * half, K_PASS + (h + 1) * half) for h in range(2)]
+        x_bf0 = [sb([P, 2, P, PACK], BF16, f"x_bf0_{u}") for u in range(2)]
+        for u in range(2):
+            weave_x(x_bf0[u][:], x_raw0[:, :, :, 2 * u : 2 * u + 2], u == 0)
+        quantize_x(0, 1, x_bf0[0][:, 0:1, :, :])
         score(0)
-        quantize_x(1, 2, x_bf[0, 0][:, 1:2, :, :])
+        quantize_x(1, 2, x_bf0[0][:, 1:2, :, :])
         score(1)
-        load_y(0, 2)
+        quantize_x(2, 4, x_bf0[1][:])
+        score(2)
+        score(3)
+        load_y(0, 0)
         xn_sb = load_column("xn_sb", xn)
+        load_y(0, 2)
+        x_bf1 = sb([P, PACK, P, PACK], BF16, "x_bf1")
+
+        def weave_x1(h, u, on_vector):
+            pair = slice(2 * u, 2 * u + 2)
+            weave_x(x_bf1[:, pair, h * cols : (h + 1) * cols, :], x_raw1[h][:, :, :, pair], on_vector)
+
+        weave_x1(0, 0, False)
+        weave_x1(0, 1, False)
 
         diff = [sb([P, N], F32, f"diff{k}") for k in range(TILES)]
         e = [sb([P, N], F32, f"e{k}") for k in range(TILES)]
@@ -202,20 +209,17 @@ def tile_attend_gkl_w_clip_kernel(tc, xT, wT, y, wt, xn, xm, offs, out):
                 )
             nc.gpsimd.tensor_tensor(root[g][:], larger[:], minus_half[:], ALU.pow)
 
-        exponential(0)
-        quantize_x(2, 4, x_bf[0, 1][:])
-        score(2)
-        score(3)
-        exponential(1)
         load_y(1, 0)
-        weave_x(1, 0, slice(0, P), False)
-        weave_x(1, 1, slice(0, P), True)
-        exponential(2)
+        exponential(0)
         load_y(1, 2)
+        exponential(1)
+        weave_x1(1, 0, False)
+        weave_x1(1, 1, True)
+        exponential(2)
         wt_sb = load_column("wt_sb", wt)
         difference(0)
         for u in range(2):
-            quantize_x(PACK + 2 * u, PACK + 2 * u + 2, x_bf[1, u][:])
+            quantize_x(PACK + 2 * u, PACK + 2 * u + 2, x_bf1[:, 2 * u : 2 * u + 2, :, :])
             score(PACK + 2 * u)
             score(PACK + 2 * u + 1)
         exponential(3)

@@ -25,8 +25,17 @@ D_BLOCKS = D // P
 RUN = 4
 LIST_GROUP = 16
 
-WINDOWS = 3
 TILES = PASSES * PACK
+LAST_TILE = TILES - 1
+HALF = N // 2
+EARLY_BLOCKS = 2
+
+WINDOWS = 3
+WINDOWS_ON_VECTOR = 2
+
+X0_VECTOR = 76
+X1_VECTOR = 32
+G0_VECTOR = 223
 
 
 def tile_attend_gkl_w_clip_kernel(tc, xT, wT, y, wt, xn, xm, offs, out):
@@ -38,20 +47,20 @@ def tile_attend_gkl_w_clip_kernel(tc, xT, wT, y, wt, xn, xm, offs, out):
         follows = {
             "x_raw0": "w_plane0",
             "x_raw1_0": "w_plane2",
-            "x_raw1_1": "w_bf",
             "y_pair0_0": "w_plane3",
-            "xn_sb": "x_raw0",
-            "y_pair0_2": "x_bf0_0",
-            "y_pair1_0": "x_bf0_1",
+            "x_raw1_1": "w_bf",
+            "y_pair0_2": "x_raw0",
+            "y_pair1_0": "x_bf0",
+            "xn_sb": "x_raw1_0",
             "y_pair1_2": "neg_max0",
             "wt_sb": "neg_max1",
             "xm_raw0": "neg_max2",
             "xm_raw1": "y_pair0_2",
-            "neg_max6": "sumsq0",
-            "neg_max7": "sums_sq0",
+            f"neg_max{LAST_TILE - 1}": "sumsq0",
+            f"neg_max{LAST_TILE}": "sums_sq0",
             "g_rows": "y_pair1_2",
             "g_bf0": "sumsq1",
-            "m_bf0": f"e{TILES - 1}",
+            "m_bf0": f"e{LAST_TILE}",
             "m_bf2": "g_bf1",
             "early1": "g_rows",
         }
@@ -62,6 +71,11 @@ def tile_attend_gkl_w_clip_kernel(tc, xT, wT, y, wt, xn, xm, offs, out):
         def sb(shape, dtype, name):
             return keep.tile(shape, dtype, name=name, tag=slot_of(name), align_bytes=64)
 
+        def copy(on_vector, dst, src):
+            if on_vector:
+                nc.vector.tensor_copy(dst, src)
+            else:
+                nc.scalar.copy(dst, src)
 
         offsets = keep.tile([P, N // LIST_GROUP], U16, name="offsets")
         w_rows = wT.rearrange("(p j) c -> p j c", j=PACK)
@@ -74,16 +88,14 @@ def tile_attend_gkl_w_clip_kernel(tc, xT, wT, y, wt, xn, xm, offs, out):
                 nc.sync.dma_start(offsets[:], offs)
 
         x_rows = xT.rearrange("b (p j) r -> p (b j) r", j=PACK)
-        half = K_PASS // 2
-        x_raw = {}
         y_rows = y.rearrange("b (g p t) i -> p (b g) t i", g=PASSES, t=PACK)
+        xm_rows = xm.rearrange("b (g p t) d -> p (b g) t d", g=PASSES, t=PACK)
         y_sb = []
-        cols = P // 2
-        x_bf = {}
+        xm_raw = []
 
-        def load_x(name, c0, c1):
-            raw = sb([P, PACK, c1 - c0], F32, name)
-            nc.sync.dma_start(raw[:], x_rows[:, :, c0:c1])
+        def load_x(name, r0, r1):
+            raw = sb([P, PACK, r1 - r0], F32, name)
+            nc.sync.dma_start(raw[:], x_rows[:, :, r0:r1])
             return raw[:].rearrange("p j (m t) -> p m j t", t=PACK)
 
         def load_y(g, t0):
@@ -91,19 +103,15 @@ def tile_attend_gkl_w_clip_kernel(tc, xT, wT, y, wt, xn, xm, offs, out):
             nc.sync.dma_start(pair[:], y_rows[:, g, t0 : t0 + 2, :])
             y_sb.extend([pair[:, 0, :], pair[:, 1, :]])
 
-        xm_rows = xm.rearrange("b (g p t) d -> p (b g) t d", g=PASSES, t=PACK)
-        xm_raw = []
-
-        def load_column(name, values):
-            tile_sb = sb([P, PASSES, PACK], F32, name)
-            nc.sync.dma_start(tile_sb[:], values.rearrange("b (g p t) o -> p (b g) (t o)", g=PASSES, t=PACK))
-            return tile_sb
+        def load_per_row(name, values):
+            per_row = sb([P, PASSES, PACK], F32, name)
+            nc.sync.dma_start(per_row[:], values.rearrange("b (g p t) o -> p (b g) (t o)", g=PASSES, t=PACK))
+            return per_row
 
         def load_xm(g):
             raw = sb([P, PACK, D], F32, f"xm_raw{g}")
             nc.sync.dma_start(raw[:], xm_rows[:, g, :, :])
             xm_raw.append(raw)
-
 
         minus_half = sb([P, PACK], F32, "minus_half")
         ones = sb([P, PACK], F32, "ones")
@@ -111,9 +119,9 @@ def tile_attend_gkl_w_clip_kernel(tc, xT, wT, y, wt, xn, xm, offs, out):
         nc.scalar.activation(minus_half[:], ones[:], ACT.Copy, scale=-0.5)
 
         windows = []
-        for k in range(WINDOWS):
-            window = sb([P, T], F32, f"window{k}")
-            engine = nc.vector if k < 2 else nc.gpsimd
+        for w in range(WINDOWS):
+            window = sb([P, T], F32, f"window{w}")
+            engine = nc.vector if w < WINDOWS_ON_VECTOR else nc.gpsimd
             engine.memset(window[:], 0.0)
             windows.append(window)
 
@@ -130,55 +138,46 @@ def tile_attend_gkl_w_clip_kernel(tc, xT, wT, y, wt, xn, xm, offs, out):
         x_scales = sb([P, TILES, P], U8, "x_scales")
         scores = {}
 
-        def quantize_x(k0, k1, woven):
+        def weave_x(woven, raw, on_vector):
+            if on_vector:
+                nc.vector.tensor_copy(
+                    woven.rearrange("p (u t) m j -> p u m j t", u=2), raw.rearrange("p m j (u t) -> p u m j t", u=2)
+                )
+            else:
+                nc.scalar.activation(woven.rearrange("p t m j -> p m j t"), raw, ACT.Copy)
+
+        def score(g, t0, t1, woven):
+            k0, k1 = PACK * g + t0, PACK * g + t1
             nc.vector.quantize_mx(
                 out=x_codes[:, k0:k1, :].rearrange("p t m -> p (t m)").bitcast(E4M3),
                 scales=x_scales[:, k0:k1, :].rearrange("p t m -> p (t m)"),
-                in_=woven.rearrange("p t m j -> p (t m j)"),
+                in_=woven[:, t0:t1, :, :].rearrange("p t m j -> p (t m j)"),
             )
+            for k in range(k0, k1):
+                scores[k] = psum.tile([P, N], F32, name=f"scores{k}", tag=f"bank{k}")
+                nc.tensor.matmul_mx(
+                    out=scores[k][:],
+                    lhsT=x_codes[:, k, :].bitcast(E4M3),
+                    lhsT_scale=x_scales[:, k, :],
+                    rhs=w_codes[:].bitcast(E4M3),
+                    rhs_scale=w_scales[:],
+                    start=True,
+                    stop=True,
+                )
 
-        def score(k):
-            scores[k] = psum.tile([P, N], F32, name=f"scores{k}", tag=f"bank{k}")
-            nc.tensor.matmul_mx(
-                out=scores[k][:],
-                lhsT=x_codes[:, k, :].bitcast(E4M3),
-                lhsT_scale=x_scales[:, k, :],
-                rhs=w_codes[:].bitcast(E4M3),
-                rhs_scale=w_scales[:],
-                start=True,
-                stop=True,
-            )
-
-        def weave_x(woven, raw, on_vector):
-            dst = woven.rearrange("p t m j -> p m j t")
-            if on_vector:
-                nc.vector.tensor_copy(dst, raw)
-            else:
-                nc.scalar.activation(dst, raw, ACT.Copy)
-
+        rows_half, m_half = K_PASS // 2, P // 2
         x_raw0 = load_x("x_raw0", 0, K_PASS)
-        x_raw1 = [load_x(f"x_raw1_{h}", K_PASS + h * half, K_PASS + (h + 1) * half) for h in range(2)]
-        x_bf0 = [sb([P, 2, P, PACK], BF16, f"x_bf0_{u}") for u in range(2)]
-        for u in range(2):
-            weave_x(x_bf0[u][:], x_raw0[:, :, :, 2 * u : 2 * u + 2], u == 0)
-        quantize_x(0, 1, x_bf0[0][:, 0:1, :, :])
-        score(0)
-        quantize_x(1, 2, x_bf0[0][:, 1:2, :, :])
-        score(1)
-        quantize_x(2, 4, x_bf0[1][:])
-        score(2)
-        score(3)
+        x_raw1 = [load_x(f"x_raw1_{h}", K_PASS + h * rows_half, K_PASS + (h + 1) * rows_half) for h in range(2)]
+        x_bf0 = sb([P, PACK, P, PACK], BF16, "x_bf0")
+        weave_x(x_bf0[:, :, 0:X0_VECTOR, :], x_raw0[:, 0:X0_VECTOR, :, :], True)
+        weave_x(x_bf0[:, :, X0_VECTOR:, :], x_raw0[:, X0_VECTOR:, :, :], False)
+        for t0, t1 in ((0, 1), (1, 2), (2, 4)):
+            score(0, t0, t1, x_bf0)
         load_y(0, 0)
-        xn_sb = load_column("xn_sb", xn)
         load_y(0, 2)
+        load_y(1, 0)
         x_bf1 = sb([P, PACK, P, PACK], BF16, "x_bf1")
-
-        def weave_x1(h, u, on_vector):
-            pair = slice(2 * u, 2 * u + 2)
-            weave_x(x_bf1[:, pair, h * cols : (h + 1) * cols, :], x_raw1[h][:, :, :, pair], on_vector)
-
-        weave_x1(0, 0, False)
-        weave_x1(0, 1, False)
+        weave_x(x_bf1[:, :, 0:m_half, :], x_raw1[0], False)
 
         diff = [sb([P, N], F32, f"diff{k}") for k in range(TILES)]
         e = [sb([P, N], F32, f"e{k}") for k in range(TILES)]
@@ -209,19 +208,17 @@ def tile_attend_gkl_w_clip_kernel(tc, xT, wT, y, wt, xn, xm, offs, out):
                 )
             nc.gpsimd.tensor_tensor(root[g][:], larger[:], minus_half[:], ALU.pow)
 
-        load_y(1, 0)
         exponential(0)
         load_y(1, 2)
+        xn_sb = load_per_row("xn_sb", xn)
         exponential(1)
-        weave_x1(1, 0, False)
-        weave_x1(1, 1, True)
+        weave_x(x_bf1[:, :, m_half + X1_VECTOR :, :], x_raw1[1][:, X1_VECTOR:, :, :], False)
+        weave_x(x_bf1[:, :, m_half : m_half + X1_VECTOR, :], x_raw1[1][:, 0:X1_VECTOR, :, :], True)
         exponential(2)
-        wt_sb = load_column("wt_sb", wt)
+        wt_sb = load_per_row("wt_sb", wt)
         difference(0)
-        for u in range(2):
-            quantize_x(PACK + 2 * u, PACK + 2 * u + 2, x_bf1[:, 2 * u : 2 * u + 2, :, :])
-            score(PACK + 2 * u)
-            score(PACK + 2 * u + 1)
+        for t0 in (0, 2):
+            score(1, t0, t0 + 2, x_bf1)
         exponential(3)
         load_xm(0)
         difference(1)
@@ -232,37 +229,39 @@ def tile_attend_gkl_w_clip_kernel(tc, xT, wT, y, wt, xn, xm, offs, out):
         row_roots(0)
         exponential(5)
         difference(4)
-        exponential(6)
-        exponential(7)
+        exponential(LAST_TILE - 1)
+        exponential(LAST_TILE)
         for k in range(5, TILES):
             difference(k)
         row_roots(1)
 
-        HALF = N // 2
-        halves = (slice(0, HALF), slice(HALF, N))
+        first, second, whole = slice(0, HALF), slice(HALF, N), slice(0, N)
         g_codes = [sb([P, N], U32, f"g_codes{g}") for g in range(PASSES)]
         g_scales = [sb([P, N], U8, f"g_scales{g}") for g in range(PASSES)]
         for g in range(PASSES):
-            nc.vector.memset(g_codes[g][:, halves[1]], 0)
-            nc.vector.memset(g_scales[g][:, halves[1]], 0)
+            nc.vector.memset(g_codes[g][:, second], 0)
+            nc.vector.memset(g_scales[g][:, second], 0)
         g_rows = sb([P, PASSES, PACK, N], BF16, "g_rows")
         g_bf = [sb([P, N, PACK], BF16, f"g_bf{g}") for g in range(PASSES)]
 
         def scale_rows(g, slots):
             for t in range(PACK):
-                k = PACK * g + t
                 col = slice(t, t + 1)
                 nc.vector.tensor_scalar(
-                    g_rows[:, g, t, slots], diff[k][:, slots], root[g][:, col], wt_sb[:, g, col], ALU.mult, ALU.mult
+                    g_rows[:, g, t, slots],
+                    diff[PACK * g + t][:, slots],
+                    root[g][:, col],
+                    wt_sb[:, g, col],
+                    ALU.mult,
+                    ALU.mult,
                 )
 
         def weave_g(g, slots, on_vector):
-            dst = g_bf[g][:, slots, :].rearrange("p (c i) t -> p c t i", i=RUN)
-            rows = g_rows[:, g, :, slots].rearrange("p t (c i) -> p c t i", i=RUN)
-            if on_vector:
-                nc.vector.tensor_copy(dst, rows)
-            else:
-                nc.scalar.copy(dst, rows)
+            copy(
+                on_vector,
+                g_bf[g][:, slots, :].rearrange("p (c i) t -> p c t i", i=RUN),
+                g_rows[:, g, :, slots].rearrange("p t (c i) -> p c t i", i=RUN),
+            )
 
         def quantize_g(g, slots):
             nc.vector.quantize_mx(
@@ -271,26 +270,25 @@ def tile_attend_gkl_w_clip_kernel(tc, xT, wT, y, wt, xn, xm, offs, out):
                 in_=g_bf[g][:, slots, :].rearrange("p i t -> p (i t)"),
             )
 
-        m_codes = sb([P, D_BLOCKS * PASSES, P], U32, "m_codes")
-        m_scales = sb([P, D_BLOCKS * PASSES, P], U8, "m_scales")
+        m_codes = sb([P, D_BLOCKS, PASSES, P], U32, "m_codes")
+        m_scales = sb([P, D_BLOCKS, PASSES, P], U8, "m_scales")
         m_bf = {}
 
         def weave_m(b):
             if b not in m_bf:
-                pair = sb([P, 2, PASSES, P, PACK], BF16, f"m_bf{b}")
-                m_bf[b], m_bf[b + 1] = pair[:, 0, :, :, :], pair[:, 1, :, :, :]
+                two = sb([P, 2, PASSES, P, PACK], BF16, f"m_bf{b}")
+                m_bf[b], m_bf[b + 1] = two[:, 0, :, :, :], two[:, 1, :, :, :]
             for g in range(PASSES):
                 nc.scalar.copy(
                     m_bf[b][:, g, :, :].rearrange("p (c i) t -> p c t i", i=RUN),
                     xm_raw[g][:, :, b * P : (b + 1) * P].rearrange("p t (c i) -> p c t i", i=RUN),
                 )
 
-        def quantize_m(b0, b1):
-            u0, u1 = PASSES * b0, PASSES * b1
+        def quantize_m(b):
             nc.vector.quantize_mx(
-                out=m_codes[:, u0:u1, :].rearrange("p u m -> p (u m)").bitcast(E4M3),
-                scales=m_scales[:, u0:u1, :].rearrange("p u m -> p (u m)"),
-                in_=m_bf[b0].rearrange("p u m t -> p (u m t)"),
+                out=m_codes[:, b, :, :].rearrange("p g m -> p (g m)").bitcast(E4M3),
+                scales=m_scales[:, b, :, :].rearrange("p g m -> p (g m)"),
+                in_=m_bf[b].rearrange("p g m t -> p (g m t)"),
             )
 
         def multiply(b, slots, bank, name):
@@ -298,56 +296,54 @@ def tile_attend_gkl_w_clip_kernel(tc, xT, wT, y, wt, xn, xm, offs, out):
             for g in range(PASSES):
                 nc.tensor.matmul_mx(
                     out=acc[:],
-                    lhsT=m_codes[:, PASSES * b + g, :].bitcast(E4M3),
-                    lhsT_scale=m_scales[:, PASSES * b + g, :],
+                    lhsT=m_codes[:, b, g, :].bitcast(E4M3),
+                    lhsT_scale=m_scales[:, b, g, :],
                     rhs=g_codes[g][:].bitcast(E5M2),
                     rhs_scale=g_scales[g][:],
                     start=(g == 0),
                     stop=(g == PASSES - 1),
                 )
-            sums_out = sb([P, slots.stop - slots.start], F32, name)
-            nc.scalar.activation(sums_out[:], acc[:, slots], ACT.Copy, scale=-1.0)
-            return sums_out
+            dw = sb([P, slots.stop - slots.start], F32, name)
+            nc.scalar.activation(dw[:], acc[:, slots], ACT.Copy, scale=-1.0)
+            return dw
 
-        def scatter(b, slots, values):
+        def scatter(b, slots, dw):
             listed = offsets[:, slots.start // LIST_GROUP : slots.stop // LIST_GROUP]
-            nc.vector.tensor_copy(windows[b % WINDOWS][:].indirect(listed), values[:])
+            nc.vector.tensor_copy(windows[b % WINDOWS][:].indirect(listed), dw[:])
 
         def store(b):
             nc.sync.dma_start(out[b * P : (b + 1) * P, :], windows[b % WINDOWS][:])
 
-        whole = slice(0, N)
-        first, second = halves
         for g in range(PASSES):
             scale_rows(g, first)
         weave_m(0)
-        one_port = slice(0, 223)
-        nc.vector.tensor_copy(g_bf[0][:, one_port, :], g_rows[:, 0, :, one_port].rearrange("p t i -> p i t"))
-        rest = slice(223, HALF)
-        nc.scalar.copy(g_bf[0][:, rest, :], g_rows[:, 0, :, rest].rearrange("p t i -> p i t"))
-        quantize_m(0, 1)
+        for slots, on_vector in ((slice(0, G0_VECTOR), True), (slice(G0_VECTOR, HALF), False)):
+            copy(on_vector, g_bf[0][:, slots, :], g_rows[:, 0, :, slots].rearrange("p t i -> p i t"))
+        quantize_m(0)
         weave_g(1, first, True)
         for g in range(PASSES):
             quantize_g(g, first)
         weave_m(1)
-        early = [multiply(0, first, 0, "early0")]
-        scale_rows(0, second)
-        scale_rows(1, second)
+        early0 = multiply(0, first, 0, "early0")
+
+        for g in range(PASSES):
+            scale_rows(g, second)
         weave_g(0, second, False)
-        quantize_m(1, 2)
+        quantize_m(1)
         quantize_g(0, second)
         weave_g(1, second, False)
-        early.append(multiply(1, first, 1, "early1"))
-        scatter(0, first, early[0])
+        early1 = multiply(1, first, 1, "early1")
+        scatter(0, first, early0)
         quantize_g(1, second)
-        scatter(1, first, early[1])
-        for b in range(2):
-            weave_m(2 + b)
-            late = multiply(b, second, 2 + b, f"late{b}")
-            quantize_m(2 + b, 3 + b)
+        scatter(1, first, early1)
+
+        for b in range(EARLY_BLOCKS):
+            weave_m(EARLY_BLOCKS + b)
+            late = multiply(b, second, EARLY_BLOCKS + b, f"late{b}")
+            quantize_m(EARLY_BLOCKS + b)
             scatter(b, second, late)
             store(b)
-        for b in range(2, D_BLOCKS):
-            values = multiply(b, whole, b + 2, f"dw{b}")
-            scatter(b, whole, values)
+        for b in range(EARLY_BLOCKS, D_BLOCKS):
+            dw = multiply(b, whole, EARLY_BLOCKS + b, f"dw{b}")
+            scatter(b, whole, dw)
             store(b)

@@ -45,17 +45,6 @@ def tile_attend_gkl_w_clip_kernel(tc, xT, wT, y, wt, xn, xm, offs, out):
         psum = ctx.enter_context(tc.psum_pool(name="psum", bufs=1))
 
         follows = {
-            "x_raw0": "w_plane0",
-            "x_raw1_0": "w_plane2",
-            "y_pair0_0": "w_plane3",
-            "x_raw1_1": "w_bf",
-            "y_pair0_2": "x_raw0",
-            "y_pair1_0": "x_bf0",
-            "xn_sb": "x_raw1_0",
-            "y_pair1_2": "neg_max0",
-            "wt_sb": "neg_max1",
-            "xm_raw0": "neg_max2",
-            "xm_raw1": "y_pair0_2",
             f"neg_max{LAST_TILE - 1}": "sumsq0",
             f"neg_max{LAST_TILE}": "sums_sq0",
             "g_rows": "y_pair1_2",
@@ -113,6 +102,18 @@ def tile_attend_gkl_w_clip_kernel(tc, xT, wT, y, wt, xn, xm, offs, out):
             nc.sync.dma_start(raw[:], xm_rows[:, g, :, :])
             xm_raw.append(raw)
 
+        rows_half, m_half = K_PASS // 2, P // 2
+        x_raw0 = load_x("x_raw0", 0, K_PASS)
+        x_raw1 = [load_x(f"x_raw1_{h}", K_PASS + h * rows_half, K_PASS + (h + 1) * rows_half) for h in range(2)]
+        load_y(0, 0)
+        load_y(0, 2)
+        xn_sb = load_per_row("xn_sb", xn)
+        load_y(1, 0)
+        load_y(1, 2)
+        wt_sb = load_per_row("wt_sb", wt)
+        load_xm(0)
+        load_xm(1)
+
         minus_half = sb([P, PACK], F32, "minus_half")
         ones = sb([P, PACK], F32, "ones")
         nc.gpsimd.memset(ones[:], 1.0)
@@ -165,17 +166,11 @@ def tile_attend_gkl_w_clip_kernel(tc, xT, wT, y, wt, xn, xm, offs, out):
                     stop=True,
                 )
 
-        rows_half, m_half = K_PASS // 2, P // 2
-        x_raw0 = load_x("x_raw0", 0, K_PASS)
-        x_raw1 = [load_x(f"x_raw1_{h}", K_PASS + h * rows_half, K_PASS + (h + 1) * rows_half) for h in range(2)]
         x_bf0 = sb([P, PACK, P, PACK], BF16, "x_bf0")
         weave_x(x_bf0[:, :, 0:X0_VECTOR, :], x_raw0[:, 0:X0_VECTOR, :, :], True)
         weave_x(x_bf0[:, :, X0_VECTOR:, :], x_raw0[:, X0_VECTOR:, :, :], False)
         for t0, t1 in ((0, 1), (1, 2), (2, 4)):
             score(0, t0, t1, x_bf0)
-        load_y(0, 0)
-        load_y(0, 2)
-        load_y(1, 0)
         x_bf1 = sb([P, PACK, P, PACK], BF16, "x_bf1")
         weave_x(x_bf1[:, :, 0:m_half, :], x_raw1[0], False)
 
@@ -209,23 +204,18 @@ def tile_attend_gkl_w_clip_kernel(tc, xT, wT, y, wt, xn, xm, offs, out):
             nc.gpsimd.tensor_tensor(root[g][:], larger[:], minus_half[:], ALU.pow)
 
         exponential(0)
-        load_y(1, 2)
-        xn_sb = load_per_row("xn_sb", xn)
         exponential(1)
         weave_x(x_bf1[:, :, m_half + X1_VECTOR :, :], x_raw1[1][:, X1_VECTOR:, :, :], False)
         weave_x(x_bf1[:, :, m_half : m_half + X1_VECTOR, :], x_raw1[1][:, 0:X1_VECTOR, :, :], True)
         exponential(2)
-        wt_sb = load_per_row("wt_sb", wt)
         difference(0)
         for t0 in (0, 2):
             score(1, t0, t0 + 2, x_bf1)
         exponential(3)
-        load_xm(0)
         difference(1)
         difference(2)
         exponential(4)
         difference(3)
-        load_xm(1)
         row_roots(0)
         exponential(5)
         difference(4)

@@ -28,6 +28,7 @@ LIST_GROUP = 16
 TILES = PASSES * PACK
 LAST_TILE = TILES - 1
 HALF = N // 2
+QUARTER = N // 4
 EARLY_BLOCKS = 2
 
 WINDOWS = 3
@@ -35,7 +36,8 @@ WINDOWS_ON_VECTOR = 2
 
 X0_VECTOR = 76
 X1_VECTOR = 32
-G0_VECTOR = 223
+G0_VECTOR = 255
+M0_VECTOR = 127
 
 
 def tile_attend_gkl_w_clip_kernel(tc, xT, wT, y, wt, xn, xm, offs, out):
@@ -45,13 +47,16 @@ def tile_attend_gkl_w_clip_kernel(tc, xT, wT, y, wt, xn, xm, offs, out):
         psum = ctx.enter_context(tc.psum_pool(name="psum", bufs=1))
 
         follows = {
-            f"neg_max{LAST_TILE - 1}": "sumsq0",
-            f"neg_max{LAST_TILE}": "sums_sq0",
-            "g_rows": "y_pair1_2",
-            "g_bf0": "sumsq1",
-            "m_bf0": f"e{LAST_TILE}",
-            "m_bf2": "g_bf1",
-            "early1": "g_rows",
+            "neg_max6": "sumsq0",
+            "neg_max7": "sums_sq0",
+            "g_bf0_0": "length",
+            "m_bf0": "e6",
+            "g_rows0_1": "e7",
+            "m_bf1": "sumsq1",
+            "g_bf1_0": "m_bf0",
+            "g_bf1_1": "m_bf1",
+            "m_bf2": "g_bf1_1",
+            "g_rows1_1": "g_bf1_0",
         }
 
         def slot_of(name):
@@ -60,27 +65,18 @@ def tile_attend_gkl_w_clip_kernel(tc, xT, wT, y, wt, xn, xm, offs, out):
         def sb(shape, dtype, name):
             return keep.tile(shape, dtype, name=name, tag=slot_of(name), align_bytes=64)
 
-        def copy(on_vector, dst, src):
-            if on_vector:
-                nc.vector.tensor_copy(dst, src)
-            else:
-                nc.scalar.copy(dst, src)
-
         offsets = keep.tile([P, N // LIST_GROUP], U16, name="offsets")
         w_rows = wT.rearrange("(p j) c -> p j c", j=PACK)
-        w_plane = []
-        for j in range(PACK):
-            plane = sb([P, T], F32, f"w_plane{j}")
-            nc.sync.dma_start(plane[:], w_rows[:, j, :])
-            w_plane.append(plane)
-            if j == 0:
-                nc.sync.dma_start(offsets[:], offs)
-
         x_rows = xT.rearrange("b (p j) r -> p (b j) r", j=PACK)
         y_rows = y.rearrange("b (g p t) i -> p (b g) t i", g=PASSES, t=PACK)
         xm_rows = xm.rearrange("b (g p t) d -> p (b g) t d", g=PASSES, t=PACK)
+        w_plane = []
         y_sb = []
-        xm_raw = []
+
+        def load_w(j):
+            plane = sb([P, T], F32, f"w_plane{j}")
+            nc.sync.dma_start(plane[:], w_rows[:, j, :])
+            w_plane.append(plane)
 
         def load_x(name, r0, r1):
             raw = sb([P, PACK, r1 - r0], F32, name)
@@ -97,27 +93,28 @@ def tile_attend_gkl_w_clip_kernel(tc, xT, wT, y, wt, xn, xm, offs, out):
             nc.sync.dma_start(per_row[:], values.rearrange("b (g p t) o -> p (b g) (t o)", g=PASSES, t=PACK))
             return per_row
 
-        def load_xm(g):
-            raw = sb([P, PACK, D], F32, f"xm_raw{g}")
-            nc.sync.dma_start(raw[:], xm_rows[:, g, :, :])
-            xm_raw.append(raw)
-
         rows_half, m_half = K_PASS // 2, P // 2
+        load_w(0)
+        nc.sync.dma_start(offsets[:], offs)
+        xn_sb = load_per_row("xn_sb", xn)
+        for j in range(1, PACK):
+            load_w(j)
         x_raw0 = load_x("x_raw0", 0, K_PASS)
         x_raw1 = [load_x(f"x_raw1_{h}", K_PASS + h * rows_half, K_PASS + (h + 1) * rows_half) for h in range(2)]
-        load_y(0, 0)
-        load_y(0, 2)
-        xn_sb = load_per_row("xn_sb", xn)
-        load_y(1, 0)
-        load_y(1, 2)
+        for g in range(PASSES):
+            for t0 in (0, 2):
+                load_y(g, t0)
         wt_sb = load_per_row("wt_sb", wt)
-        load_xm(0)
-        load_xm(1)
+        xm_raw = sb([P, PASSES, PACK, D], F32, "xm_raw")
+        for g in range(PASSES):
+            nc.sync.dma_start(xm_raw[:, g, :, :], xm_rows[:, g, :, :])
 
         minus_half = sb([P, PACK], F32, "minus_half")
         ones = sb([P, PACK], F32, "ones")
         nc.gpsimd.memset(ones[:], 1.0)
         nc.scalar.activation(minus_half[:], ones[:], ACT.Copy, scale=-0.5)
+        half = sb([P, TILES], F32, "half")
+        nc.gpsimd.memset(half[:], 0.5)
 
         windows = []
         for w in range(WINDOWS):
@@ -125,6 +122,20 @@ def tile_attend_gkl_w_clip_kernel(tc, xT, wT, y, wt, xn, xm, offs, out):
             engine = nc.vector if w < WINDOWS_ON_VECTOR else nc.gpsimd
             engine.memset(window[:], 0.0)
             windows.append(window)
+
+        first, second, whole = slice(0, HALF), slice(HALF, N), slice(0, N)
+        g_codes = [sb([P, N], U32, f"g_codes{g}") for g in range(PASSES)]
+        g_scales = [sb([P, N], U8, f"g_scales{g}") for g in range(PASSES)]
+        for g in range(PASSES):
+            nc.vector.memset(g_codes[g][:, second], 0)
+            nc.vector.memset(g_scales[g][:, second], 0)
+
+        xn_over = sb([P, TILES], F32, "xn_over")
+        length = sb([P, TILES], F32, "length")
+        nc.gpsimd.tensor_scalar(
+            xn_over[:], xn_sb[:].rearrange("p g t -> p (g t)"), 1.0 / (CLIP * CLIP), 0.0, ALU.mult, ALU.add
+        )
+        nc.gpsimd.tensor_tensor(length[:], xn_over[:], half[:], ALU.pow)
 
         w_bf = sb([P, N, PACK], BF16, "w_bf")
         for j in range(PACK):
@@ -137,9 +148,11 @@ def tile_attend_gkl_w_clip_kernel(tc, xT, wT, y, wt, xn, xm, offs, out):
 
         x_codes = sb([P, TILES, P], U32, "x_codes")
         x_scales = sb([P, TILES, P], U8, "x_scales")
+        x_bf = [sb([P, PACK, P, PACK], BF16, f"x_bf{g}") for g in range(PASSES)]
         scores = {}
 
-        def weave_x(woven, raw, on_vector):
+        def weave_x(g, m0, m1, raw, on_vector):
+            woven = x_bf[g][:, :, m0:m1, :]
             if on_vector:
                 nc.vector.tensor_copy(
                     woven.rearrange("p (u t) m j -> p u m j t", u=2), raw.rearrange("p m j (u t) -> p u m j t", u=2)
@@ -147,12 +160,12 @@ def tile_attend_gkl_w_clip_kernel(tc, xT, wT, y, wt, xn, xm, offs, out):
             else:
                 nc.scalar.activation(woven.rearrange("p t m j -> p m j t"), raw, ACT.Copy)
 
-        def score(g, t0, t1, woven):
+        def score(g, t0, t1):
             k0, k1 = PACK * g + t0, PACK * g + t1
             nc.vector.quantize_mx(
                 out=x_codes[:, k0:k1, :].rearrange("p t m -> p (t m)").bitcast(E4M3),
                 scales=x_scales[:, k0:k1, :].rearrange("p t m -> p (t m)"),
-                in_=woven[:, t0:t1, :, :].rearrange("p t m j -> p (t m j)"),
+                in_=x_bf[g][:, t0:t1, :, :].rearrange("p t m j -> p (t m j)"),
             )
             for k in range(k0, k1):
                 scores[k] = psum.tile([P, N], F32, name=f"scores{k}", tag=f"bank{k}")
@@ -166,19 +179,11 @@ def tile_attend_gkl_w_clip_kernel(tc, xT, wT, y, wt, xn, xm, offs, out):
                     stop=True,
                 )
 
-        x_bf0 = sb([P, PACK, P, PACK], BF16, "x_bf0")
-        weave_x(x_bf0[:, :, 0:X0_VECTOR, :], x_raw0[:, 0:X0_VECTOR, :, :], True)
-        weave_x(x_bf0[:, :, X0_VECTOR:, :], x_raw0[:, X0_VECTOR:, :, :], False)
-        for t0, t1 in ((0, 1), (1, 2), (2, 4)):
-            score(0, t0, t1, x_bf0)
-        x_bf1 = sb([P, PACK, P, PACK], BF16, "x_bf1")
-        weave_x(x_bf1[:, :, 0:m_half, :], x_raw1[0], False)
-
-        diff = [sb([P, N], F32, f"diff{k}") for k in range(TILES)]
+        diffs = [sb([P, PACK, N], F32, f"diffs{g}") for g in range(PASSES)]
         e = [sb([P, N], F32, f"e{k}") for k in range(TILES)]
         sums = [sb([P, PACK], F32, f"sums{g}") for g in range(PASSES)]
         sumsq = [sb([P, PACK], F32, f"sumsq{g}") for g in range(PASSES)]
-        root = [sb([P, PACK], F32, f"root{g}") for g in range(PASSES)]
+        sums_sq, root, factor = {}, {}, {}
 
         def exponential(k):
             g, t = divmod(k, PACK)
@@ -189,90 +194,100 @@ def tile_attend_gkl_w_clip_kernel(tc, xT, wT, y, wt, xn, xm, offs, out):
         def difference(k):
             g, t = divmod(k, PACK)
             col = slice(t, t + 1)
-            nc.vector.scalar_tensor_tensor(diff[k][:], y_sb[k], sums[g][:, col], e[k][:], ALU.mult, ALU.subtract)
-            nc.scalar.activation(e[k][:], diff[k][:], ACT.Square, scale=1.0 / CLIP, accum_out=sumsq[g][:, col])
+            nc.vector.scalar_tensor_tensor(diffs[g][:, t, :], y_sb[k], sums[g][:, col], e[k][:], ALU.mult, ALU.subtract)
+            nc.scalar.activation(
+                e[k][:], diffs[g][:, t, :], ACT.Square, scale=length[:, k : k + 1], accum_out=sumsq[g][:, col]
+            )
+
+        def square_sums(g):
+            sums_sq[g] = sb([P, PACK], F32, f"sums_sq{g}")
+            nc.vector.tensor_tensor(sums_sq[g][:], sums[g][:], sums[g][:], ALU.mult)
 
         def row_roots(g):
-            sums_sq = sb([P, PACK], F32, f"sums_sq{g}")
-            nc.vector.tensor_tensor(sums_sq[:], sums[g][:], sums[g][:], ALU.mult)
             larger = sb([P, PACK], F32, f"larger{g}")
-            for t in range(PACK):
-                col = slice(t, t + 1)
-                nc.vector.tensor_scalar(
-                    larger[:, col], sumsq[g][:, col], xn_sb[:, g, col], sums_sq[:, col], ALU.mult, ALU.max
-                )
+            nc.vector.tensor_tensor(larger[:], sumsq[g][:], sums_sq[g][:], ALU.max)
+            root[g] = sb([P, PACK], F32, f"root{g}")
             nc.gpsimd.tensor_tensor(root[g][:], larger[:], minus_half[:], ALU.pow)
 
-        exponential(0)
-        exponential(1)
-        weave_x(x_bf1[:, :, m_half + X1_VECTOR :, :], x_raw1[1][:, X1_VECTOR:, :, :], False)
-        weave_x(x_bf1[:, :, m_half : m_half + X1_VECTOR, :], x_raw1[1][:, 0:X1_VECTOR, :, :], True)
-        exponential(2)
-        difference(0)
-        for t0 in (0, 2):
-            score(1, t0, t0 + 2, x_bf1)
-        exponential(3)
-        difference(1)
-        difference(2)
-        exponential(4)
-        difference(3)
-        row_roots(0)
-        exponential(5)
-        difference(4)
-        exponential(LAST_TILE - 1)
-        exponential(LAST_TILE)
-        for k in range(5, TILES):
-            difference(k)
-        row_roots(1)
+        def row_factors(g):
+            factor[g] = sb([P, PACK], F32, f"factor{g}")
+            nc.vector.tensor_tensor(factor[g][:], root[g][:], wt_sb[:, g, :], ALU.mult)
 
-        first, second, whole = slice(0, HALF), slice(HALF, N), slice(0, N)
-        g_codes = [sb([P, N], U32, f"g_codes{g}") for g in range(PASSES)]
-        g_scales = [sb([P, N], U8, f"g_scales{g}") for g in range(PASSES)]
-        for g in range(PASSES):
-            nc.vector.memset(g_codes[g][:, second], 0)
-            nc.vector.memset(g_scales[g][:, second], 0)
-        g_rows = sb([P, PASSES, PACK, N], BF16, "g_rows")
-        g_bf = [sb([P, N, PACK], BF16, f"g_bf{g}") for g in range(PASSES)]
+        g_rows, g_bf = {}, {}
 
-        def scale_rows(g, slots):
-            for t in range(PACK):
-                col = slice(t, t + 1)
-                nc.vector.tensor_scalar(
-                    g_rows[:, g, t, slots],
-                    diff[PACK * g + t][:, slots],
-                    root[g][:, col],
-                    wt_sb[:, g, col],
-                    ALU.mult,
-                    ALU.mult,
-                )
+        def woven_g(g, slots):
+            h = slots.start // HALF
+            if (g, h) not in g_bf:
+                g_bf[g, h] = sb([P, HALF, PACK], BF16, f"g_bf{g}_{h}")
+            return g_bf[g, h][:, slots.start - h * HALF : slots.stop - h * HALF, :]
 
-        def weave_g(g, slots, on_vector):
-            copy(
-                on_vector,
-                g_bf[g][:, slots, :].rearrange("p (c i) t -> p c t i", i=RUN),
-                g_rows[:, g, :, slots].rearrange("p t (c i) -> p c t i", i=RUN),
+        def scale_and_weave(g, slots):
+            runs = (slots.stop - slots.start) // RUN
+            nc.vector.tensor_tensor(
+                woven_g(g, slots).rearrange("p (c i) t -> p c t i", i=RUN),
+                diffs[g][:, :, slots].rearrange("p t (c i) -> p c t i", i=RUN),
+                factor[g][:].unsqueeze(1).unsqueeze(3).to_broadcast([P, runs, PACK, RUN]),
+                ALU.mult,
             )
+
+        def scale_rows(g, slots, tiles, on_vector):
+            h = slots.start // HALF
+            if (g, h) not in g_rows:
+                if (g, h) == (0, 0):
+                    g_rows[g, h] = y_sb[LAST_TILE].bitcast(BF16).rearrange("p (t i) -> p t i", t=PACK)
+                else:
+                    g_rows[g, h] = sb([P, PACK, HALF], BF16, f"g_rows{g}_{h}")
+            for t in tiles:
+                col = factor[g][:, t : t + 1]
+                if on_vector:
+                    nc.vector.tensor_scalar(g_rows[g, h][:, t, :], diffs[g][:, t, slots], col, None, ALU.mult)
+                else:
+                    nc.scalar.activation(g_rows[g, h][:, t, :], diffs[g][:, t, slots], ACT.Copy, scale=col)
+
+        def weave_g(g):
+            nc.scalar.copy(
+                woven_g(g, second).rearrange("p (c i) t -> p c t i", i=RUN),
+                g_rows[g, 1][:].rearrange("p t (c i) -> p c t i", i=RUN),
+            )
+
+        def weave_g0():
+            rows = g_rows[0, 0].rearrange("p t i -> p i t")
+            nc.vector.tensor_copy(woven_g(0, slice(0, G0_VECTOR)), rows[:, 0:G0_VECTOR, :])
+            nc.scalar.copy(woven_g(0, slice(G0_VECTOR, HALF)), rows[:, G0_VECTOR:, :])
 
         def quantize_g(g, slots):
             nc.vector.quantize_mx(
                 out=g_codes[g][:, slots].bitcast(E5M2),
                 scales=g_scales[g][:, slots],
-                in_=g_bf[g][:, slots, :].rearrange("p i t -> p (i t)"),
+                in_=woven_g(g, slots).rearrange("p i t -> p (i t)"),
             )
 
         m_codes = sb([P, D_BLOCKS, PASSES, P], U32, "m_codes")
         m_scales = sb([P, D_BLOCKS, PASSES, P], U8, "m_scales")
         m_bf = {}
+        late_pair = []
 
         def weave_m(b):
-            if b not in m_bf:
-                two = sb([P, 2, PASSES, P, PACK], BF16, f"m_bf{b}")
-                m_bf[b], m_bf[b + 1] = two[:, 0, :, :, :], two[:, 1, :, :, :]
+            if b == EARLY_BLOCKS + 1:
+                m_bf[b] = late_pair[0][:, 1, :, :, :]
+            elif b == EARLY_BLOCKS:
+                late_pair.append(sb([P, 2, PASSES, P, PACK], BF16, f"m_bf{b}"))
+                m_bf[b] = late_pair[0][:, 0, :, :, :]
+            else:
+                m_bf[b] = sb([P, PASSES, P, PACK], BF16, f"m_bf{b}")[:]
             for g in range(PASSES):
                 nc.scalar.copy(
                     m_bf[b][:, g, :, :].rearrange("p (c i) t -> p c t i", i=RUN),
-                    xm_raw[g][:, :, b * P : (b + 1) * P].rearrange("p t (c i) -> p c t i", i=RUN),
+                    xm_raw[:, g, :, b * P : (b + 1) * P].rearrange("p t (c i) -> p c t i", i=RUN),
                 )
+
+        def weave_m0():
+            m_bf[0] = sb([P, PASSES, P, PACK], BF16, "m_bf0")[:]
+            for g in range(PASSES):
+                nc.vector.tensor_copy(
+                    m_bf[0][:, g, 0:M0_VECTOR, :], xm_raw[:, g, :, 0:M0_VECTOR].rearrange("p t m -> p m t")
+                )
+            nc.scalar.copy(m_bf[0][:, :, M0_VECTOR:, :], xm_raw[:, :, :, M0_VECTOR:P].rearrange("p g t m -> p g m t"))
 
         def quantize_m(b):
             nc.vector.quantize_mx(
@@ -281,7 +296,7 @@ def tile_attend_gkl_w_clip_kernel(tc, xT, wT, y, wt, xn, xm, offs, out):
                 in_=m_bf[b].rearrange("p g m t -> p (g m t)"),
             )
 
-        def multiply(b, slots, bank, name):
+        def multiply(b, bank, name):
             acc = psum.tile([P, N], F32, name=f"acc_{name}", tag=f"bank{bank}")
             for g in range(PASSES):
                 nc.tensor.matmul_mx(
@@ -293,6 +308,9 @@ def tile_attend_gkl_w_clip_kernel(tc, xT, wT, y, wt, xn, xm, offs, out):
                     start=(g == 0),
                     stop=(g == PASSES - 1),
                 )
+            return acc
+
+        def leave_psum(acc, slots, name):
             dw = sb([P, slots.stop - slots.start], F32, name)
             nc.scalar.activation(dw[:], acc[:, slots], ACT.Copy, scale=-1.0)
             return dw
@@ -304,36 +322,67 @@ def tile_attend_gkl_w_clip_kernel(tc, xT, wT, y, wt, xn, xm, offs, out):
         def store(b):
             nc.sync.dma_start(out[b * P : (b + 1) * P, :], windows[b % WINDOWS][:])
 
-        for g in range(PASSES):
-            scale_rows(g, first)
+        weave_x(0, 0, X0_VECTOR, x_raw0[:, 0:X0_VECTOR, :, :], True)
+        weave_x(0, X0_VECTOR, P, x_raw0[:, X0_VECTOR:, :, :], False)
+        for t0, t1 in ((0, 1), (1, 2), (2, 4)):
+            score(0, t0, t1)
+        weave_x(1, 0, m_half, x_raw1[0], False)
+        weave_x(1, m_half + X1_VECTOR, P, x_raw1[1][:, X1_VECTOR:, :, :], False)
+        weave_x(1, m_half, m_half + X1_VECTOR, x_raw1[1][:, 0:X1_VECTOR, :, :], True)
+        exponential(0)
+        exponential(1)
+        score(1, 0, 2)
+        difference(0)
+        exponential(2)
+        difference(1)
+        exponential(3)
+        score(1, 2, 4)
+        difference(2)
+        square_sums(0)
+        exponential(4)
+        difference(3)
+        exponential(5)
+        difference(4)
+        row_roots(0)
+        exponential(6)
+        exponential(7)
+        row_factors(0)
+        difference(5)
+        difference(6)
+        difference(7)
+        square_sums(1)
+        scale_rows(0, first, range(PACK), True)
+        row_roots(1)
         weave_m(0)
-        for slots, on_vector in ((slice(0, G0_VECTOR), True), (slice(G0_VECTOR, HALF), False)):
-            copy(on_vector, g_bf[0][:, slots, :], g_rows[:, 0, :, slots].rearrange("p t i -> p i t"))
+        weave_g0()
+        scale_rows(0, second, range(PACK), False)
+        weave_g(0)
+        row_factors(1)
         quantize_m(0)
-        weave_g(1, first, True)
-        for g in range(PASSES):
-            quantize_g(g, first)
+        quantize_g(0, first)
+        for q in range(2):
+            scale_and_weave(1, slice(q * QUARTER, (q + 1) * QUARTER))
+        for q in range(2):
+            quantize_g(1, slice(q * QUARTER, (q + 1) * QUARTER))
+        early0 = leave_psum(multiply(0, 0, "early0"), first, "early0")
         weave_m(1)
-        early0 = multiply(0, first, 0, "early0")
-
-        for g in range(PASSES):
-            scale_rows(g, second)
-        weave_g(0, second, False)
-        quantize_m(1)
         quantize_g(0, second)
-        weave_g(1, second, False)
-        early1 = multiply(1, first, 1, "early1")
+        scale_rows(1, second, range(PACK), True)
+        quantize_m(1)
+        acc1 = multiply(1, 1, "early1")
+        weave_g(1)
+        early1 = leave_psum(acc1, first, "early1")
         scatter(0, first, early0)
         quantize_g(1, second)
         scatter(1, first, early1)
 
         for b in range(EARLY_BLOCKS):
             weave_m(EARLY_BLOCKS + b)
-            late = multiply(b, second, EARLY_BLOCKS + b, f"late{b}")
+            late = leave_psum(multiply(b, EARLY_BLOCKS + b, f"late{b}"), second, f"late{b}")
             quantize_m(EARLY_BLOCKS + b)
             scatter(b, second, late)
             store(b)
         for b in range(EARLY_BLOCKS, D_BLOCKS):
-            dw = multiply(b, whole, EARLY_BLOCKS + b, f"dw{b}")
+            dw = leave_psum(multiply(b, EARLY_BLOCKS + b, f"dw{b}"), whole, f"dw{b}")
             scatter(b, whole, dw)
             store(b)

@@ -34,7 +34,7 @@ EARLY_BLOCKS = 2
 WINDOWS = 3
 WINDOWS_ON_VECTOR = 2
 
-X0_VECTOR = 76
+X0_VECTOR = 84
 X1_VECTOR = 32
 G0_VECTOR = 255
 M0_VECTOR = 127
@@ -57,6 +57,7 @@ def tile_attend_gkl_w_clip_kernel(tc, xT, wT, y, wt, xn, xm, offs, out):
             "g_bf1_1": "m_bf1",
             "m_bf2": "g_bf1_1",
             "g_rows1_1": "g_bf1_0",
+            "factor1": "y_pair1_2",
         }
 
         def slot_of(name):
@@ -154,9 +155,7 @@ def tile_attend_gkl_w_clip_kernel(tc, xT, wT, y, wt, xn, xm, offs, out):
         def weave_x(g, m0, m1, raw, on_vector):
             woven = x_bf[g][:, :, m0:m1, :]
             if on_vector:
-                nc.vector.tensor_copy(
-                    woven.rearrange("p (u t) m j -> p u m j t", u=2), raw.rearrange("p m j (u t) -> p u m j t", u=2)
-                )
+                nc.vector.tensor_copy(woven.rearrange("p t m j -> p m j t"), raw)
             else:
                 nc.scalar.activation(woven.rearrange("p t m j -> p m j t"), raw, ACT.Copy)
 
@@ -357,8 +356,8 @@ def tile_attend_gkl_w_clip_kernel(tc, xT, wT, y, wt, xn, xm, offs, out):
         weave_g0()
         scale_rows(0, second, range(PACK), False)
         weave_g(0)
-        row_factors(1)
         quantize_m(0)
+        row_factors(1)
         quantize_g(0, first)
         for q in range(2):
             scale_and_weave(1, slice(q * QUARTER, (q + 1) * QUARTER))

@@ -1,6 +1,7 @@
 from contextlib import ExitStack
 
 import concourse.mybir as mybir
+from concourse.masks import make_identity
 
 N, T, D, R = 512, 2048, 512, 1024
 CLIP = 1.4
@@ -24,20 +25,15 @@ PASSES = R // K_PASS
 D_BLOCKS = D // P
 RUN = 4
 LIST_GROUP = 16
-
 TILES = PASSES * PACK
 LAST_TILE = TILES - 1
 HALF = N // 2
-QUARTER = N // 4
-EARLY_BLOCKS = 2
-
 WINDOWS = 3
 WINDOWS_ON_VECTOR = 2
 
-X0_VECTOR = 84
-X1_VECTOR = 32
-G0_VECTOR = 255
-M0_VECTOR = 127
+PAIR_VECTOR = (40, 60)
+X_GPSIMD_CUTS = (0, 22, 44, 64)
+G0_BEFORE_BOUND = 192
 
 
 def tile_attend_gkl_w_clip_kernel(tc, xT, wT, y, wt, xn, xm, offs, out):
@@ -47,17 +43,18 @@ def tile_attend_gkl_w_clip_kernel(tc, xT, wT, y, wt, xn, xm, offs, out):
         psum = ctx.enter_context(tc.psum_pool(name="psum", bufs=1))
 
         follows = {
+            "x_codes1_0": "neg_max1",
+            "x_codes1_2": "neg_max2",
+            "m_bf0_0": "y_pair0_2",
             "neg_max6": "sumsq0",
             "neg_max7": "sums_sq0",
-            "g_bf0_0": "length",
-            "m_bf0": "e6",
-            "g_rows0_1": "e7",
+            "m_bf0_1": "e6",
             "m_bf1": "sumsq1",
-            "g_bf1_0": "m_bf0",
-            "g_bf1_1": "m_bf1",
+            "m_codes0_0": "sums_sq1",
             "m_bf2": "g_bf1_1",
-            "g_rows1_1": "g_bf1_0",
-            "factor1": "y_pair1_2",
+            "m_bf3": "early_sums",
+            "g_bf0_0": "length",
+            "late_bf": "y_pair1_2",
         }
 
         def slot_of(name):
@@ -66,49 +63,42 @@ def tile_attend_gkl_w_clip_kernel(tc, xT, wT, y, wt, xn, xm, offs, out):
         def sb(shape, dtype, name):
             return keep.tile(shape, dtype, name=name, tag=slot_of(name), align_bytes=64)
 
+        def bank(index, name, width):
+            return psum.tile([P, width], F32, name=name, tag=f"bank{index}")
+
         offsets = keep.tile([P, N // LIST_GROUP], U16, name="offsets")
         w_rows = wT.rearrange("(p j) c -> p j c", j=PACK)
         x_rows = xT.rearrange("b (p j) r -> p (b j) r", j=PACK)
         y_rows = y.rearrange("b (g p t) i -> p (b g) t i", g=PASSES, t=PACK)
         xm_rows = xm.rearrange("b (g p t) d -> p (b g) t d", g=PASSES, t=PACK)
-        w_plane = []
-        y_sb = []
 
-        def load_w(j):
-            plane = sb([P, T], F32, f"w_plane{j}")
-            nc.sync.dma_start(plane[:], w_rows[:, j, :])
-            w_plane.append(plane)
+        def load(name, shape, source):
+            tile = sb(shape, F32, name)
+            nc.sync.dma_start(tile[:], source)
+            return tile
 
         def load_x(name, r0, r1):
-            raw = sb([P, PACK, r1 - r0], F32, name)
-            nc.sync.dma_start(raw[:], x_rows[:, :, r0:r1])
-            return raw[:].rearrange("p j (m t) -> p m j t", t=PACK)
+            return load(name, [P, PACK, r1 - r0], x_rows[:, :, r0:r1])[:].rearrange("p j (m t) -> p m j t", t=PACK)
 
         def load_y(g, t0):
-            pair = sb([P, 2, N], F32, f"y_pair{g}_{t0}")
-            nc.sync.dma_start(pair[:], y_rows[:, g, t0 : t0 + 2, :])
-            y_sb.extend([pair[:, 0, :], pair[:, 1, :]])
+            return load(f"y_pair{g}_{t0}", [P, 2, N], y_rows[:, g, t0 : t0 + 2, :])
 
         def load_per_row(name, values):
-            per_row = sb([P, PASSES, PACK], F32, name)
-            nc.sync.dma_start(per_row[:], values.rearrange("b (g p t) o -> p (b g) (t o)", g=PASSES, t=PACK))
-            return per_row
+            return load(name, [P, PASSES, PACK], values.rearrange("b (g p t) o -> p (b g) (t o)", g=PASSES, t=PACK))
 
         rows_half, m_half = K_PASS // 2, P // 2
-        load_w(0)
+        w_plane = [load("w_plane0", [P, T], w_rows[:, 0, :])]
         nc.sync.dma_start(offsets[:], offs)
         xn_sb = load_per_row("xn_sb", xn)
-        for j in range(1, PACK):
-            load_w(j)
+        w_plane.extend(load(f"w_plane{j}", [P, T], w_rows[:, j, :]) for j in range(1, PACK))
         x_raw0 = load_x("x_raw0", 0, K_PASS)
         x_raw1 = [load_x(f"x_raw1_{h}", K_PASS + h * rows_half, K_PASS + (h + 1) * rows_half) for h in range(2)]
-        for g in range(PASSES):
-            for t0 in (0, 2):
-                load_y(g, t0)
+        y_pair = [load_y(0, 0), load_y(0, 2)]
+        xm_raw = [load("xm_raw0", [P, PACK, D], xm_rows[:, 0, :, :])]
+        y_pair.extend([load_y(1, 0), load_y(1, 2)])
         wt_sb = load_per_row("wt_sb", wt)
-        xm_raw = sb([P, PASSES, PACK, D], F32, "xm_raw")
-        for g in range(PASSES):
-            nc.sync.dma_start(xm_raw[:, g, :, :], xm_rows[:, g, :, :])
+        xm_raw.append(load("xm_raw1", [P, PACK, D], xm_rows[:, 1, :, :]))
+        y_sb = [y_pair[k // 2][:, k % 2, :] for k in range(TILES)]
 
         minus_half = sb([P, PACK], F32, "minus_half")
         ones = sb([P, PACK], F32, "ones")
@@ -116,6 +106,10 @@ def tile_attend_gkl_w_clip_kernel(tc, xT, wT, y, wt, xn, xm, offs, out):
         nc.scalar.activation(minus_half[:], ones[:], ACT.Copy, scale=-0.5)
         half = sb([P, TILES], F32, "half")
         nc.gpsimd.memset(half[:], 0.5)
+        identity = sb([P, P], F32, "identity")
+        make_identity(nc, identity[:])
+        factor_square = sb([P, P], F32, "factor_square")
+        nc.vector.memset(factor_square[:], 0.0)
 
         windows = []
         for w in range(WINDOWS):
@@ -147,42 +141,60 @@ def tile_attend_gkl_w_clip_kernel(tc, xT, wT, y, wt, xn, xm, offs, out):
             out=w_codes[:].bitcast(E4M3), scales=w_scales[:], in_=w_bf[:].rearrange("p i j -> p (i j)")
         )
 
-        x_codes = sb([P, TILES, P], U32, "x_codes")
-        x_scales = sb([P, TILES, P], U8, "x_scales")
         x_bf = [sb([P, PACK, P, PACK], BF16, f"x_bf{g}") for g in range(PASSES)]
         scores = {}
 
-        def weave_x(g, m0, m1, raw, on_vector):
-            woven = x_bf[g][:, :, m0:m1, :]
-            if on_vector:
-                nc.vector.tensor_copy(woven.rearrange("p t m j -> p m j t"), raw)
-            else:
-                nc.scalar.activation(woven.rearrange("p t m j -> p m j t"), raw, ACT.Copy)
+        def weave_pair(u):
+            tiles = slice(2 * u, 2 * u + 2)
+            woven = x_bf[0][:, tiles, :, :].rearrange("p t m j -> p m j t")
+            cut = PAIR_VECTOR[u]
+            nc.vector.tensor_copy(woven[:, 0:cut, :, :], x_raw0[:, 0:cut, :, tiles])
+            nc.scalar.activation(woven[:, cut:, :, :], x_raw0[:, cut:, :, tiles], ACT.Copy)
 
         def score(g, t0, t1):
-            k0, k1 = PACK * g + t0, PACK * g + t1
+            codes = sb([P, t1 - t0, P], U32, f"x_codes{g}_{t0}")
+            scales = sb([P, t1 - t0, P], U8, f"x_scales{g}_{t0}")
             nc.vector.quantize_mx(
-                out=x_codes[:, k0:k1, :].rearrange("p t m -> p (t m)").bitcast(E4M3),
-                scales=x_scales[:, k0:k1, :].rearrange("p t m -> p (t m)"),
+                out=codes[:].rearrange("p t m -> p (t m)").bitcast(E4M3),
+                scales=scales[:].rearrange("p t m -> p (t m)"),
                 in_=x_bf[g][:, t0:t1, :, :].rearrange("p t m j -> p (t m j)"),
             )
-            for k in range(k0, k1):
-                scores[k] = psum.tile([P, N], F32, name=f"scores{k}", tag=f"bank{k}")
+            for t in range(t0, t1):
+                k = PACK * g + t
+                scores[k] = bank(k, f"scores{k}", N)
                 nc.tensor.matmul_mx(
                     out=scores[k][:],
-                    lhsT=x_codes[:, k, :].bitcast(E4M3),
-                    lhsT_scale=x_scales[:, k, :],
+                    lhsT=codes[:, t - t0, :].bitcast(E4M3),
+                    lhsT_scale=scales[:, t - t0, :],
                     rhs=w_codes[:].bitcast(E4M3),
                     rhs_scale=w_scales[:],
                     start=True,
                     stop=True,
                 )
 
+        weave_pair(0)
+        score(0, 0, 1)
+        score(0, 1, 2)
+        weave_pair(1)
+        score(0, 2, 4)
+        nc.scalar.activation(x_bf[1][:, :, 0:m_half, :].rearrange("p t m j -> p m j t"), x_raw1[0], ACT.Copy)
+        for m0, m1 in zip(X_GPSIMD_CUTS, X_GPSIMD_CUTS[1:]):
+            nc.gpsimd.tensor_scalar(
+                x_bf[1][:, :, m_half + m0 : m_half + m1, :].rearrange("p t m j -> p m t j"),
+                x_raw1[1][:, m0:m1, :, :].rearrange("p m j t -> p m t j"),
+                1.0,
+                0.0,
+                ALU.mult,
+                ALU.add,
+            )
+
         diffs = [sb([P, PACK, N], F32, f"diffs{g}") for g in range(PASSES)]
         e = [sb([P, N], F32, f"e{k}") for k in range(TILES)]
         sums = [sb([P, PACK], F32, f"sums{g}") for g in range(PASSES)]
         sumsq = [sb([P, PACK], F32, f"sumsq{g}") for g in range(PASSES)]
-        sums_sq, root, factor = {}, {}, {}
+        sums_sq, root = {}, {}
+
+        late_bf = sb([P, PACK * G0_BEFORE_BOUND + N], BF16, "late_bf")
 
         def exponential(k):
             g, t = divmod(k, PACK)
@@ -194,8 +206,9 @@ def tile_attend_gkl_w_clip_kernel(tc, xT, wT, y, wt, xn, xm, offs, out):
             g, t = divmod(k, PACK)
             col = slice(t, t + 1)
             nc.vector.scalar_tensor_tensor(diffs[g][:, t, :], y_sb[k], sums[g][:, col], e[k][:], ALU.mult, ALU.subtract)
+            spent = late_bf[:, PACK * G0_BEFORE_BOUND :] if k == LAST_TILE else e[k][:]
             nc.scalar.activation(
-                e[k][:], diffs[g][:, t, :], ACT.Square, scale=length[:, k : k + 1], accum_out=sumsq[g][:, col]
+                spent, diffs[g][:, t, :], ACT.Square, scale=length[:, k : k + 1], accum_out=sumsq[g][:, col]
             )
 
         def square_sums(g):
@@ -208,105 +221,63 @@ def tile_attend_gkl_w_clip_kernel(tc, xT, wT, y, wt, xn, xm, offs, out):
             root[g] = sb([P, PACK], F32, f"root{g}")
             nc.gpsimd.tensor_tensor(root[g][:], larger[:], minus_half[:], ALU.pow)
 
-        def row_factors(g):
-            factor[g] = sb([P, PACK], F32, f"factor{g}")
-            nc.vector.tensor_tensor(factor[g][:], root[g][:], wt_sb[:, g, :], ALU.mult)
-
-        g_rows, g_bf = {}, {}
-
-        def woven_g(g, slots):
-            h = slots.start // HALF
-            if (g, h) not in g_bf:
-                g_bf[g, h] = sb([P, HALF, PACK], BF16, f"g_bf{g}_{h}")
-            return g_bf[g, h][:, slots.start - h * HALF : slots.stop - h * HALF, :]
-
-        def scale_and_weave(g, slots):
+        def scale_and_weave(woven, g, slots, factor):
             runs = (slots.stop - slots.start) // RUN
             nc.vector.tensor_tensor(
-                woven_g(g, slots).rearrange("p (c i) t -> p c t i", i=RUN),
+                woven.rearrange("p (c i) t -> p c t i", i=RUN),
                 diffs[g][:, :, slots].rearrange("p t (c i) -> p c t i", i=RUN),
-                factor[g][:].unsqueeze(1).unsqueeze(3).to_broadcast([P, runs, PACK, RUN]),
+                factor.unsqueeze(1).unsqueeze(3).to_broadcast([P, runs, PACK, RUN]),
                 ALU.mult,
             )
 
-        def scale_rows(g, slots, tiles, on_vector):
-            h = slots.start // HALF
-            if (g, h) not in g_rows:
-                if (g, h) == (0, 0):
-                    g_rows[g, h] = y_sb[LAST_TILE].bitcast(BF16).rearrange("p (t i) -> p t i", t=PACK)
-                else:
-                    g_rows[g, h] = sb([P, PACK, HALF], BF16, f"g_rows{g}_{h}")
-            for t in tiles:
-                col = factor[g][:, t : t + 1]
-                if on_vector:
-                    nc.vector.tensor_scalar(g_rows[g, h][:, t, :], diffs[g][:, t, slots], col, None, ALU.mult)
-                else:
-                    nc.scalar.activation(g_rows[g, h][:, t, :], diffs[g][:, t, slots], ACT.Copy, scale=col)
-
-        def weave_g(g):
-            nc.scalar.copy(
-                woven_g(g, second).rearrange("p (c i) t -> p c t i", i=RUN),
-                g_rows[g, 1][:].rearrange("p t (c i) -> p c t i", i=RUN),
-            )
-
-        def weave_g0():
-            rows = g_rows[0, 0].rearrange("p t i -> p i t")
-            nc.vector.tensor_copy(woven_g(0, slice(0, G0_VECTOR)), rows[:, 0:G0_VECTOR, :])
-            nc.scalar.copy(woven_g(0, slice(G0_VECTOR, HALF)), rows[:, G0_VECTOR:, :])
-
-        def quantize_g(g, slots):
+        def quantize_g(g, slots, woven):
             nc.vector.quantize_mx(
                 out=g_codes[g][:, slots].bitcast(E5M2),
                 scales=g_scales[g][:, slots],
-                in_=woven_g(g, slots).rearrange("p i t -> p (i t)"),
+                in_=woven.rearrange("p i t -> p (i t)"),
             )
 
-        m_codes = sb([P, D_BLOCKS, PASSES, P], U32, "m_codes")
-        m_scales = sb([P, D_BLOCKS, PASSES, P], U8, "m_scales")
-        m_bf = {}
-        late_pair = []
+        m_codes, m_scales = {}, {}
 
-        def weave_m(b):
-            if b == EARLY_BLOCKS + 1:
-                m_bf[b] = late_pair[0][:, 1, :, :, :]
-            elif b == EARLY_BLOCKS:
-                late_pair.append(sb([P, 2, PASSES, P, PACK], BF16, f"m_bf{b}"))
-                m_bf[b] = late_pair[0][:, 0, :, :, :]
-            else:
-                m_bf[b] = sb([P, PASSES, P, PACK], BF16, f"m_bf{b}")[:]
+        def weave_m(woven, b, g):
+            nc.scalar.copy(
+                woven.rearrange("p (c i) t -> p c t i", i=RUN),
+                xm_raw[g][:, :, b * P : (b + 1) * P].rearrange("p t (c i) -> p c t i", i=RUN),
+            )
+
+        def weave_block(b):
+            woven = sb([P, PASSES, P, PACK], BF16, f"m_bf{b}")
             for g in range(PASSES):
-                nc.scalar.copy(
-                    m_bf[b][:, g, :, :].rearrange("p (c i) t -> p c t i", i=RUN),
-                    xm_raw[:, g, :, b * P : (b + 1) * P].rearrange("p t (c i) -> p c t i", i=RUN),
-                )
+                weave_m(woven[:, g, :, :], b, g)
+            return woven[:]
 
-        def weave_m0():
-            m_bf[0] = sb([P, PASSES, P, PACK], BF16, "m_bf0")[:]
-            for g in range(PASSES):
-                nc.vector.tensor_copy(
-                    m_bf[0][:, g, 0:M0_VECTOR, :], xm_raw[:, g, :, 0:M0_VECTOR].rearrange("p t m -> p m t")
-                )
-            nc.scalar.copy(m_bf[0][:, :, M0_VECTOR:, :], xm_raw[:, :, :, M0_VECTOR:P].rearrange("p g t m -> p g m t"))
-
-        def quantize_m(b):
+        def quantize_m(b, g0, woven):
+            passes = woven.shape[1]
+            codes = sb([P, passes, P], U32, f"m_codes{b}_{g0}")
+            scales = sb([P, passes, P], U8, f"m_scales{b}_{g0}")
             nc.vector.quantize_mx(
-                out=m_codes[:, b, :, :].rearrange("p g m -> p (g m)").bitcast(E4M3),
-                scales=m_scales[:, b, :, :].rearrange("p g m -> p (g m)"),
-                in_=m_bf[b].rearrange("p g m t -> p (g m t)"),
+                out=codes[:].rearrange("p g m -> p (g m)").bitcast(E4M3),
+                scales=scales[:].rearrange("p g m -> p (g m)"),
+                in_=woven.rearrange("p g m t -> p (g m t)"),
+            )
+            for g in range(passes):
+                m_codes[b, g0 + g], m_scales[b, g0 + g] = codes[:, g, :], scales[:, g, :]
+
+        def multiply(acc, b, g):
+            nc.tensor.matmul_mx(
+                out=acc[:],
+                lhsT=m_codes[b, g].bitcast(E4M3),
+                lhsT_scale=m_scales[b, g],
+                rhs=g_codes[g][:].bitcast(E5M2),
+                rhs_scale=g_scales[g][:],
+                start=(g == 0),
+                stop=(g == PASSES - 1),
             )
 
-        def multiply(b, bank, name):
-            acc = psum.tile([P, N], F32, name=f"acc_{name}", tag=f"bank{bank}")
+        def product(b, index, name):
+            acc = bank(index, f"acc_{name}", N)
             for g in range(PASSES):
-                nc.tensor.matmul_mx(
-                    out=acc[:],
-                    lhsT=m_codes[:, b, g, :].bitcast(E4M3),
-                    lhsT_scale=m_scales[:, b, g, :],
-                    rhs=g_codes[g][:].bitcast(E5M2),
-                    rhs_scale=g_scales[g][:],
-                    start=(g == 0),
-                    stop=(g == PASSES - 1),
-                )
+                multiply(acc, b, g)
             return acc
 
         def leave_psum(acc, slots, name):
@@ -321,67 +292,84 @@ def tile_attend_gkl_w_clip_kernel(tc, xT, wT, y, wt, xn, xm, offs, out):
         def store(b):
             nc.sync.dma_start(out[b * P : (b + 1) * P, :], windows[b % WINDOWS][:])
 
-        weave_x(0, 0, X0_VECTOR, x_raw0[:, 0:X0_VECTOR, :, :], True)
-        weave_x(0, X0_VECTOR, P, x_raw0[:, X0_VECTOR:, :, :], False)
-        for t0, t1 in ((0, 1), (1, 2), (2, 4)):
-            score(0, t0, t1)
-        weave_x(1, 0, m_half, x_raw1[0], False)
-        weave_x(1, m_half + X1_VECTOR, P, x_raw1[1][:, X1_VECTOR:, :, :], False)
-        weave_x(1, m_half, m_half + X1_VECTOR, x_raw1[1][:, 0:X1_VECTOR, :, :], True)
-        exponential(0)
-        exponential(1)
-        score(1, 0, 2)
+        for k in range(PACK):
+            exponential(k)
         difference(0)
-        exponential(2)
         difference(1)
-        exponential(3)
-        score(1, 2, 4)
+        score(1, 0, 2)
         difference(2)
+        score(1, 2, 4)
         square_sums(0)
-        exponential(4)
         difference(3)
+        m_bf00 = sb([P, 1, P, PACK], BF16, "m_bf0_0")
+        nc.gpsimd.tensor_scalar(
+            m_bf00[:, 0, :, :], xm_raw[0][:, :, 0:P].rearrange("p t m -> p m t"), 1.0, 0.0, ALU.mult, ALU.add
+        )
+        exponential(4)
         exponential(5)
-        difference(4)
         row_roots(0)
         exponential(6)
         exponential(7)
-        row_factors(0)
-        difference(5)
-        difference(6)
-        difference(7)
+        nc.gpsimd.tensor_tensor(factor_square[:, 0:PACK], root[0][:], wt_sb[:, 0, :], ALU.mult)
+        turned = bank(0, "turned", P)
+        nc.tensor.transpose(turned[:], factor_square[:], identity[:])
+        difference(4)
+        turned_sb = sb([P, P], F32, "turned_sb")
+        nc.scalar.copy(turned_sb[:], turned[:])
+        factor0 = bank(1, "factor0", P)
+        nc.tensor.transpose(factor0[:], turned_sb[:], identity[:])
+        for k in range(PACK + 1, TILES):
+            difference(k)
         square_sums(1)
-        scale_rows(0, first, range(PACK), True)
+        g_bf01 = late_bf[:, 0 : PACK * HALF].rearrange("p (i t) -> p i t", t=PACK)
+        cut = G0_BEFORE_BOUND
+        scale_and_weave(g_bf01[:, 0:cut, :], 0, slice(HALF, HALF + cut), factor_square[:, 0:PACK])
         row_roots(1)
-        weave_m(0)
-        weave_g0()
-        scale_rows(0, second, range(PACK), False)
-        weave_g(0)
-        quantize_m(0)
-        row_factors(1)
-        quantize_g(0, first)
-        for q in range(2):
-            scale_and_weave(1, slice(q * QUARTER, (q + 1) * QUARTER))
-        for q in range(2):
-            quantize_g(1, slice(q * QUARTER, (q + 1) * QUARTER))
-        early0 = leave_psum(multiply(0, 0, "early0"), first, "early0")
-        weave_m(1)
-        quantize_g(0, second)
-        scale_rows(1, second, range(PACK), True)
-        quantize_m(1)
-        acc1 = multiply(1, 1, "early1")
-        weave_g(1)
-        early1 = leave_psum(acc1, first, "early1")
-        scatter(0, first, early0)
-        quantize_g(1, second)
-        scatter(1, first, early1)
+        g_bf00 = sb([P, HALF, PACK], BF16, "g_bf0_0")
+        scale_and_weave(g_bf00[:], 0, first, factor0[:, 0:PACK])
+        scale_and_weave(g_bf01[:, cut:, :], 0, slice(HALF + cut, N), factor0[:, 0:PACK])
+        m_bf01 = sb([P, 1, P, PACK], BF16, "m_bf0_1")
+        weave_m(m_bf01[:, 0, :, :], 0, 1)
+        m_bf1 = weave_block(1)
 
-        for b in range(EARLY_BLOCKS):
-            weave_m(EARLY_BLOCKS + b)
-            late = leave_psum(multiply(b, EARLY_BLOCKS + b, f"late{b}"), second, f"late{b}")
-            quantize_m(EARLY_BLOCKS + b)
-            scatter(b, second, late)
-            store(b)
-        for b in range(EARLY_BLOCKS, D_BLOCKS):
-            dw = leave_psum(multiply(b, EARLY_BLOCKS + b, f"dw{b}"), whole, f"dw{b}")
+        quantize_m(0, 0, m_bf00[:])
+        factor1 = sb([P, PACK], F32, "factor1")
+        nc.vector.tensor_tensor(factor1[:], root[1][:], wt_sb[:, 1, :], ALU.mult)
+        quantize_g(0, first, g_bf00[:])
+        early = bank(2, "acc_early", N)
+        multiply(early, 0, 0)
+        g_bf10 = sb([P, HALF, PACK], BF16, "g_bf1_0")
+        quarters = (slice(0, HALF // 2), slice(HALF // 2, HALF))
+        for slots in quarters:
+            scale_and_weave(g_bf10[:, slots, :], 1, slots, factor1[:])
+        quantize_m(0, 1, m_bf01[:])
+        for slots in quarters:
+            quantize_g(1, slots, g_bf10[:, slots, :])
+        multiply(early, 0, 1)
+
+        g_rows = sb([P, PACK, HALF], BF16, "g_rows")
+        for t in range(PACK):
+            nc.scalar.activation(g_rows[:, t, :], diffs[1][:, t, second], ACT.Copy, scale=factor1[:, t : t + 1])
+        g_bf11 = sb([P, HALF, PACK], BF16, "g_bf1_1")
+        nc.scalar.copy(
+            g_bf11[:].rearrange("p (c i) t -> p c t i", i=RUN), g_rows[:].rearrange("p t (c i) -> p c t i", i=RUN)
+        )
+        early_sums = leave_psum(early, first, "early_sums")
+        quantize_g(0, second, g_bf01)
+        quantize_m(1, 0, m_bf1)
+        quantize_g(1, second, g_bf11[:])
+        scatter(0, first, early_sums)
+
+        m_bf2 = weave_block(2)
+        late_sums = leave_psum(product(0, 3, "late"), second, "late_sums")
+        quantize_m(2, 0, m_bf2)
+        scatter(0, second, late_sums)
+        store(0)
+        dw = leave_psum(product(1, 4, "dw1"), whole, "dw1")
+        quantize_m(3, 0, weave_block(3))
+        scatter(1, whole, dw)
+        store(1)
+        for b in range(2, D_BLOCKS):
+            dw = leave_psum(product(b, 3 + b, f"dw{b}"), whole, f"dw{b}")
             scatter(b, whole, dw)
             store(b)

@@ -33,6 +33,7 @@ WINDOWS_ON_VECTOR = 2
 
 PAIR_VECTOR = (40, 60)
 X_GPSIMD_CUTS = (0, 22, 44, 64)
+G1_VECTOR = 96
 G0_BEFORE_BOUND = 192
 
 
@@ -45,10 +46,9 @@ def tile_attend_gkl_w_clip_kernel(tc, xT, wT, y, wt, xn, xm, offs, out):
         follows = {
             "x_codes1_0": "neg_max1",
             "x_codes1_2": "neg_max2",
-            "m_bf0_0": "y_pair0_2",
             "neg_max6": "sumsq0",
             "neg_max7": "sums_sq0",
-            "m_bf0_1": "e6",
+            "m_bf0": "e6",
             "m_bf1": "sumsq1",
             "m_codes0_0": "sums_sq1",
             "m_bf2": "g_bf1_1",
@@ -301,16 +301,12 @@ def tile_attend_gkl_w_clip_kernel(tc, xT, wT, y, wt, xn, xm, offs, out):
         score(1, 2, 4)
         square_sums(0)
         difference(3)
-        m_bf00 = sb([P, 1, P, PACK], BF16, "m_bf0_0")
-        nc.gpsimd.tensor_scalar(
-            m_bf00[:, 0, :, :], xm_raw[0][:, :, 0:P].rearrange("p t m -> p m t"), 1.0, 0.0, ALU.mult, ALU.add
-        )
         exponential(4)
         exponential(5)
         row_roots(0)
         exponential(6)
         exponential(7)
-        nc.gpsimd.tensor_tensor(factor_square[:, 0:PACK], root[0][:], wt_sb[:, 0, :], ALU.mult)
+        nc.vector.tensor_tensor(factor_square[:, 0:PACK], root[0][:], wt_sb[:, 0, :], ALU.mult)
         turned = bank(0, "turned", P)
         nc.tensor.transpose(turned[:], factor_square[:], identity[:])
         difference(4)
@@ -328,11 +324,10 @@ def tile_attend_gkl_w_clip_kernel(tc, xT, wT, y, wt, xn, xm, offs, out):
         g_bf00 = sb([P, HALF, PACK], BF16, "g_bf0_0")
         scale_and_weave(g_bf00[:], 0, first, factor0[:, 0:PACK])
         scale_and_weave(g_bf01[:, cut:, :], 0, slice(HALF + cut, N), factor0[:, 0:PACK])
-        m_bf01 = sb([P, 1, P, PACK], BF16, "m_bf0_1")
-        weave_m(m_bf01[:, 0, :, :], 0, 1)
+        m_bf0 = weave_block(0)
         m_bf1 = weave_block(1)
 
-        quantize_m(0, 0, m_bf00[:])
+        quantize_m(0, 0, m_bf0[:, 0:1, :, :])
         factor1 = sb([P, PACK], F32, "factor1")
         nc.vector.tensor_tensor(factor1[:], root[1][:], wt_sb[:, 1, :], ALU.mult)
         quantize_g(0, first, g_bf00[:])
@@ -342,19 +337,24 @@ def tile_attend_gkl_w_clip_kernel(tc, xT, wT, y, wt, xn, xm, offs, out):
         quarters = (slice(0, HALF // 2), slice(HALF // 2, HALF))
         for slots in quarters:
             scale_and_weave(g_bf10[:, slots, :], 1, slots, factor1[:])
-        quantize_m(0, 1, m_bf01[:])
+        quantize_m(0, 1, m_bf0[:, 1:2, :, :])
         for slots in quarters:
             quantize_g(1, slots, g_bf10[:, slots, :])
         multiply(early, 0, 1)
 
-        g_rows = sb([P, PACK, HALF], BF16, "g_rows")
+        share = HALF - G1_VECTOR
+        g_rows = sb([P, PACK, share], BF16, "g_rows")
         for t in range(PACK):
-            nc.scalar.activation(g_rows[:, t, :], diffs[1][:, t, second], ACT.Copy, scale=factor1[:, t : t + 1])
+            nc.scalar.activation(
+                g_rows[:, t, :], diffs[1][:, t, HALF : HALF + share], ACT.Copy, scale=factor1[:, t : t + 1]
+            )
         g_bf11 = sb([P, HALF, PACK], BF16, "g_bf1_1")
         nc.scalar.copy(
-            g_bf11[:].rearrange("p (c i) t -> p c t i", i=RUN), g_rows[:].rearrange("p t (c i) -> p c t i", i=RUN)
+            g_bf11[:, 0:share, :].rearrange("p (c i) t -> p c t i", i=RUN),
+            g_rows[:].rearrange("p t (c i) -> p c t i", i=RUN),
         )
         early_sums = leave_psum(early, first, "early_sums")
+        scale_and_weave(g_bf11[:, share:, :], 1, slice(HALF + share, N), factor1[:])
         quantize_g(0, second, g_bf01)
         quantize_m(1, 0, m_bf1)
         quantize_g(1, second, g_bf11[:])

@@ -32,7 +32,7 @@ WINDOWS = 3
 WINDOWS_ON_VECTOR = 2
 
 PAIR_VECTOR = (40, 60)
-X_GPSIMD_CUTS = (0, 22, 44, 64)
+X_GPSIMD_CUTS = (0, 21, 42)
 G1_VECTOR = 96
 G0_BEFORE_BOUND = 192
 
@@ -55,6 +55,7 @@ def tile_attend_gkl_w_clip_kernel(tc, xT, wT, y, wt, xn, xm, offs, out):
             "m_bf3": "early_sums",
             "g_bf0_0": "length",
             "late_bf": "y_pair1_2",
+            "neg_max5": "e3",
         }
 
         def slot_of(name):
@@ -178,6 +179,10 @@ def tile_attend_gkl_w_clip_kernel(tc, xT, wT, y, wt, xn, xm, offs, out):
         weave_pair(1)
         score(0, 2, 4)
         nc.scalar.activation(x_bf[1][:, :, 0:m_half, :].rearrange("p t m j -> p m j t"), x_raw1[0], ACT.Copy)
+        m_rest = X_GPSIMD_CUTS[-1]
+        nc.scalar.activation(
+            x_bf[1][:, :, m_half + m_rest :, :].rearrange("p t m j -> p m j t"), x_raw1[1][:, m_rest:, :, :], ACT.Copy
+        )
         for m0, m1 in zip(X_GPSIMD_CUTS, X_GPSIMD_CUTS[1:]):
             nc.gpsimd.tensor_scalar(
                 x_bf[1][:, :, m_half + m0 : m_half + m1, :].rearrange("p t m j -> p m t j"),
@@ -298,12 +303,12 @@ def tile_attend_gkl_w_clip_kernel(tc, xT, wT, y, wt, xn, xm, offs, out):
         difference(1)
         score(1, 0, 2)
         difference(2)
+        difference(3)
         score(1, 2, 4)
         square_sums(0)
-        difference(3)
         exponential(4)
-        exponential(5)
         row_roots(0)
+        exponential(5)
         exponential(6)
         exponential(7)
         nc.vector.tensor_tensor(factor_square[:, 0:PACK], root[0][:], wt_sb[:, 0, :], ALU.mult)

@@ -95,10 +95,9 @@ def tile_attend_gkl_w_clip_kernel(tc, xT, wT, y, wt, xn, xm, offs, out):
         x_raw0 = load_x("x_raw0", 0, K_PASS)
         x_raw1 = [load_x(f"x_raw1_{h}", K_PASS + h * rows_half, K_PASS + (h + 1) * rows_half) for h in range(2)]
         y_pair = [load_y(0, 0), load_y(0, 2)]
-        xm_raw = [load("xm_raw0", [P, PACK, D], xm_rows[:, 0, :, :])]
         y_pair.extend([load_y(1, 0), load_y(1, 2)])
         wt_sb = load_per_row("wt_sb", wt)
-        xm_raw.append(load("xm_raw1", [P, PACK, D], xm_rows[:, 1, :, :]))
+        xm_raw = [load(f"xm_raw{g}", [P, PACK, D], xm_rows[:, g, :, :]) for g in range(PASSES)]
         y_sb = [y_pair[k // 2][:, k % 2, :] for k in range(TILES)]
 
         minus_half = sb([P, PACK], F32, "minus_half")

@@ -26,14 +26,13 @@ D_BLOCKS = D // P
 RUN = 4
 LIST_GROUP = 16
 TILES = PASSES * PACK
-LAST_TILE = TILES - 1
 HALF = N // 2
-WINDOWS = 3
+QUARTER = N // 4
 WINDOWS_ON_VECTOR = 2
 
 PAIR_VECTOR = (40, 60)
 X_GPSIMD_CUTS = (0, 21, 42)
-G1_VECTOR = 96
+G1_SCALAR = 128
 G0_BEFORE_BOUND = 192
 
 
@@ -46,16 +45,18 @@ def tile_attend_gkl_w_clip_kernel(tc, xT, wT, y, wt, xn, xm, offs, out):
         follows = {
             "x_codes1_0": "neg_max1",
             "x_codes1_2": "neg_max2",
+            "neg_max5": "e3",
             "neg_max6": "sumsq0",
             "neg_max7": "sums_sq0",
+            "g0_early": "y_pair1_2",
+            "g0_late": "length",
             "m_bf0": "e6",
             "m_bf1": "sumsq1",
-            "m_codes0_0": "sums_sq1",
-            "m_bf2": "g_bf1_1",
-            "m_bf3": "early_sums",
-            "g_bf0_0": "length",
-            "late_bf": "y_pair1_2",
-            "neg_max5": "e3",
+            "m_codes0": "sums_sq1",
+            "m_bf2_0": "g_rows",
+            "m_bf2_1": "g0_late",
+            "m_codes1": "g_bf1_1",
+            "m_bf3": "dw0_1",
         }
 
         def slot_of(name):
@@ -112,18 +113,14 @@ def tile_attend_gkl_w_clip_kernel(tc, xT, wT, y, wt, xn, xm, offs, out):
         nc.vector.memset(factor_square[:], 0.0)
 
         windows = []
-        for w in range(WINDOWS):
+        for w in range(D_BLOCKS):
             window = sb([P, T], F32, f"window{w}")
             engine = nc.vector if w < WINDOWS_ON_VECTOR else nc.gpsimd
             engine.memset(window[:], 0.0)
             windows.append(window)
 
         first, second, whole = slice(0, HALF), slice(HALF, N), slice(0, N)
-        g_codes = [sb([P, N], U32, f"g_codes{g}") for g in range(PASSES)]
-        g_scales = [sb([P, N], U8, f"g_scales{g}") for g in range(PASSES)]
-        for g in range(PASSES):
-            nc.vector.memset(g_codes[g][:, second], 0)
-            nc.vector.memset(g_scales[g][:, second], 0)
+        halves = (first, second)
 
         xn_over = sb([P, TILES], F32, "xn_over")
         length = sb([P, TILES], F32, "length")
@@ -198,8 +195,6 @@ def tile_attend_gkl_w_clip_kernel(tc, xT, wT, y, wt, xn, xm, offs, out):
         sumsq = [sb([P, PACK], F32, f"sumsq{g}") for g in range(PASSES)]
         sums_sq, root = {}, {}
 
-        late_bf = sb([P, PACK * G0_BEFORE_BOUND + N], BF16, "late_bf")
-
         def exponential(k):
             g, t = divmod(k, PACK)
             neg_max = sb([P, 1], F32, f"neg_max{k}")
@@ -210,9 +205,8 @@ def tile_attend_gkl_w_clip_kernel(tc, xT, wT, y, wt, xn, xm, offs, out):
             g, t = divmod(k, PACK)
             col = slice(t, t + 1)
             nc.vector.scalar_tensor_tensor(diffs[g][:, t, :], y_sb[k], sums[g][:, col], e[k][:], ALU.mult, ALU.subtract)
-            spent = late_bf[:, PACK * G0_BEFORE_BOUND :] if k == LAST_TILE else e[k][:]
             nc.scalar.activation(
-                spent, diffs[g][:, t, :], ACT.Square, scale=length[:, k : k + 1], accum_out=sumsq[g][:, col]
+                e[k][:], diffs[g][:, t, :], ACT.Square, scale=length[:, k : k + 1], accum_out=sumsq[g][:, col]
             )
 
         def square_sums(g):
@@ -234,6 +228,9 @@ def tile_attend_gkl_w_clip_kernel(tc, xT, wT, y, wt, xn, xm, offs, out):
                 ALU.mult,
             )
 
+        g_codes = [sb([P, N], U32, f"g_codes{g}") for g in range(PASSES)]
+        g_scales = [sb([P, N], U8, f"g_scales{g}") for g in range(PASSES)]
+
         def quantize_g(g, slots, woven):
             nc.vector.quantize_mx(
                 out=g_codes[g][:, slots].bitcast(E5M2),
@@ -243,21 +240,21 @@ def tile_attend_gkl_w_clip_kernel(tc, xT, wT, y, wt, xn, xm, offs, out):
 
         m_codes, m_scales = {}, {}
 
-        def weave_m(woven, b, g):
-            nc.scalar.copy(
+        def weave_m(copy, woven, b, g):
+            copy(
                 woven.rearrange("p (c i) t -> p c t i", i=RUN),
                 xm_raw[g][:, :, b * P : (b + 1) * P].rearrange("p t (c i) -> p c t i", i=RUN),
             )
 
-        def weave_block(b):
+        def weave_block(copy, b):
             woven = sb([P, PASSES, P, PACK], BF16, f"m_bf{b}")
             for g in range(PASSES):
-                weave_m(woven[:, g, :, :], b, g)
+                weave_m(copy, woven[:, g, :, :], b, g)
             return woven[:]
 
-        def quantize_m(b, g0, woven):
+        def quantize_m(b, g0, woven, name):
             passes = woven.shape[1]
-            codes = sb([P, passes, P], U32, f"m_codes{b}_{g0}")
+            codes = sb([P, passes, P], U32, name)
             scales = sb([P, passes, P], U8, f"m_scales{b}_{g0}")
             nc.vector.quantize_mx(
                 out=codes[:].rearrange("p g m -> p (g m)").bitcast(E4M3),
@@ -267,34 +264,39 @@ def tile_attend_gkl_w_clip_kernel(tc, xT, wT, y, wt, xn, xm, offs, out):
             for g in range(passes):
                 m_codes[b, g0 + g], m_scales[b, g0 + g] = codes[:, g, :], scales[:, g, :]
 
-        def multiply(acc, b, g):
-            nc.tensor.matmul_mx(
-                out=acc[:],
-                lhsT=m_codes[b, g].bitcast(E4M3),
-                lhsT_scale=m_scales[b, g],
-                rhs=g_codes[g][:].bitcast(E5M2),
-                rhs_scale=g_scales[g][:],
-                start=(g == 0),
-                stop=(g == PASSES - 1),
-            )
-
-        def product(b, index, name):
-            acc = bank(index, f"acc_{name}", N)
+        def product(b, slots, index):
+            acc = bank(index, f"acc{index}", slots.stop - slots.start)
             for g in range(PASSES):
-                multiply(acc, b, g)
+                nc.tensor.matmul_mx(
+                    out=acc[:],
+                    lhsT=m_codes[b, g].bitcast(E4M3),
+                    lhsT_scale=m_scales[b, g],
+                    rhs=g_codes[g][:, slots].bitcast(E5M2),
+                    rhs_scale=g_scales[g][:, slots],
+                    start=(g == 0),
+                    stop=(g == PASSES - 1),
+                )
             return acc
 
-        def leave_psum(acc, slots, name):
-            dw = sb([P, slots.stop - slots.start], F32, name)
-            nc.scalar.activation(dw[:], acc[:, slots], ACT.Copy, scale=-1.0)
+        def leave_on_scalar(sums_ap, name):
+            dw = sb([P, sums_ap.shape[1]], F32, name)
+            nc.scalar.activation(dw[:], sums_ap, ACT.Copy, scale=-1.0)
             return dw
 
-        def scatter(b, slots, dw):
-            listed = offsets[:, slots.start // LIST_GROUP : slots.stop // LIST_GROUP]
-            nc.vector.tensor_copy(windows[b % WINDOWS][:].indirect(listed), dw[:])
+        def leave_on_vector(dw_ap, sums_ap):
+            nc.vector.tensor_scalar(dw_ap, sums_ap, -1.0, None, ALU.mult)
+
+        def listed(b, slots):
+            return windows[b][:].indirect(offsets[:, slots.start // LIST_GROUP : slots.stop // LIST_GROUP])
+
+        def scatter_on_scalar(b, slots, dw):
+            nc.scalar.activation(listed(b, slots), dw[:], ACT.Copy)
+
+        def scatter_on_vector(b, slots, dw):
+            nc.vector.tensor_copy(listed(b, slots), dw[:])
 
         def store(b):
-            nc.sync.dma_start(out[b * P : (b + 1) * P, :], windows[b % WINDOWS][:])
+            nc.sync.dma_start(out[b * P : (b + 1) * P, :], windows[b][:])
 
         for k in range(PACK):
             exponential(k)
@@ -321,32 +323,36 @@ def tile_attend_gkl_w_clip_kernel(tc, xT, wT, y, wt, xn, xm, offs, out):
         for k in range(PACK + 1, TILES):
             difference(k)
         square_sums(1)
-        g_bf01 = late_bf[:, 0 : PACK * HALF].rearrange("p (i t) -> p i t", t=PACK)
         cut = G0_BEFORE_BOUND
-        scale_and_weave(g_bf01[:, 0:cut, :], 0, slice(HALF, HALF + cut), factor_square[:, 0:PACK])
+        g0_early = sb([P, cut, PACK], BF16, "g0_early")
+        scale_and_weave(g0_early[:], 0, slice(0, cut), factor_square[:, 0:PACK])
         row_roots(1)
-        g_bf00 = sb([P, HALF, PACK], BF16, "g_bf0_0")
-        scale_and_weave(g_bf00[:], 0, first, factor0[:, 0:PACK])
-        scale_and_weave(g_bf01[:, cut:, :], 0, slice(HALF + cut, N), factor0[:, 0:PACK])
-        m_bf0 = weave_block(0)
-        m_bf1 = weave_block(1)
+        g0_late = sb([P, N - cut, PACK], BF16, "g0_late")
 
-        quantize_m(0, 0, m_bf0[:, 0:1, :, :])
+        def late_piece(slots):
+            return g0_late[:, slots.start - cut : slots.stop - cut, :]
+
+        third, fourth = slice(HALF, HALF + QUARTER), slice(HALF + QUARTER, N)
+        scale_and_weave(late_piece(slice(cut, HALF)), 0, slice(cut, HALF), factor0[:, 0:PACK])
+        scale_and_weave(late_piece(third), 0, third, factor0[:, 0:PACK])
+        m_bf0 = weave_block(nc.scalar.copy, 0)
+        m_bf1 = weave_block(nc.scalar.copy, 1)
+
         factor1 = sb([P, PACK], F32, "factor1")
         nc.vector.tensor_tensor(factor1[:], root[1][:], wt_sb[:, 1, :], ALU.mult)
-        quantize_g(0, first, g_bf00[:])
-        early = bank(2, "acc_early", N)
-        multiply(early, 0, 0)
+        quantize_g(0, slice(0, QUARTER), g0_early[:, 0:QUARTER, :])
         g_bf10 = sb([P, HALF, PACK], BF16, "g_bf1_0")
-        quarters = (slice(0, HALF // 2), slice(HALF // 2, HALF))
+        quarters = (slice(0, QUARTER), slice(QUARTER, HALF))
         for slots in quarters:
             scale_and_weave(g_bf10[:, slots, :], 1, slots, factor1[:])
-        quantize_m(0, 1, m_bf0[:, 1:2, :, :])
+        quantize_g(0, slice(QUARTER, cut), g0_early[:, QUARTER:, :])
+        quantize_g(0, slice(cut, HALF), late_piece(slice(cut, HALF)))
+        quantize_m(0, 0, m_bf0, "m_codes0")
         for slots in quarters:
             quantize_g(1, slots, g_bf10[:, slots, :])
-        multiply(early, 0, 1)
+        acc00 = product(0, first, 2)
 
-        share = HALF - G1_VECTOR
+        share = G1_SCALAR
         g_rows = sb([P, PACK, share], BF16, "g_rows")
         for t in range(PACK):
             nc.scalar.activation(
@@ -357,23 +363,41 @@ def tile_attend_gkl_w_clip_kernel(tc, xT, wT, y, wt, xn, xm, offs, out):
             g_bf11[:, 0:share, :].rearrange("p (c i) t -> p c t i", i=RUN),
             g_rows[:].rearrange("p t (c i) -> p c t i", i=RUN),
         )
-        early_sums = leave_psum(early, first, "early_sums")
-        scale_and_weave(g_bf11[:, share:, :], 1, slice(HALF + share, N), factor1[:])
-        quantize_g(0, second, g_bf01)
-        quantize_m(1, 0, m_bf1)
-        quantize_g(1, second, g_bf11[:])
-        scatter(0, first, early_sums)
+        dw = leave_on_scalar(acc00[:], "dw0_0")
+        scatter_on_scalar(0, first, dw)
+        m_bf20 = sb([P, 1, P, PACK], BF16, "m_bf2_0")
+        weave_m(nc.scalar.copy, m_bf20[:, 0, :, :], 2, 0)
 
-        m_bf2 = weave_block(2)
-        late_sums = leave_psum(product(0, 3, "late"), second, "late_sums")
-        quantize_m(2, 0, m_bf2)
-        scatter(0, second, late_sums)
+        scale_and_weave(late_piece(fourth), 0, fourth, factor0[:, 0:PACK])
+        scale_and_weave(g_bf11[:, share:, :], 1, slice(HALF + share, N), factor1[:])
+        quantize_g(0, second, late_piece(second))
+        quantize_g(1, second, g_bf11[:])
+        acc01 = product(0, second, 3)
+        quantize_m(1, 0, m_bf1, "m_codes1")
+        acc1 = product(1, whole, 4)
+        dw01 = sb([P, HALF], F32, "dw0_1")
+        leave_on_vector(dw01[:], acc01[:])
+        scatter_on_vector(0, second, dw01)
         store(0)
-        dw = leave_psum(product(1, 4, "dw1"), whole, "dw1")
-        quantize_m(3, 0, weave_block(3))
-        scatter(1, whole, dw)
+
+        dws = [leave_on_scalar(acc1[:, slots], f"dw1_{h}") for h, slots in enumerate(halves)]
+        for slots, dw in zip(halves, dws):
+            scatter_on_scalar(1, slots, dw)
         store(1)
-        for b in range(2, D_BLOCKS):
-            dw = leave_psum(product(b, 3 + b, f"dw{b}"), whole, f"dw{b}")
-            scatter(b, whole, dw)
-            store(b)
+
+        m_bf21 = sb([P, 1, P, PACK], BF16, "m_bf2_1")
+        weave_m(nc.vector.tensor_copy, m_bf21[:, 0, :, :], 2, 1)
+        quantize_m(2, 0, m_bf20[:], "m_codes2_0")
+        quantize_m(2, 1, m_bf21[:], "m_codes2_1")
+        acc2 = product(2, whole, 5)
+        quantize_m(3, 0, weave_block(nc.vector.tensor_copy, 3), "m_codes3")
+        acc3 = product(3, whole, 6)
+        dw2 = sb([P, N], F32, "dw2")
+        for slots in halves:
+            leave_on_vector(dw2[:, slots], acc2[:, slots])
+        scatter_on_vector(2, whole, dw2)
+        store(2)
+        dws = [leave_on_scalar(acc3[:, slots], f"dw3_{h}") for h, slots in enumerate(halves)]
+        for slots, dw in zip(halves, dws):
+            scatter_on_scalar(3, slots, dw)
+        store(3)

@@ -27,13 +27,10 @@ RUN = 4
 LIST_GROUP = 16
 TILES = PASSES * PACK
 HALF = N // 2
-QUARTER = N // 4
 WINDOWS_ON_VECTOR = 2
 
 PAIR_VECTOR = (40, 60)
 X_GPSIMD_CUTS = (0, 21, 42)
-G1_SCALAR = 128
-G0_BEFORE_BOUND = 192
 
 
 def tile_attend_gkl_w_clip_kernel(tc, xT, wT, y, wt, xn, xm, offs, out):
@@ -48,15 +45,17 @@ def tile_attend_gkl_w_clip_kernel(tc, xT, wT, y, wt, xn, xm, offs, out):
             "neg_max5": "e3",
             "neg_max6": "sumsq0",
             "neg_max7": "sums_sq0",
-            "g0_early": "y_pair1_2",
-            "g0_late": "length",
+            "g_bf0_0": "y_pair1_2",
+            "g_bf0_1": "length",
+            "g_codes0": "larger1",
             "m_bf0": "e6",
-            "m_bf1": "sumsq1",
-            "m_codes0": "sums_sq1",
-            "m_bf2_0": "g_rows",
-            "m_bf2_1": "g0_late",
-            "m_codes1": "g_bf1_1",
-            "m_bf3": "dw0_1",
+            "m_bf1": "e7",
+            "m_bf2": "sumsq1",
+            "m_bf3_0": "sums_sq1",
+            "m_bf3_1": "g_bf1_1",
+            "m_codes3_0": "m_bf2",
+            "dw3": "dw1",
+            "m_codes0": "root1",
         }
 
         def slot_of(name):
@@ -264,17 +263,20 @@ def tile_attend_gkl_w_clip_kernel(tc, xT, wT, y, wt, xn, xm, offs, out):
             for g in range(passes):
                 m_codes[b, g0 + g], m_scales[b, g0 + g] = codes[:, g, :], scales[:, g, :]
 
-        def product(b, slots, index):
+        in_order = list(range(PASSES))
+        last_first = in_order[::-1]
+
+        def product(b, slots, index, order=in_order):
             acc = bank(index, f"acc{index}", slots.stop - slots.start)
-            for g in range(PASSES):
+            for g in order:
                 nc.tensor.matmul_mx(
                     out=acc[:],
                     lhsT=m_codes[b, g].bitcast(E4M3),
                     lhsT_scale=m_scales[b, g],
                     rhs=g_codes[g][:, slots].bitcast(E5M2),
                     rhs_scale=g_scales[g][:, slots],
-                    start=(g == 0),
-                    stop=(g == PASSES - 1),
+                    start=(g == order[0]),
+                    stop=(g == order[-1]),
                 )
             return acc
 
@@ -323,81 +325,60 @@ def tile_attend_gkl_w_clip_kernel(tc, xT, wT, y, wt, xn, xm, offs, out):
         for k in range(PACK + 1, TILES):
             difference(k)
         square_sums(1)
-        cut = G0_BEFORE_BOUND
-        g0_early = sb([P, cut, PACK], BF16, "g0_early")
-        scale_and_weave(g0_early[:], 0, slice(0, cut), factor_square[:, 0:PACK])
+
+        def weave_g(g, h, factor):
+            woven = sb([P, HALF, PACK], BF16, f"g_bf{g}_{h}")
+            scale_and_weave(woven[:], g, halves[h], factor)
+            return woven[:]
+
+        g_bf00 = weave_g(0, 0, factor_square[:, 0:PACK])
         row_roots(1)
-        g0_late = sb([P, N - cut, PACK], BF16, "g0_late")
-
-        def late_piece(slots):
-            return g0_late[:, slots.start - cut : slots.stop - cut, :]
-
-        third, fourth = slice(HALF, HALF + QUARTER), slice(HALF + QUARTER, N)
-        scale_and_weave(late_piece(slice(cut, HALF)), 0, slice(cut, HALF), factor0[:, 0:PACK])
-        scale_and_weave(late_piece(third), 0, third, factor0[:, 0:PACK])
-        m_bf0 = weave_block(nc.scalar.copy, 0)
-        m_bf1 = weave_block(nc.scalar.copy, 1)
+        g_bf01 = weave_g(0, 1, factor0[:, 0:PACK])
+        m_bf = [weave_block(nc.scalar.copy, b) for b in range(D_BLOCKS - 1)]
+        m_bf30 = sb([P, 1, P, PACK], BF16, "m_bf3_0")
+        weave_m(nc.scalar.copy, m_bf30[:, 0, :, :], 3, 0)
 
         factor1 = sb([P, PACK], F32, "factor1")
         nc.vector.tensor_tensor(factor1[:], root[1][:], wt_sb[:, 1, :], ALU.mult)
-        quantize_g(0, slice(0, QUARTER), g0_early[:, 0:QUARTER, :])
-        g_bf10 = sb([P, HALF, PACK], BF16, "g_bf1_0")
-        quarters = (slice(0, QUARTER), slice(QUARTER, HALF))
-        for slots in quarters:
-            scale_and_weave(g_bf10[:, slots, :], 1, slots, factor1[:])
-        quantize_g(0, slice(QUARTER, cut), g0_early[:, QUARTER:, :])
-        quantize_g(0, slice(cut, HALF), late_piece(slice(cut, HALF)))
-        quantize_m(0, 0, m_bf0, "m_codes0")
-        for slots in quarters:
-            quantize_g(1, slots, g_bf10[:, slots, :])
-        acc00 = product(0, first, 2)
-
-        share = G1_SCALAR
-        g_rows = sb([P, PACK, share], BF16, "g_rows")
-        for t in range(PACK):
-            nc.scalar.activation(
-                g_rows[:, t, :], diffs[1][:, t, HALF : HALF + share], ACT.Copy, scale=factor1[:, t : t + 1]
-            )
-        g_bf11 = sb([P, HALF, PACK], BF16, "g_bf1_1")
-        nc.scalar.copy(
-            g_bf11[:, 0:share, :].rearrange("p (c i) t -> p c t i", i=RUN),
-            g_rows[:].rearrange("p t (c i) -> p c t i", i=RUN),
-        )
-        dw = leave_on_scalar(acc00[:], "dw0_0")
+        quantize_g(0, first, g_bf00)
+        g_bf10 = weave_g(1, 0, factor1[:])
+        quantize_m(0, 0, m_bf[0], "m_codes0")
+        quantize_g(1, first, g_bf10)
+        dw = leave_on_scalar(product(0, first, 2)[:], "dw0_0")
         scatter_on_scalar(0, first, dw)
-        m_bf20 = sb([P, 1, P, PACK], BF16, "m_bf2_0")
-        weave_m(nc.scalar.copy, m_bf20[:, 0, :, :], 2, 0)
 
-        scale_and_weave(late_piece(fourth), 0, fourth, factor0[:, 0:PACK])
-        scale_and_weave(g_bf11[:, share:, :], 1, slice(HALF + share, N), factor1[:])
-        quantize_g(0, second, late_piece(second))
-        quantize_g(1, second, g_bf11[:])
+        quantize_g(0, second, g_bf01)
+        quantize_m(1, 0, m_bf[1], "m_codes1")
+        acc10 = product(1, first, 4)
+        dw1 = sb([P, N], F32, "dw1")
+        nc.scalar.activation(dw1[:, first], acc10[:], ACT.Copy, scale=-1.0)
+        g_bf11 = weave_g(1, 1, factor1[:])
+        quantize_m(2, 0, m_bf[2], "m_codes2")
+        quantize_g(1, second, g_bf11)
         acc01 = product(0, second, 3)
-        quantize_m(1, 0, m_bf1, "m_codes1")
-        acc1 = product(1, whole, 4)
+        acc11 = product(1, second, 7)
+        acc2 = product(2, whole, 5, last_first)
+        m_bf31 = sb([P, 1, P, PACK], BF16, "m_bf3_1")
+        weave_m(nc.vector.tensor_copy, m_bf31[:, 0, :, :], 3, 1)
         dw01 = sb([P, HALF], F32, "dw0_1")
         leave_on_vector(dw01[:], acc01[:])
-        scatter_on_vector(0, second, dw01)
+        scatter_on_scalar(0, second, dw01)
         store(0)
 
-        dws = [leave_on_scalar(acc1[:, slots], f"dw1_{h}") for h, slots in enumerate(halves)]
-        for slots, dw in zip(halves, dws):
-            scatter_on_scalar(1, slots, dw)
+        quantize_m(3, 0, m_bf30[:], "m_codes3_0")
+        quantize_m(3, 1, m_bf31[:], "m_codes3_1")
+        leave_on_vector(dw1[:, second], acc11[:])
+        scatter_on_vector(1, whole, dw1)
         store(1)
 
-        m_bf21 = sb([P, 1, P, PACK], BF16, "m_bf2_1")
-        weave_m(nc.vector.tensor_copy, m_bf21[:, 0, :, :], 2, 1)
-        quantize_m(2, 0, m_bf20[:], "m_codes2_0")
-        quantize_m(2, 1, m_bf21[:], "m_codes2_1")
-        acc2 = product(2, whole, 5)
-        quantize_m(3, 0, weave_block(nc.vector.tensor_copy, 3), "m_codes3")
-        acc3 = product(3, whole, 6)
-        dw2 = sb([P, N], F32, "dw2")
-        for slots in halves:
-            leave_on_vector(dw2[:, slots], acc2[:, slots])
-        scatter_on_vector(2, whole, dw2)
-        store(2)
-        dws = [leave_on_scalar(acc3[:, slots], f"dw3_{h}") for h, slots in enumerate(halves)]
+        dws = [leave_on_scalar(acc2[:, slots], f"dw2_{h}") for h, slots in enumerate(halves)]
         for slots, dw in zip(halves, dws):
-            scatter_on_scalar(3, slots, dw)
+            scatter_on_scalar(2, slots, dw)
+        store(2)
+
+        acc3 = product(3, whole, 6, last_first)
+        dw3 = sb([P, N], F32, "dw3")
+        for slots in halves:
+            leave_on_vector(dw3[:, slots], acc3[:, slots])
+        scatter_on_vector(3, whole, dw3)
         store(3)

@@ -28,6 +28,7 @@ LIST_GROUP = 16
 TILES = PASSES * PACK
 HALF = N // 2
 WINDOWS_ON_VECTOR = 2
+G0_BESIDE_POW = 192
 
 PAIR_VECTOR = (40, 60)
 X_GPSIMD_CUTS = (0, 21, 42)
@@ -47,15 +48,14 @@ def tile_attend_gkl_w_clip_kernel(tc, xT, wT, y, wt, xn, xm, offs, out):
             "neg_max7": "sums_sq0",
             "g_bf0_0": "y_pair1_2",
             "g_bf0_1": "length",
-            "g_codes0": "larger1",
+            "g_codes0": "sumsq1",
             "m_bf0": "e6",
             "m_bf1": "e7",
-            "m_bf2": "sumsq1",
-            "m_bf3_0": "sums_sq1",
+            "m_bf2": "minus_half",
+            "m_bf3_0": "root1",
             "m_bf3_1": "g_bf1_1",
             "m_codes3_0": "m_bf2",
-            "dw3": "dw1",
-            "m_codes0": "root1",
+            "m_codes0": "inverse1",
         }
 
         def slot_of(name):
@@ -192,7 +192,7 @@ def tile_attend_gkl_w_clip_kernel(tc, xT, wT, y, wt, xn, xm, offs, out):
         e = [sb([P, N], F32, f"e{k}") for k in range(TILES)]
         sums = [sb([P, PACK], F32, f"sums{g}") for g in range(PASSES)]
         sumsq = [sb([P, PACK], F32, f"sumsq{g}") for g in range(PASSES)]
-        sums_sq, root = {}, {}
+        inverse, root = {}, {}
 
         def exponential(k):
             g, t = divmod(k, PACK)
@@ -208,15 +208,23 @@ def tile_attend_gkl_w_clip_kernel(tc, xT, wT, y, wt, xn, xm, offs, out):
                 e[k][:], diffs[g][:, t, :], ACT.Square, scale=length[:, k : k + 1], accum_out=sumsq[g][:, col]
             )
 
-        def square_sums(g):
-            sums_sq[g] = sb([P, PACK], F32, f"sums_sq{g}")
-            nc.vector.tensor_tensor(sums_sq[g][:], sums[g][:], sums[g][:], ALU.mult)
+        def invert_sums(g):
+            inverse[g] = sb([P, PACK], F32, f"inverse{g}")
+            nc.vector.reciprocal(inverse[g][:], sums[g][:])
 
         def row_roots(g):
-            larger = sb([P, PACK], F32, f"larger{g}")
-            nc.vector.tensor_tensor(larger[:], sumsq[g][:], sums_sq[g][:], ALU.max)
             root[g] = sb([P, PACK], F32, f"root{g}")
-            nc.gpsimd.tensor_tensor(root[g][:], larger[:], minus_half[:], ALU.pow)
+            nc.gpsimd.tensor_tensor(root[g][:], sumsq[g][:], minus_half[:], ALU.pow)
+
+        def clipped_roots(g):
+            sums_sq = sb([P, PACK], F32, f"sums_sq{g}")
+            nc.vector.tensor_tensor(sums_sq[:], sums[g][:], sums[g][:], ALU.mult)
+            return sums_sq
+
+        def lesser(g):
+            bound = sb([P, PACK], F32, f"bound{g}")
+            nc.vector.tensor_tensor(bound[:], root[g][:], inverse[g][:], ALU.min)
+            return bound
 
         def scale_and_weave(woven, g, slots, factor):
             runs = (slots.stop - slots.start) // RUN
@@ -308,13 +316,16 @@ def tile_attend_gkl_w_clip_kernel(tc, xT, wT, y, wt, xn, xm, offs, out):
         difference(2)
         difference(3)
         score(1, 2, 4)
-        square_sums(0)
+        sums_sq0 = clipped_roots(0)
         exponential(4)
-        row_roots(0)
+        larger0 = sb([P, PACK], F32, "larger0")
+        nc.vector.tensor_tensor(larger0[:], sumsq[0][:], sums_sq0[:], ALU.max)
+        bound0 = sb([P, PACK], F32, "bound0")
+        nc.gpsimd.tensor_tensor(bound0[:], larger0[:], minus_half[:], ALU.pow)
         exponential(5)
         exponential(6)
         exponential(7)
-        nc.vector.tensor_tensor(factor_square[:, 0:PACK], root[0][:], wt_sb[:, 0, :], ALU.mult)
+        nc.vector.tensor_tensor(factor_square[:, 0:PACK], bound0[:], wt_sb[:, 0, :], ALU.mult)
         turned = bank(0, "turned", P)
         nc.tensor.transpose(turned[:], factor_square[:], identity[:])
         difference(4)
@@ -324,25 +335,29 @@ def tile_attend_gkl_w_clip_kernel(tc, xT, wT, y, wt, xn, xm, offs, out):
         nc.tensor.transpose(factor0[:], turned_sb[:], identity[:])
         for k in range(PACK + 1, TILES):
             difference(k)
-        square_sums(1)
+        invert_sums(1)
 
         def weave_g(g, h, factor):
             woven = sb([P, HALF, PACK], BF16, f"g_bf{g}_{h}")
             scale_and_weave(woven[:], g, halves[h], factor)
             return woven[:]
 
-        g_bf00 = weave_g(0, 0, factor_square[:, 0:PACK])
+        g_bf00 = weave_g(0, 0, factor0[:, 0:PACK])
         row_roots(1)
-        g_bf01 = weave_g(0, 1, factor0[:, 0:PACK])
+        g_bf01 = sb([P, HALF, PACK], BF16, "g_bf0_1")[:]
+        cut = G0_BESIDE_POW
+        scale_and_weave(g_bf01[:, 0:cut, :], 0, slice(HALF, HALF + cut), factor0[:, 0:PACK])
         m_bf = [weave_block(nc.scalar.copy, b) for b in range(D_BLOCKS - 1)]
         m_bf30 = sb([P, 1, P, PACK], BF16, "m_bf3_0")
         weave_m(nc.scalar.copy, m_bf30[:, 0, :, :], 3, 0)
 
-        factor1 = sb([P, PACK], F32, "factor1")
-        nc.vector.tensor_tensor(factor1[:], root[1][:], wt_sb[:, 1, :], ALU.mult)
+        bound1 = lesser(1)
         quantize_g(0, first, g_bf00)
-        g_bf10 = weave_g(1, 0, factor1[:])
+        factor1 = sb([P, PACK], F32, "factor1")
+        nc.vector.tensor_tensor(factor1[:], bound1[:], wt_sb[:, 1, :], ALU.mult)
         quantize_m(0, 0, m_bf[0], "m_codes0")
+        g_bf10 = weave_g(1, 0, factor1[:])
+        scale_and_weave(g_bf01[:, cut:, :], 0, slice(HALF + cut, N), factor0[:, 0:PACK])
         quantize_g(1, first, g_bf10)
         dw = leave_on_scalar(product(0, first, 2)[:], "dw0_0")
         scatter_on_scalar(0, first, dw)
@@ -372,13 +387,14 @@ def tile_attend_gkl_w_clip_kernel(tc, xT, wT, y, wt, xn, xm, offs, out):
         store(1)
 
         dws = [leave_on_scalar(acc2[:, slots], f"dw2_{h}") for h, slots in enumerate(halves)]
-        for slots, dw in zip(halves, dws):
-            scatter_on_scalar(2, slots, dw)
+        acc30 = product(3, first, 6, last_first)
+        acc31 = product(3, second, 0, last_first)
+        dw3 = sb([P, N], F32, "dw3")
+        scatter_on_scalar(2, first, dws[0])
+        nc.scalar.activation(dw3[:, first], acc30[:], ACT.Copy, scale=-1.0)
+        scatter_on_scalar(2, second, dws[1])
         store(2)
 
-        acc3 = product(3, whole, 6, last_first)
-        dw3 = sb([P, N], F32, "dw3")
-        for slots in halves:
-            leave_on_vector(dw3[:, slots], acc3[:, slots])
+        leave_on_vector(dw3[:, second], acc31[:])
         scatter_on_vector(3, whole, dw3)
         store(3)

@@ -52,7 +52,7 @@ def tile_attend_gkl_w_clip_kernel(tc, xT, wT, y, wt, xn, xm, offs, out):
             "m_bf0": "e6",
             "m_bf1": "e7",
             "m_bf2": "minus_half",
-            "m_bf3_0": "root1",
+            "m_bf3_0": "e5",
             "m_bf3_1": "g_bf1_1",
             "m_codes3_0": "m_bf2",
             "m_codes0": "inverse1",
@@ -343,13 +343,20 @@ def tile_attend_gkl_w_clip_kernel(tc, xT, wT, y, wt, xn, xm, offs, out):
             return woven[:]
 
         g_bf00 = weave_g(0, 0, factor0[:, 0:PACK])
+        m_bf30 = sb([P, 1, P, PACK], BF16, "m_bf3_0")
+        nc.gpsimd.tensor_scalar(
+            m_bf30[:, 0, :, :],
+            xm_raw[0][:, :, (D_BLOCKS - 1) * P :].rearrange("p t m -> p m t"),
+            1.0,
+            0.0,
+            ALU.mult,
+            ALU.add,
+        )
         row_roots(1)
         g_bf01 = sb([P, HALF, PACK], BF16, "g_bf0_1")[:]
         cut = G0_BESIDE_POW
         scale_and_weave(g_bf01[:, 0:cut, :], 0, slice(HALF, HALF + cut), factor0[:, 0:PACK])
         m_bf = [weave_block(nc.scalar.copy, b) for b in range(D_BLOCKS - 1)]
-        m_bf30 = sb([P, 1, P, PACK], BF16, "m_bf3_0")
-        weave_m(nc.scalar.copy, m_bf30[:, 0, :, :], 3, 0)
 
         bound1 = lesser(1)
         quantize_g(0, first, g_bf00)

@@ -29,6 +29,8 @@ TILES = PASSES * PACK
 HALF = N // 2
 WINDOWS_ON_VECTOR = 2
 G0_BESIDE_POW = 192
+BLOCK_WORDS = 8
+QUARTER = N // 4
 
 PAIR_VECTOR = (40, 60)
 X_GPSIMD_CUTS = (0, 21, 42)
@@ -53,9 +55,11 @@ def tile_attend_gkl_w_clip_kernel(tc, xT, wT, y, wt, xn, xm, offs, out):
             "m_bf1": "e7",
             "m_bf2": "minus_half",
             "m_bf3_0": "e5",
-            "m_bf3_1": "g_bf1_1",
+            "m_bf3_1": "g_bf1_q3",
+            "m_codes2": "g_bf0_1",
             "m_codes3_0": "m_bf2",
             "m_codes0": "inverse1",
+            "m_codes1": "g_bf1_q0",
         }
 
         def slot_of(name):
@@ -222,9 +226,7 @@ def tile_attend_gkl_w_clip_kernel(tc, xT, wT, y, wt, xn, xm, offs, out):
             return sums_sq
 
         def lesser(g):
-            bound = sb([P, PACK], F32, f"bound{g}")
-            nc.vector.tensor_tensor(bound[:], root[g][:], inverse[g][:], ALU.min)
-            return bound
+            nc.vector.tensor_tensor(bounds[:, g, 0:PACK], root[g][:], inverse[g][:], ALU.min)
 
         def scale_and_weave(woven, g, slots, factor):
             runs = (slots.stop - slots.start) // RUN
@@ -275,7 +277,7 @@ def tile_attend_gkl_w_clip_kernel(tc, xT, wT, y, wt, xn, xm, offs, out):
         last_first = in_order[::-1]
 
         def product(b, slots, index, order=in_order):
-            acc = bank(index, f"acc{index}", slots.stop - slots.start)
+            acc = bank(index, f"acc{b}_{slots.start}", slots.stop - slots.start)
             for g in order:
                 nc.tensor.matmul_mx(
                     out=acc[:],
@@ -320,12 +322,13 @@ def tile_attend_gkl_w_clip_kernel(tc, xT, wT, y, wt, xn, xm, offs, out):
         exponential(4)
         larger0 = sb([P, PACK], F32, "larger0")
         nc.vector.tensor_tensor(larger0[:], sumsq[0][:], sums_sq0[:], ALU.max)
-        bound0 = sb([P, PACK], F32, "bound0")
-        nc.gpsimd.tensor_tensor(bound0[:], larger0[:], minus_half[:], ALU.pow)
+        bounds = sb([P, PASSES, BLOCK_WORDS], F32, "bounds")
+        bound0 = bounds[:, 0, 0:PACK]
+        nc.gpsimd.tensor_tensor(bound0, larger0[:], minus_half[:], ALU.pow)
         exponential(5)
         exponential(6)
         exponential(7)
-        nc.vector.tensor_tensor(factor_square[:, 0:PACK], bound0[:], wt_sb[:, 0, :], ALU.mult)
+        nc.vector.tensor_tensor(factor_square[:, 0:PACK], bound0, wt_sb[:, 0, :], ALU.mult)
         turned = bank(0, "turned", P)
         nc.tensor.transpose(turned[:], factor_square[:], identity[:])
         difference(4)
@@ -358,32 +361,45 @@ def tile_attend_gkl_w_clip_kernel(tc, xT, wT, y, wt, xn, xm, offs, out):
         scale_and_weave(g_bf01[:, 0:cut, :], 0, slice(HALF, HALF + cut), factor0[:, 0:PACK])
         m_bf = [weave_block(nc.scalar.copy, b) for b in range(D_BLOCKS - 1)]
 
-        bound1 = lesser(1)
+        lesser(1)
         quantize_g(0, first, g_bf00)
-        factor1 = sb([P, PACK], F32, "factor1")
-        nc.vector.tensor_tensor(factor1[:], bound1[:], wt_sb[:, 1, :], ALU.mult)
+        factors = sb([P, PASSES, PACK], F32, "factors")
+        nc.vector.tensor_tensor(factors[:], bounds[:, :, 0:PACK], wt_sb[:], ALU.mult)
+        factor1 = factors[:, 1, :]
         quantize_m(0, 0, m_bf[0], "m_codes0")
-        g_bf10 = weave_g(1, 0, factor1[:])
-        scale_and_weave(g_bf01[:, cut:, :], 0, slice(HALF + cut, N), factor0[:, 0:PACK])
-        quantize_g(1, first, g_bf10)
-        dw = leave_on_scalar(product(0, first, 2)[:], "dw0_0")
+        quarters = (slice(0, QUARTER), slice(QUARTER, HALF))
+        g_quarter = [sb([P, QUARTER, PACK], BF16, f"g_bf1_q{i}") for i in range(2)]
+        for woven, slots in zip(g_quarter, quarters):
+            scale_and_weave(woven[:], 1, slots, factor1)
+        dw = sb([P, HALF], F32, "dw0_0")
+        for woven, slots, index in zip(g_quarter, quarters, (2, 1)):
+            quantize_g(1, slots, woven[:])
+            nc.scalar.activation(dw[:, slots], product(0, slots, index)[:], ACT.Copy, scale=-1.0)
         scatter_on_scalar(0, first, dw)
+        scale_and_weave(g_bf01[:, cut:, :], 0, slice(HALF + cut, N), factors[:, 0, :])
 
-        quantize_g(0, second, g_bf01)
         quantize_m(1, 0, m_bf[1], "m_codes1")
         acc10 = product(1, first, 4)
         dw1 = sb([P, N], F32, "dw1")
         nc.scalar.activation(dw1[:, first], acc10[:], ACT.Copy, scale=-1.0)
-        g_bf11 = weave_g(1, 1, factor1[:])
+        third, fourth = slice(HALF, HALF + QUARTER), slice(HALF + QUARTER, N)
+        g_third = sb([P, QUARTER, PACK], BF16, "g_bf1_q2")
+        g_fourth = sb([P, QUARTER, PACK], BF16, "g_bf1_q3")
+        scale_and_weave(g_third[:], 1, third, factor1)
+        scale_and_weave(g_fourth[:], 1, fourth, factor1)
+        quantize_g(1, third, g_third[:])
+        quantize_g(0, second, g_bf01)
+        quantize_g(1, fourth, g_fourth[:])
+        acc02 = product(0, third, 3, last_first)
+        acc03 = product(0, fourth, 2)
+        acc11 = product(1, second, 7, last_first)
         quantize_m(2, 0, m_bf[2], "m_codes2")
-        quantize_g(1, second, g_bf11)
-        acc01 = product(0, second, 3)
-        acc11 = product(1, second, 7)
         acc2 = product(2, whole, 5, last_first)
         m_bf31 = sb([P, 1, P, PACK], BF16, "m_bf3_1")
         weave_m(nc.vector.tensor_copy, m_bf31[:, 0, :, :], 3, 1)
         dw01 = sb([P, HALF], F32, "dw0_1")
-        leave_on_vector(dw01[:], acc01[:])
+        leave_on_vector(dw01[:, 0:QUARTER], acc02[:])
+        leave_on_vector(dw01[:, QUARTER:], acc03[:])
         scatter_on_scalar(0, second, dw01)
         store(0)
 

@@ -55,7 +55,8 @@ def tile_attend_gkl_w_clip_kernel(tc, xT, wT, y, wt, xn, xm, offs, out):
             "m_bf1": "e7",
             "m_bf2": "minus_half",
             "m_bf3_0": "e5",
-            "m_bf3_1": "g_bf1_q3",
+            "m_bf3_1": "root1",
+            "m_codes3_1": "g_bf1_q3",
             "m_codes2": "g_bf0_1",
             "m_codes3_0": "m_bf2",
             "m_codes0": "inverse1",
@@ -360,6 +361,8 @@ def tile_attend_gkl_w_clip_kernel(tc, xT, wT, y, wt, xn, xm, offs, out):
         cut = G0_BESIDE_POW
         scale_and_weave(g_bf01[:, 0:cut, :], 0, slice(HALF, HALF + cut), factor0[:, 0:PACK])
         m_bf = [weave_block(nc.scalar.copy, b) for b in range(D_BLOCKS - 1)]
+        m_bf31 = sb([P, 1, P, PACK], BF16, "m_bf3_1")
+        weave_m(nc.scalar.copy, m_bf31[:, 0, :, :], 3, 1)
 
         lesser(1)
         quantize_g(0, first, g_bf00)
@@ -395,8 +398,6 @@ def tile_attend_gkl_w_clip_kernel(tc, xT, wT, y, wt, xn, xm, offs, out):
         acc11 = product(1, second, 7, last_first)
         quantize_m(2, 0, m_bf[2], "m_codes2")
         acc2 = product(2, whole, 5, last_first)
-        m_bf31 = sb([P, 1, P, PACK], BF16, "m_bf3_1")
-        weave_m(nc.vector.tensor_copy, m_bf31[:, 0, :, :], 3, 1)
         dw01 = sb([P, HALF], F32, "dw0_1")
         leave_on_vector(dw01[:, 0:QUARTER], acc02[:])
         leave_on_vector(dw01[:, QUARTER:], acc03[:])

@@ -28,12 +28,10 @@ LIST_GROUP = 16
 TILES = PASSES * PACK
 HALF = N // 2
 WINDOWS_ON_VECTOR = 2
-G0_BESIDE_POW = 192
 BLOCK_WORDS = 8
 QUARTER = N // 4
 
-PAIR_VECTOR = (40, 60)
-X_GPSIMD_CUTS = (0, 21, 42)
+PAIR1_VECTOR = 64
 
 
 def tile_attend_gkl_w_clip_kernel(tc, xT, wT, y, wt, xn, xm, offs, out):
@@ -50,17 +48,24 @@ def tile_attend_gkl_w_clip_kernel(tc, xT, wT, y, wt, xn, xm, offs, out):
             "neg_max7": "sums_sq0",
             "g_bf0_0": "y_pair1_2",
             "g_bf0_1": "length",
-            "g_codes0": "sumsq1",
+            "g_codes0_0": "sumsq1",
+            "g_codes0_1": "m_bf1_0",
             "m_bf0": "e6",
-            "m_bf1": "e7",
+            "m_bf1_0": "e5",
+            "m_bf1_1": "e7",
             "m_bf2": "minus_half",
-            "m_bf3_0": "e5",
-            "m_bf3_1": "root1",
-            "m_codes3_1": "g_bf1_q3",
-            "m_codes2": "g_bf0_1",
-            "m_codes3_0": "m_bf2",
+            "m_bf3": "root1",
             "m_codes0": "inverse1",
-            "m_codes1": "g_bf1_q0",
+            "m_codes1_0": "m_bf0",
+            "g_bf1_q2": "g_bf1_q0",
+            "g_bf1_q3": "g_bf1_q1",
+            "m_codes1_1": "g_bf0_1",
+            "m_codes2": "g_bf1_q3",
+            "m_codes3": "dw0_1",
+            "dw2_0": "dw0_0",
+            "dw2_1": "dw1_0",
+            "dw3_0": "m_bf3",
+            "dw3_1": "dw1_1",
         }
 
         def slot_of(name):
@@ -83,8 +88,9 @@ def tile_attend_gkl_w_clip_kernel(tc, xT, wT, y, wt, xn, xm, offs, out):
             nc.sync.dma_start(tile[:], source)
             return tile
 
-        def load_x(name, r0, r1):
-            return load(name, [P, PACK, r1 - r0], x_rows[:, :, r0:r1])[:].rearrange("p j (m t) -> p m j t", t=PACK)
+        def load_x(g, s):
+            source = x_rows[:, 2 * s : 2 * s + 2, g * K_PASS : (g + 1) * K_PASS]
+            return load(f"x_raw{g}_{s}", [P, 2, K_PASS], source)[:].rearrange("p j (m t) -> p m j t", t=PACK)
 
         def load_y(g, t0):
             return load(f"y_pair{g}_{t0}", [P, 2, N], y_rows[:, g, t0 : t0 + 2, :])
@@ -92,17 +98,22 @@ def tile_attend_gkl_w_clip_kernel(tc, xT, wT, y, wt, xn, xm, offs, out):
         def load_per_row(name, values):
             return load(name, [P, PASSES, PACK], values.rearrange("b (g p t) o -> p (b g) (t o)", g=PASSES, t=PACK))
 
-        rows_half, m_half = K_PASS // 2, P // 2
         w_plane = [load("w_plane0", [P, T], w_rows[:, 0, :])]
         nc.sync.dma_start(offsets[:], offs)
         xn_sb = load_per_row("xn_sb", xn)
         w_plane.extend(load(f"w_plane{j}", [P, T], w_rows[:, j, :]) for j in range(1, PACK))
-        x_raw0 = load_x("x_raw0", 0, K_PASS)
-        x_raw1 = [load_x(f"x_raw1_{h}", K_PASS + h * rows_half, K_PASS + (h + 1) * rows_half) for h in range(2)]
+        x_raw = [[load_x(g, s) for s in range(2)] for g in range(PASSES)]
         y_pair = [load_y(0, 0), load_y(0, 2)]
         y_pair.extend([load_y(1, 0), load_y(1, 2)])
         wt_sb = load_per_row("wt_sb", wt)
-        xm_raw = [load(f"xm_raw{g}", [P, PACK, D], xm_rows[:, g, :, :]) for g in range(PASSES)]
+        xm_raw = {}
+        for c in range(2):
+            for g in range(PASSES):
+                xm_raw[g, c] = load(f"xm_raw{g}_{c}", [P, PACK, 2 * P], xm_rows[:, g, :, c * 2 * P : (c + 1) * 2 * P])
+
+        def xm_block(b, g):
+            return xm_raw[g, b // 2][:, :, (b % 2) * P : (b % 2 + 1) * P]
+
         y_sb = [y_pair[k // 2][:, k % 2, :] for k in range(TILES)]
 
         minus_half = sb([P, PACK], F32, "minus_half")
@@ -123,7 +134,7 @@ def tile_attend_gkl_w_clip_kernel(tc, xT, wT, y, wt, xn, xm, offs, out):
             engine.memset(window[:], 0.0)
             windows.append(window)
 
-        first, second, whole = slice(0, HALF), slice(HALF, N), slice(0, N)
+        first, second = slice(0, HALF), slice(HALF, N)
         halves = (first, second)
 
         xn_over = sb([P, TILES], F32, "xn_over")
@@ -142,15 +153,25 @@ def tile_attend_gkl_w_clip_kernel(tc, xT, wT, y, wt, xn, xm, offs, out):
             out=w_codes[:].bitcast(E4M3), scales=w_scales[:], in_=w_bf[:].rearrange("p i j -> p (i j)")
         )
 
-        x_bf = [sb([P, PACK, P, PACK], BF16, f"x_bf{g}") for g in range(PASSES)]
+        x_bf = [[sb([P, 2, P, PACK], BF16, f"x_bf0_{u}")[:] for u in range(2)]]
+        x_bf1 = sb([P, PACK, P, PACK], BF16, "x_bf1")
+        x_bf.append([x_bf1[:, 0:2, :, :], x_bf1[:, 2:4, :, :]])
         scores = {}
 
-        def weave_pair(u):
-            tiles = slice(2 * u, 2 * u + 2)
-            woven = x_bf[0][:, tiles, :, :].rearrange("p t m j -> p m j t")
-            cut = PAIR_VECTOR[u]
-            nc.vector.tensor_copy(woven[:, 0:cut, :, :], x_raw0[:, 0:cut, :, tiles])
-            nc.scalar.activation(woven[:, cut:, :, :], x_raw0[:, cut:, :, tiles], ACT.Copy)
+        def on_vector(dst, src):
+            nc.vector.tensor_copy(dst, src)
+
+        def on_scalar(dst, src):
+            nc.scalar.activation(dst, src, ACT.Copy)
+
+        def on_gpsimd(dst, src):
+            nc.gpsimd.tensor_scalar(dst, src, 1.0, 0.0, ALU.mult, ALU.add)
+
+        def weave_x(copy, g, u, s, m0=0, m1=P):
+            copy(
+                x_bf[g][u][:, :, m0:m1, 2 * s : 2 * s + 2].rearrange("p t m j -> p m t j"),
+                x_raw[g][s][:, m0:m1, :, 2 * u : 2 * u + 2].rearrange("p m j t -> p m t j"),
+            )
 
         def score(g, t0, t1):
             codes = sb([P, t1 - t0, P], U32, f"x_codes{g}_{t0}")
@@ -158,7 +179,7 @@ def tile_attend_gkl_w_clip_kernel(tc, xT, wT, y, wt, xn, xm, offs, out):
             nc.vector.quantize_mx(
                 out=codes[:].rearrange("p t m -> p (t m)").bitcast(E4M3),
                 scales=scales[:].rearrange("p t m -> p (t m)"),
-                in_=x_bf[g][:, t0:t1, :, :].rearrange("p t m j -> p (t m j)"),
+                in_=x_bf[g][t0 // 2][:, t0 % 2 : t0 % 2 + t1 - t0, :, :].rearrange("p t m j -> p (t m j)"),
             )
             for t in range(t0, t1):
                 k = PACK * g + t
@@ -173,25 +194,17 @@ def tile_attend_gkl_w_clip_kernel(tc, xT, wT, y, wt, xn, xm, offs, out):
                     stop=True,
                 )
 
-        weave_pair(0)
+        weave_x(on_scalar, 0, 0, 0)
+        weave_x(on_scalar, 0, 1, 0, 0, PAIR1_VECTOR)
+        weave_x(on_gpsimd, 0, 1, 0, PAIR1_VECTOR, P)
+        weave_x(on_vector, 0, 0, 1)
+        weave_x(on_vector, 0, 1, 1, 0, PAIR1_VECTOR)
+        weave_x(on_scalar, 0, 1, 1, PAIR1_VECTOR, P)
         score(0, 0, 1)
         score(0, 1, 2)
-        weave_pair(1)
         score(0, 2, 4)
-        nc.scalar.activation(x_bf[1][:, :, 0:m_half, :].rearrange("p t m j -> p m j t"), x_raw1[0], ACT.Copy)
-        m_rest = X_GPSIMD_CUTS[-1]
-        nc.scalar.activation(
-            x_bf[1][:, :, m_half + m_rest :, :].rearrange("p t m j -> p m j t"), x_raw1[1][:, m_rest:, :, :], ACT.Copy
-        )
-        for m0, m1 in zip(X_GPSIMD_CUTS, X_GPSIMD_CUTS[1:]):
-            nc.gpsimd.tensor_scalar(
-                x_bf[1][:, :, m_half + m0 : m_half + m1, :].rearrange("p t m j -> p m t j"),
-                x_raw1[1][:, m0:m1, :, :].rearrange("p m j t -> p m t j"),
-                1.0,
-                0.0,
-                ALU.mult,
-                ALU.add,
-            )
+        on_scalar(x_bf1[:, :, :, 0:2].rearrange("p t m j -> p m t j"), x_raw[1][0].rearrange("p m j t -> p m t j"))
+        on_gpsimd(x_bf1[:, :, :, 2:4].rearrange("p t m j -> p m t j"), x_raw[1][1].rearrange("p m j t -> p m t j"))
 
         diffs = [sb([P, PACK, N], F32, f"diffs{g}") for g in range(PASSES)]
         e = [sb([P, N], F32, f"e{k}") for k in range(TILES)]
@@ -238,13 +251,20 @@ def tile_attend_gkl_w_clip_kernel(tc, xT, wT, y, wt, xn, xm, offs, out):
                 ALU.mult,
             )
 
-        g_codes = [sb([P, N], U32, f"g_codes{g}") for g in range(PASSES)]
-        g_scales = [sb([P, N], U8, f"g_scales{g}") for g in range(PASSES)]
+        g_codes, g_scales = {}, {}
+
+        def within_half(slots):
+            h = slots.start // HALF
+            return h, slice(slots.start - h * HALF, slots.stop - h * HALF)
 
         def quantize_g(g, slots, woven):
+            h, cols = within_half(slots)
+            if (g, h) not in g_codes:
+                g_codes[g, h] = sb([P, HALF], U32, f"g_codes{g}_{h}")
+                g_scales[g, h] = sb([P, HALF], U8, f"g_scales{g}_{h}")
             nc.vector.quantize_mx(
-                out=g_codes[g][:, slots].bitcast(E5M2),
-                scales=g_scales[g][:, slots],
+                out=g_codes[g, h][:, cols].bitcast(E5M2),
+                scales=g_scales[g, h][:, cols],
                 in_=woven.rearrange("p i t -> p (i t)"),
             )
 
@@ -253,7 +273,7 @@ def tile_attend_gkl_w_clip_kernel(tc, xT, wT, y, wt, xn, xm, offs, out):
         def weave_m(copy, woven, b, g):
             copy(
                 woven.rearrange("p (c i) t -> p c t i", i=RUN),
-                xm_raw[g][:, :, b * P : (b + 1) * P].rearrange("p t (c i) -> p c t i", i=RUN),
+                xm_block(b, g).rearrange("p t (c i) -> p c t i", i=RUN),
             )
 
         def weave_block(copy, b):
@@ -279,13 +299,14 @@ def tile_attend_gkl_w_clip_kernel(tc, xT, wT, y, wt, xn, xm, offs, out):
 
         def product(b, slots, index, order=in_order):
             acc = bank(index, f"acc{b}_{slots.start}", slots.stop - slots.start)
+            h, cols = within_half(slots)
             for g in order:
                 nc.tensor.matmul_mx(
                     out=acc[:],
                     lhsT=m_codes[b, g].bitcast(E4M3),
                     lhsT_scale=m_scales[b, g],
-                    rhs=g_codes[g][:, slots].bitcast(E5M2),
-                    rhs_scale=g_scales[g][:, slots],
+                    rhs=g_codes[g, h][:, cols].bitcast(E5M2),
+                    rhs_scale=g_scales[g, h][:, cols],
                     start=(g == order[0]),
                     stop=(g == order[-1]),
                 )
@@ -347,78 +368,64 @@ def tile_attend_gkl_w_clip_kernel(tc, xT, wT, y, wt, xn, xm, offs, out):
             return woven[:]
 
         g_bf00 = weave_g(0, 0, factor0[:, 0:PACK])
-        m_bf30 = sb([P, 1, P, PACK], BF16, "m_bf3_0")
-        nc.gpsimd.tensor_scalar(
-            m_bf30[:, 0, :, :],
-            xm_raw[0][:, :, (D_BLOCKS - 1) * P :].rearrange("p t m -> p m t"),
-            1.0,
-            0.0,
-            ALU.mult,
-            ALU.add,
-        )
+        m_bf1 = [sb([P, 1, P, PACK], BF16, f"m_bf1_{g}") for g in range(PASSES)]
+        on_gpsimd(m_bf1[0][:, 0, :, :], xm_block(1, 0).rearrange("p t m -> p m t"))
         row_roots(1)
-        g_bf01 = sb([P, HALF, PACK], BF16, "g_bf0_1")[:]
-        cut = G0_BESIDE_POW
-        scale_and_weave(g_bf01[:, 0:cut, :], 0, slice(HALF, HALF + cut), factor0[:, 0:PACK])
-        m_bf = [weave_block(nc.scalar.copy, b) for b in range(D_BLOCKS - 1)]
-        m_bf31 = sb([P, 1, P, PACK], BF16, "m_bf3_1")
-        weave_m(nc.scalar.copy, m_bf31[:, 0, :, :], 3, 1)
+        g_bf01 = weave_g(0, 1, factor0[:, 0:PACK])
+        m_bf0 = weave_block(nc.scalar.copy, 0)
+        weave_m(nc.scalar.copy, m_bf1[1][:, 0, :, :], 1, 1)
+        m_bf2 = weave_block(nc.scalar.copy, 2)
+        m_bf3 = weave_block(nc.scalar.copy, 3)
 
         lesser(1)
         quantize_g(0, first, g_bf00)
-        factors = sb([P, PASSES, PACK], F32, "factors")
-        nc.vector.tensor_tensor(factors[:], bounds[:, :, 0:PACK], wt_sb[:], ALU.mult)
-        factor1 = factors[:, 1, :]
-        quantize_m(0, 0, m_bf[0], "m_codes0")
+        factor1 = sb([P, PACK], F32, "factor1")[:]
+        nc.vector.tensor_tensor(factor1, bounds[:, 1, 0:PACK], wt_sb[:, 1, :], ALU.mult)
+        quantize_m(0, 0, m_bf0, "m_codes0")
         quarters = (slice(0, QUARTER), slice(QUARTER, HALF))
         g_quarter = [sb([P, QUARTER, PACK], BF16, f"g_bf1_q{i}") for i in range(2)]
         for woven, slots in zip(g_quarter, quarters):
             scale_and_weave(woven[:], 1, slots, factor1)
-        dw = sb([P, HALF], F32, "dw0_0")
-        for woven, slots, index in zip(g_quarter, quarters, (2, 1)):
+        dw = {(0, 0): sb([P, HALF], F32, "dw0_0")}
+        for woven, slots, index in zip(g_quarter, quarters, (2, 3)):
             quantize_g(1, slots, woven[:])
-            nc.scalar.activation(dw[:, slots], product(0, slots, index)[:], ACT.Copy, scale=-1.0)
-        scatter_on_scalar(0, first, dw)
-        scale_and_weave(g_bf01[:, cut:, :], 0, slice(HALF + cut, N), factors[:, 0, :])
+            nc.scalar.activation(dw[0, 0][:, slots], product(0, slots, index)[:], ACT.Copy, scale=-1.0)
+        scatter_on_scalar(0, first, dw[0, 0])
 
-        quantize_m(1, 0, m_bf[1], "m_codes1")
-        acc10 = product(1, first, 4)
-        dw1 = sb([P, N], F32, "dw1")
-        nc.scalar.activation(dw1[:, first], acc10[:], ACT.Copy, scale=-1.0)
+        quantize_m(1, 0, m_bf1[0][:], "m_codes1_0")
+        quantize_g(0, second, g_bf01)
         third, fourth = slice(HALF, HALF + QUARTER), slice(HALF + QUARTER, N)
         g_third = sb([P, QUARTER, PACK], BF16, "g_bf1_q2")
         g_fourth = sb([P, QUARTER, PACK], BF16, "g_bf1_q3")
         scale_and_weave(g_third[:], 1, third, factor1)
         scale_and_weave(g_fourth[:], 1, fourth, factor1)
         quantize_g(1, third, g_third[:])
-        quantize_g(0, second, g_bf01)
         quantize_g(1, fourth, g_fourth[:])
-        acc02 = product(0, third, 3, last_first)
-        acc03 = product(0, fourth, 2)
-        acc11 = product(1, second, 7, last_first)
-        quantize_m(2, 0, m_bf[2], "m_codes2")
-        acc2 = product(2, whole, 5, last_first)
-        dw01 = sb([P, HALF], F32, "dw0_1")
-        leave_on_vector(dw01[:, 0:QUARTER], acc02[:])
-        leave_on_vector(dw01[:, QUARTER:], acc03[:])
-        scatter_on_scalar(0, second, dw01)
+        acc02 = product(0, third, 0)
+        acc03 = product(0, fourth, 4)
+        quantize_m(1, 1, m_bf1[1][:], "m_codes1_1")
+        acc = {(1, 0): product(1, first, 5), (1, 1): product(1, second, 6)}
+        quantize_m(2, 0, m_bf2, "m_codes2")
+        acc[2, 0], acc[2, 1] = product(2, first, 7), product(2, second, 3)
+        dw[0, 1] = sb([P, HALF], F32, "dw0_1")
+        leave_on_vector(dw[0, 1][:, 0:QUARTER], acc02[:])
+        leave_on_vector(dw[0, 1][:, QUARTER:], acc03[:])
+
+        def first_half_on_vector(b):
+            dw[b, 0] = sb([P, HALF], F32, f"dw{b}_0")
+            leave_on_vector(dw[b, 0][:], acc[b, 0][:])
+
+        first_half_on_vector(1)
+        scatter_on_vector(0, second, dw[0, 1])
         store(0)
+        first_half_on_vector(2)
+        quantize_m(3, 0, m_bf3, "m_codes3")
+        acc[3, 0], acc[3, 1] = product(3, first, 2), product(3, second, 1)
 
-        quantize_m(3, 0, m_bf30[:], "m_codes3_0")
-        quantize_m(3, 1, m_bf31[:], "m_codes3_1")
-        leave_on_vector(dw1[:, second], acc11[:])
-        scatter_on_vector(1, whole, dw1)
-        store(1)
-
-        dws = [leave_on_scalar(acc2[:, slots], f"dw2_{h}") for h, slots in enumerate(halves)]
-        acc30 = product(3, first, 6, last_first)
-        acc31 = product(3, second, 0, last_first)
-        dw3 = sb([P, N], F32, "dw3")
-        scatter_on_scalar(2, first, dws[0])
-        nc.scalar.activation(dw3[:, first], acc30[:], ACT.Copy, scale=-1.0)
-        scatter_on_scalar(2, second, dws[1])
-        store(2)
-
-        leave_on_vector(dw3[:, second], acc31[:])
-        scatter_on_vector(3, whole, dw3)
-        store(3)
+        for b in range(1, D_BLOCKS):
+            dw[b, 1] = leave_on_scalar(acc[b, 1][:], f"dw{b}_1")
+            scatter_on_scalar(b, first, dw[b, 0])
+            scatter_on_vector(b, second, dw[b, 1])
+            store(b)
+            if b == 1:
+                first_half_on_vector(3)

@@ -30,8 +30,10 @@ HALF = N // 2
 WINDOWS_ON_VECTOR = 2
 BLOCK_WORDS = 8
 QUARTER = N // 4
+GATHER_SCALAR = 128
 
 PAIR1_VECTOR = 64
+X1_GPSIMD = 104
 
 
 def tile_attend_gkl_w_clip_kernel(tc, xT, wT, y, wt, xn, xm, offs, out):
@@ -96,7 +98,9 @@ def tile_attend_gkl_w_clip_kernel(tc, xT, wT, y, wt, xn, xm, offs, out):
             return load(f"y_pair{g}_{t0}", [P, 2, N], y_rows[:, g, t0 : t0 + 2, :])
 
         def load_per_row(name, values):
-            return load(name, [P, PASSES, PACK], values.rearrange("b (g p t) o -> p (b g) (t o)", g=PASSES, t=PACK))
+            tile = sb([P, PASSES, BLOCK_WORDS], F32, name)
+            nc.sync.dma_start(tile[:, :, 0:PACK], values.rearrange("b (g p t) o -> p (b g) (t o)", g=PASSES, t=PACK))
+            return tile[:, :, 0:PACK]
 
         w_plane = [load("w_plane0", [P, T], w_rows[:, 0, :])]
         nc.sync.dma_start(offsets[:], offs)
@@ -140,13 +144,20 @@ def tile_attend_gkl_w_clip_kernel(tc, xT, wT, y, wt, xn, xm, offs, out):
         xn_over = sb([P, TILES], F32, "xn_over")
         length = sb([P, TILES], F32, "length")
         nc.gpsimd.tensor_scalar(
-            xn_over[:], xn_sb[:].rearrange("p g t -> p (g t)"), 1.0 / (CLIP * CLIP), 0.0, ALU.mult, ALU.add
+            xn_over[:].rearrange("p (g t) -> p g t", t=PACK), xn_sb, 1.0 / (CLIP * CLIP), 0.0, ALU.mult, ALU.add
         )
         nc.gpsimd.tensor_tensor(length[:], xn_over[:], half[:], ALU.pow)
 
         w_bf = sb([P, N, PACK], BF16, "w_bf")
+        cut = N - GATHER_SCALAR
+        staged = sb([P, PACK, GATHER_SCALAR], BF16, "staged")
         for j in range(PACK):
-            nc.vector.tensor_copy(w_bf[:, :, j], w_plane[j][:].indirect(offsets[:]))
+            nc.vector.tensor_copy(w_bf[:, 0:cut, j], w_plane[j][:].indirect(offsets[:, 0 : cut // LIST_GROUP]))
+            nc.scalar.activation(staged[:, j, :], w_plane[j][:].indirect(offsets[:, cut // LIST_GROUP :]), ACT.Copy)
+        nc.scalar.copy(
+            w_bf[:, cut:, :].rearrange("p (c i) t -> p c t i", i=RUN),
+            staged[:].rearrange("p t (c i) -> p c t i", i=RUN),
+        )
         w_codes = sb([P, N], U32, "w_codes")
         w_scales = sb([P, N], U8, "w_scales")
         nc.vector.quantize_mx(
@@ -196,7 +207,7 @@ def tile_attend_gkl_w_clip_kernel(tc, xT, wT, y, wt, xn, xm, offs, out):
 
         weave_x(on_scalar, 0, 0, 0)
         weave_x(on_scalar, 0, 1, 0, 0, PAIR1_VECTOR)
-        weave_x(on_gpsimd, 0, 1, 0, PAIR1_VECTOR, P)
+        weave_x(on_scalar, 0, 1, 0, PAIR1_VECTOR, P)
         weave_x(on_vector, 0, 0, 1)
         weave_x(on_vector, 0, 1, 1, 0, PAIR1_VECTOR)
         weave_x(on_scalar, 0, 1, 1, PAIR1_VECTOR, P)
@@ -204,7 +215,14 @@ def tile_attend_gkl_w_clip_kernel(tc, xT, wT, y, wt, xn, xm, offs, out):
         score(0, 1, 2)
         score(0, 2, 4)
         on_scalar(x_bf1[:, :, :, 0:2].rearrange("p t m j -> p m t j"), x_raw[1][0].rearrange("p m j t -> p m t j"))
-        on_gpsimd(x_bf1[:, :, :, 2:4].rearrange("p t m j -> p m t j"), x_raw[1][1].rearrange("p m j t -> p m t j"))
+
+        def finish_x1(copy, m0, m1):
+            copy(
+                x_bf1[:, :, m0:m1, 2:4].rearrange("p t m j -> p m t j"),
+                x_raw[1][1][:, m0:m1, :, :].rearrange("p m j t -> p m t j"),
+            )
+
+        finish_x1(on_gpsimd, 0, X1_GPSIMD)
 
         diffs = [sb([P, PACK, N], F32, f"diffs{g}") for g in range(PASSES)]
         e = [sb([P, N], F32, f"e{k}") for k in range(TILES)]
@@ -334,6 +352,7 @@ def tile_attend_gkl_w_clip_kernel(tc, xT, wT, y, wt, xn, xm, offs, out):
 
         for k in range(PACK):
             exponential(k)
+        finish_x1(on_vector, X1_GPSIMD, P)
         difference(0)
         difference(1)
         score(1, 0, 2)

@@ -45,9 +45,7 @@ def tile_attend_gkl_w_clip_kernel(tc, xT, wT, y, wt, xn, xm, offs, out):
         follows = {
             "x_codes1_0": "neg_max1",
             "x_codes1_2": "neg_max2",
-            "neg_max5": "e3",
-            "neg_max6": "sumsq0",
-            "neg_max7": "sums_sq0",
+            "bounds": "neg_max4",
             "g_bf0_0": "y_pair1_2",
             "g_bf0_1": "length",
             "g_codes0_0": "sumsq1",
@@ -154,10 +152,12 @@ def tile_attend_gkl_w_clip_kernel(tc, xT, wT, y, wt, xn, xm, offs, out):
         for j in range(PACK):
             nc.vector.tensor_copy(w_bf[:, 0:cut, j], w_plane[j][:].indirect(offsets[:, 0 : cut // LIST_GROUP]))
             nc.scalar.activation(staged[:, j, :], w_plane[j][:].indirect(offsets[:, cut // LIST_GROUP :]), ACT.Copy)
-        nc.scalar.copy(
-            w_bf[:, cut:, :].rearrange("p (c i) t -> p c t i", i=RUN),
-            staged[:].rearrange("p t (c i) -> p c t i", i=RUN),
-        )
+            if j == PACK - 2:
+                nc.scalar.copy(
+                    w_bf[:, cut:, 0 : j + 1].rearrange("p (c i) t -> p c t i", i=RUN),
+                    staged[:, 0 : j + 1, :].rearrange("p t (c i) -> p c t i", i=RUN),
+                )
+        nc.scalar.copy(w_bf[:, cut:, PACK - 1], staged[:, PACK - 1, :])
         w_codes = sb([P, N], U32, "w_codes")
         w_scales = sb([P, N], U8, "w_scales")
         nc.vector.quantize_mx(
@@ -251,11 +251,6 @@ def tile_attend_gkl_w_clip_kernel(tc, xT, wT, y, wt, xn, xm, offs, out):
         def row_roots(g):
             root[g] = sb([P, PACK], F32, f"root{g}")
             nc.gpsimd.tensor_tensor(root[g][:], sumsq[g][:], minus_half[:], ALU.pow)
-
-        def clipped_roots(g):
-            sums_sq = sb([P, PACK], F32, f"sums_sq{g}")
-            nc.vector.tensor_tensor(sums_sq[:], sums[g][:], sums[g][:], ALU.mult)
-            return sums_sq
 
         def lesser(g):
             nc.vector.tensor_tensor(bounds[:, g, 0:PACK], root[g][:], inverse[g][:], ALU.min)
@@ -359,15 +354,14 @@ def tile_attend_gkl_w_clip_kernel(tc, xT, wT, y, wt, xn, xm, offs, out):
         difference(2)
         difference(3)
         score(1, 2, 4)
-        sums_sq0 = clipped_roots(0)
+        invert_sums(0)
+        row_roots(0)
         exponential(4)
-        larger0 = sb([P, PACK], F32, "larger0")
-        nc.vector.tensor_tensor(larger0[:], sumsq[0][:], sums_sq0[:], ALU.max)
-        bounds = sb([P, PASSES, BLOCK_WORDS], F32, "bounds")
-        bound0 = bounds[:, 0, 0:PACK]
-        nc.gpsimd.tensor_tensor(bound0, larger0[:], minus_half[:], ALU.pow)
         exponential(5)
         exponential(6)
+        bounds = sb([P, PASSES, BLOCK_WORDS], F32, "bounds")
+        lesser(0)
+        bound0 = bounds[:, 0, 0:PACK]
         exponential(7)
         nc.vector.tensor_tensor(factor_square[:, 0:PACK], bound0, wt_sb[:, 0, :], ALU.mult)
         turned = bank(0, "turned", P)

@@ -223,6 +223,7 @@ def tile_attend_gkl_w_clip_kernel(tc, xT, wT, y, wt, xn, xm, offs, out):
             )
 
         finish_x1(on_gpsimd, 0, X1_GPSIMD)
+        finish_x1(on_scalar, X1_GPSIMD, P)
 
         diffs = [sb([P, PACK, N], F32, f"diffs{g}") for g in range(PASSES)]
         e = [sb([P, N], F32, f"e{k}") for k in range(TILES)]
@@ -347,7 +348,6 @@ def tile_attend_gkl_w_clip_kernel(tc, xT, wT, y, wt, xn, xm, offs, out):
 
         for k in range(PACK):
             exponential(k)
-        finish_x1(on_vector, X1_GPSIMD, P)
         difference(0)
         difference(1)
         score(1, 0, 2)

@@ -33,7 +33,7 @@ QUARTER = N // 4
 GATHER_SCALAR = 128
 
 PAIR1_VECTOR = 64
-X1_GPSIMD = 104
+X1_GPSIMD = 96
 
 
 def tile_attend_gkl_w_clip_kernel(tc, xT, wT, y, wt, xn, xm, offs, out):
@@ -46,7 +46,7 @@ def tile_attend_gkl_w_clip_kernel(tc, xT, wT, y, wt, xn, xm, offs, out):
             "x_codes1_0": "neg_max1",
             "x_codes1_2": "neg_max2",
             "bounds": "neg_max4",
-            "g_bf0_0": "y_pair1_2",
+            "g_bf0_0": "y_rows1_2",
             "g_bf0_1": "length",
             "g_codes0_0": "sumsq1",
             "g_codes0_1": "m_bf1_0",
@@ -92,8 +92,9 @@ def tile_attend_gkl_w_clip_kernel(tc, xT, wT, y, wt, xn, xm, offs, out):
             source = x_rows[:, 2 * s : 2 * s + 2, g * K_PASS : (g + 1) * K_PASS]
             return load(f"x_raw{g}_{s}", [P, 2, K_PASS], source)[:].rearrange("p j (m t) -> p m j t", t=PACK)
 
-        def load_y(g, t0):
-            return load(f"y_pair{g}_{t0}", [P, 2, N], y_rows[:, g, t0 : t0 + 2, :])
+        def load_y(g, t0, t1):
+            tile = load(f"y_rows{g}_{t0}", [P, t1 - t0, N], y_rows[:, g, t0:t1, :])
+            return [tile[:, t, :] for t in range(t1 - t0)]
 
         def load_per_row(name, values):
             tile = sb([P, PASSES, BLOCK_WORDS], F32, name)
@@ -105,8 +106,7 @@ def tile_attend_gkl_w_clip_kernel(tc, xT, wT, y, wt, xn, xm, offs, out):
         xn_sb = load_per_row("xn_sb", xn)
         w_plane.extend(load(f"w_plane{j}", [P, T], w_rows[:, j, :]) for j in range(1, PACK))
         x_raw = [[load_x(g, s) for s in range(2)] for g in range(PASSES)]
-        y_pair = [load_y(0, 0), load_y(0, 2)]
-        y_pair.extend([load_y(1, 0), load_y(1, 2)])
+        y_sb = load_y(0, 0, 1) + load_y(0, 1, 2) + load_y(0, 2, 4) + load_y(1, 0, 2) + load_y(1, 2, 4)
         wt_sb = load_per_row("wt_sb", wt)
         xm_raw = {}
         for c in range(2):
@@ -116,7 +116,6 @@ def tile_attend_gkl_w_clip_kernel(tc, xT, wT, y, wt, xn, xm, offs, out):
         def xm_block(b, g):
             return xm_raw[g, b // 2][:, :, (b % 2) * P : (b % 2 + 1) * P]
 
-        y_sb = [y_pair[k // 2][:, k % 2, :] for k in range(TILES)]
 
         minus_half = sb([P, PACK], F32, "minus_half")
         ones = sb([P, PACK], F32, "ones")
@@ -351,9 +350,9 @@ def tile_attend_gkl_w_clip_kernel(tc, xT, wT, y, wt, xn, xm, offs, out):
         difference(0)
         difference(1)
         score(1, 0, 2)
+        score(1, 2, 4)
         difference(2)
         difference(3)
-        score(1, 2, 4)
         invert_sums(0)
         row_roots(0)
         exponential(4)

from contextlib import ExitStack

import concourse.mybir as mybir
from concourse.masks import make_identity

N, T, D, R = 512, 2048, 512, 1024
CLIP = 1.4
FLOPS = 2 * 2 * N * D * R

F32 = mybir.dt.float32
BF16 = mybir.dt.bfloat16
U32 = mybir.dt.uint32
U16 = mybir.dt.uint16
U8 = mybir.dt.uint8
E4M3 = mybir.dt.float8_e4m3fn_x4
E5M2 = mybir.dt.float8_e5m2_x4
ALU = mybir.AluOpType
ACT = mybir.ActivationFunctionType
AXIS = mybir.AxisListType

P = 128
PACK = 4
K_PASS = P * PACK
PASSES = R // K_PASS
D_BLOCKS = D // P
RUN = 4
LIST_GROUP = 16
TILES = PASSES * PACK
HALF = N // 2
WINDOWS_ON_VECTOR = 2
BLOCK_WORDS = 8
QUARTER = N // 4
GATHER_SCALAR = 128

PAIR1_VECTOR = 64
X1_GPSIMD = 96


def tile_attend_gkl_w_clip_kernel(tc, xT, wT, y, wt, xn, xm, offs, out):
    nc = tc.nc
    with ExitStack() as ctx:
        keep = ctx.enter_context(tc.tile_pool(name="keep", bufs=1))
        psum = ctx.enter_context(tc.psum_pool(name="psum", bufs=1))

        follows = {
            "x_codes1_0": "neg_max1",
            "x_codes1_2": "neg_max2",
            "bounds": "neg_max4",
            "g_bf0_0": "y_rows1_2",
            "g_bf0_1": "length",
            "g_codes0_0": "sumsq1",
            "g_codes0_1": "m_bf1_0",
            "m_bf0": "e6",
            "m_bf1_0": "e5",
            "m_bf1_1": "e7",
            "m_bf2": "minus_half",
            "m_bf3": "root1",
            "m_codes0": "inverse1",
            "m_codes1_0": "m_bf0",
            "g_bf1_q2": "g_bf1_q0",
            "g_bf1_q3": "g_bf1_q1",
            "m_codes1_1": "g_bf0_1",
            "m_codes2": "g_bf1_q3",
            "m_codes3": "dw0_1",
            "dw2_0": "dw0_0",
            "dw2_1": "dw1_0",
            "dw3_0": "m_bf3",
            "dw3_1": "dw1_1",
        }

        def slot_of(name):
            return slot_of(follows[name]) if name in follows else name

        def sb(shape, dtype, name):
            return keep.tile(shape, dtype, name=name, tag=slot_of(name), align_bytes=64)

        def bank(index, name, width):
            return psum.tile([P, width], F32, name=name, tag=f"bank{index}")

        offsets = keep.tile([P, N // LIST_GROUP], U16, name="offsets")
        w_rows = wT.rearrange("(p j) c -> p j c", j=PACK)
        x_rows = xT.rearrange("b (p j) r -> p (b j) r", j=PACK)
        y_rows = y.rearrange("b (g p t) i -> p (b g) t i", g=PASSES, t=PACK)
        xm_rows = xm.rearrange("b (g p t) d -> p (b g) t d", g=PASSES, t=PACK)

        def load(name, shape, source):
            tile = sb(shape, F32, name)
            nc.sync.dma_start(tile[:], source)
            return tile

        def load_x(g, s):
            source = x_rows[:, 2 * s : 2 * s + 2, g * K_PASS : (g + 1) * K_PASS]
            return load(f"x_raw{g}_{s}", [P, 2, K_PASS], source)[:].rearrange("p j (m t) -> p m j t", t=PACK)

        def load_y(g, t0, t1):
            tile = load(f"y_rows{g}_{t0}", [P, t1 - t0, N], y_rows[:, g, t0:t1, :])
            return [tile[:, t, :] for t in range(t1 - t0)]

        def load_per_row(name, values):
            tile = sb([P, PASSES, BLOCK_WORDS], F32, name)
            nc.sync.dma_start(tile[:, :, 0:PACK], values.rearrange("b (g p t) o -> p (b g) (t o)", g=PASSES, t=PACK))
            return tile[:, :, 0:PACK]

        w_plane = [load("w_plane0", [P, T], w_rows[:, 0, :])]
        nc.sync.dma_start(offsets[:], offs)
        xn_sb = load_per_row("xn_sb", xn)
        w_plane.extend(load(f"w_plane{j}", [P, T], w_rows[:, j, :]) for j in range(1, PACK))
        x_raw = [[load_x(g, s) for s in range(2)] for g in range(PASSES)]
        y_sb = load_y(0, 0, 1) + load_y(0, 1, 2) + load_y(0, 2, 4) + load_y(1, 0, 2) + load_y(1, 2, 4)
        wt_sb = load_per_row("wt_sb", wt)
        xm_raw = {}
        for c in range(2):
            for g in range(PASSES):
                xm_raw[g, c] = load(f"xm_raw{g}_{c}", [P, PACK, 2 * P], xm_rows[:, g, :, c * 2 * P : (c + 1) * 2 * P])

        def xm_block(b, g):
            return xm_raw[g, b // 2][:, :, (b % 2) * P : (b % 2 + 1) * P]


        minus_half = sb([P, PACK], F32, "minus_half")
        ones = sb([P, PACK], F32, "ones")
        nc.gpsimd.memset(ones[:], 1.0)
        nc.scalar.activation(minus_half[:], ones[:], ACT.Copy, scale=-0.5)
        half = sb([P, TILES], F32, "half")
        nc.gpsimd.memset(half[:], 0.5)
        identity = sb([P, P], F32, "identity")
        make_identity(nc, identity[:])
        factor_square = sb([P, P], F32, "factor_square")
        nc.vector.memset(factor_square[:], 0.0)

        windows = []
        for w in range(D_BLOCKS):
            window = sb([P, T], F32, f"window{w}")
            engine = nc.vector if w < WINDOWS_ON_VECTOR else nc.gpsimd
            engine.memset(window[:], 0.0)
            windows.append(window)

        first, second = slice(0, HALF), slice(HALF, N)
        halves = (first, second)

        xn_over = sb([P, TILES], F32, "xn_over")
        length = sb([P, TILES], F32, "length")
        nc.gpsimd.tensor_scalar(
            xn_over[:].rearrange("p (g t) -> p g t", t=PACK), xn_sb, 1.0 / (CLIP * CLIP), 0.0, ALU.mult, ALU.add
        )
        nc.gpsimd.tensor_tensor(length[:], xn_over[:], half[:], ALU.pow)

        w_bf = sb([P, N, PACK], BF16, "w_bf")
        cut = N - GATHER_SCALAR
        staged = sb([P, PACK, GATHER_SCALAR], BF16, "staged")
        for j in range(PACK):
            nc.vector.tensor_copy(w_bf[:, 0:cut, j], w_plane[j][:].indirect(offsets[:, 0 : cut // LIST_GROUP]))
            nc.scalar.activation(staged[:, j, :], w_plane[j][:].indirect(offsets[:, cut // LIST_GROUP :]), ACT.Copy)
            if j == PACK - 2:
                nc.scalar.copy(
                    w_bf[:, cut:, 0 : j + 1].rearrange("p (c i) t -> p c t i", i=RUN),
                    staged[:, 0 : j + 1, :].rearrange("p t (c i) -> p c t i", i=RUN),
                )
        nc.scalar.copy(w_bf[:, cut:, PACK - 1], staged[:, PACK - 1, :])
        w_codes = sb([P, N], U32, "w_codes")
        w_scales = sb([P, N], U8, "w_scales")
        nc.vector.quantize_mx(
            out=w_codes[:].bitcast(E4M3), scales=w_scales[:], in_=w_bf[:].rearrange("p i j -> p (i j)")
        )

        x_bf = [[sb([P, 2, P, PACK], BF16, f"x_bf0_{u}")[:] for u in range(2)]]
        x_bf1 = sb([P, PACK, P, PACK], BF16, "x_bf1")
        x_bf.append([x_bf1[:, 0:2, :, :], x_bf1[:, 2:4, :, :]])
        scores = {}

        def on_vector(dst, src):
            nc.vector.tensor_copy(dst, src)

        def on_scalar(dst, src):
            nc.scalar.activation(dst, src, ACT.Copy)

        def on_gpsimd(dst, src):
            nc.gpsimd.tensor_scalar(dst, src, 1.0, 0.0, ALU.mult, ALU.add)

        def weave_x(copy, g, u, s, m0=0, m1=P):
            copy(
                x_bf[g][u][:, :, m0:m1, 2 * s : 2 * s + 2].rearrange("p t m j -> p m t j"),
                x_raw[g][s][:, m0:m1, :, 2 * u : 2 * u + 2].rearrange("p m j t -> p m t j"),
            )

        def score(g, t0, t1):
            codes = sb([P, t1 - t0, P], U32, f"x_codes{g}_{t0}")
            scales = sb([P, t1 - t0, P], U8, f"x_scales{g}_{t0}")
            nc.vector.quantize_mx(
                out=codes[:].rearrange("p t m -> p (t m)").bitcast(E4M3),
                scales=scales[:].rearrange("p t m -> p (t m)"),
                in_=x_bf[g][t0 // 2][:, t0 % 2 : t0 % 2 + t1 - t0, :, :].rearrange("p t m j -> p (t m j)"),
            )
            for t in range(t0, t1):
                k = PACK * g + t
                scores[k] = bank(k, f"scores{k}", N)
                nc.tensor.matmul_mx(
                    out=scores[k][:],
                    lhsT=codes[:, t - t0, :].bitcast(E4M3),
                    lhsT_scale=scales[:, t - t0, :],
                    rhs=w_codes[:].bitcast(E4M3),
                    rhs_scale=w_scales[:],
                    start=True,
                    stop=True,
                )

        weave_x(on_scalar, 0, 0, 0)
        weave_x(on_scalar, 0, 1, 0, 0, PAIR1_VECTOR)
        weave_x(on_scalar, 0, 1, 0, PAIR1_VECTOR, P)
        weave_x(on_vector, 0, 0, 1)
        weave_x(on_vector, 0, 1, 1, 0, PAIR1_VECTOR)
        weave_x(on_scalar, 0, 1, 1, PAIR1_VECTOR, P)
        score(0, 0, 1)
        score(0, 1, 2)
        score(0, 2, 4)
        on_scalar(x_bf1[:, :, :, 0:2].rearrange("p t m j -> p m t j"), x_raw[1][0].rearrange("p m j t -> p m t j"))

        def finish_x1(copy, m0, m1):
            copy(
                x_bf1[:, :, m0:m1, 2:4].rearrange("p t m j -> p m t j"),
                x_raw[1][1][:, m0:m1, :, :].rearrange("p m j t -> p m t j"),
            )

        finish_x1(on_gpsimd, 0, X1_GPSIMD)
        finish_x1(on_scalar, X1_GPSIMD, P)

        diffs = [sb([P, PACK, N], F32, f"diffs{g}") for g in range(PASSES)]
        e = [sb([P, N], F32, f"e{k}") for k in range(TILES)]
        sums = [sb([P, PACK], F32, f"sums{g}") for g in range(PASSES)]
        sumsq = [sb([P, PACK], F32, f"sumsq{g}") for g in range(PASSES)]
        inverse, root = {}, {}

        def exponential(k):
            g, t = divmod(k, PACK)
            neg_max = sb([P, 1], F32, f"neg_max{k}")
            nc.vector.tensor_reduce(neg_max[:], scores[k][:], AXIS.X, ALU.max, negate=True)
            nc.scalar.activation(e[k][:], scores[k][:], ACT.Exp, bias=neg_max[:], accum_out=sums[g][:, t : t + 1])

        def difference(k):
            g, t = divmod(k, PACK)
            col = slice(t, t + 1)
            nc.vector.scalar_tensor_tensor(diffs[g][:, t, :], y_sb[k], sums[g][:, col], e[k][:], ALU.mult, ALU.subtract)
            nc.scalar.activation(
                e[k][:], diffs[g][:, t, :], ACT.Square, scale=length[:, k : k + 1], accum_out=sumsq[g][:, col]
            )

        def invert_sums(g):
            inverse[g] = sb([P, PACK], F32, f"inverse{g}")
            nc.vector.reciprocal(inverse[g][:], sums[g][:])

        def row_roots(g):
            root[g] = sb([P, PACK], F32, f"root{g}")
            nc.gpsimd.tensor_tensor(root[g][:], sumsq[g][:], minus_half[:], ALU.pow)

        def lesser(g):
            nc.vector.tensor_tensor(bounds[:, g, 0:PACK], root[g][:], inverse[g][:], ALU.min)

        def scale_and_weave(woven, g, slots, factor):
            runs = (slots.stop - slots.start) // RUN
            nc.vector.tensor_tensor(
                woven.rearrange("p (c i) t -> p c t i", i=RUN),
                diffs[g][:, :, slots].rearrange("p t (c i) -> p c t i", i=RUN),
                factor.unsqueeze(1).unsqueeze(3).to_broadcast([P, runs, PACK, RUN]),
                ALU.mult,
            )

        g_codes, g_scales = {}, {}

        def within_half(slots):
            h = slots.start // HALF
            return h, slice(slots.start - h * HALF, slots.stop - h * HALF)

        def quantize_g(g, slots, woven):
            h, cols = within_half(slots)
            if (g, h) not in g_codes:
                g_codes[g, h] = sb([P, HALF], U32, f"g_codes{g}_{h}")
                g_scales[g, h] = sb([P, HALF], U8, f"g_scales{g}_{h}")
            nc.vector.quantize_mx(
                out=g_codes[g, h][:, cols].bitcast(E5M2),
                scales=g_scales[g, h][:, cols],
                in_=woven.rearrange("p i t -> p (i t)"),
            )

        m_codes, m_scales = {}, {}

        def weave_m(copy, woven, b, g):
            copy(
                woven.rearrange("p (c i) t -> p c t i", i=RUN),
                xm_block(b, g).rearrange("p t (c i) -> p c t i", i=RUN),
            )

        def weave_block(copy, b):
            woven = sb([P, PASSES, P, PACK], BF16, f"m_bf{b}")
            for g in range(PASSES):
                weave_m(copy, woven[:, g, :, :], b, g)
            return woven[:]

        def quantize_m(b, g0, woven, name):
            passes = woven.shape[1]
            codes = sb([P, passes, P], U32, name)
            scales = sb([P, passes, P], U8, f"m_scales{b}_{g0}")
            nc.vector.quantize_mx(
                out=codes[:].rearrange("p g m -> p (g m)").bitcast(E4M3),
                scales=scales[:].rearrange("p g m -> p (g m)"),
                in_=woven.rearrange("p g m t -> p (g m t)"),
            )
            for g in range(passes):
                m_codes[b, g0 + g], m_scales[b, g0 + g] = codes[:, g, :], scales[:, g, :]

        in_order = list(range(PASSES))
        last_first = in_order[::-1]

        def product(b, slots, index, order=in_order):
            acc = bank(index, f"acc{b}_{slots.start}", slots.stop - slots.start)
            h, cols = within_half(slots)
            for g in order:
                nc.tensor.matmul_mx(
                    out=acc[:],
                    lhsT=m_codes[b, g].bitcast(E4M3),
                    lhsT_scale=m_scales[b, g],
                    rhs=g_codes[g, h][:, cols].bitcast(E5M2),
                    rhs_scale=g_scales[g, h][:, cols],
                    start=(g == order[0]),
                    stop=(g == order[-1]),
                )
            return acc

        def leave_on_scalar(sums_ap, name):
            dw = sb([P, sums_ap.shape[1]], F32, name)
            nc.scalar.activation(dw[:], sums_ap, ACT.Copy, scale=-1.0)
            return dw

        def leave_on_vector(dw_ap, sums_ap):
            nc.vector.tensor_scalar(dw_ap, sums_ap, -1.0, None, ALU.mult)

        def listed(b, slots):
            return windows[b][:].indirect(offsets[:, slots.start // LIST_GROUP : slots.stop // LIST_GROUP])

        def scatter_on_scalar(b, slots, dw):
            nc.scalar.activation(listed(b, slots), dw[:], ACT.Copy)

        def scatter_on_vector(b, slots, dw):
            nc.vector.tensor_copy(listed(b, slots), dw[:])

        def store(b):
            nc.sync.dma_start(out[b * P : (b + 1) * P, :], windows[b][:])

        for k in range(PACK):
            exponential(k)
        difference(0)
        difference(1)
        score(1, 0, 2)
        score(1, 2, 4)
        difference(2)
        difference(3)
        invert_sums(0)
        row_roots(0)
        exponential(4)
        exponential(5)
        exponential(6)
        bounds = sb([P, PASSES, BLOCK_WORDS], F32, "bounds")
        lesser(0)
        bound0 = bounds[:, 0, 0:PACK]
        exponential(7)
        nc.vector.tensor_tensor(factor_square[:, 0:PACK], bound0, wt_sb[:, 0, :], ALU.mult)
        turned = bank(0, "turned", P)
        nc.tensor.transpose(turned[:], factor_square[:], identity[:])
        difference(4)
        turned_sb = sb([P, P], F32, "turned_sb")
        nc.scalar.copy(turned_sb[:], turned[:])
        factor0 = bank(1, "factor0", P)
        nc.tensor.transpose(factor0[:], turned_sb[:], identity[:])
        for k in range(PACK + 1, TILES):
            difference(k)
        invert_sums(1)

        def weave_g(g, h, factor):
            woven = sb([P, HALF, PACK], BF16, f"g_bf{g}_{h}")
            scale_and_weave(woven[:], g, halves[h], factor)
            return woven[:]

        g_bf00 = weave_g(0, 0, factor0[:, 0:PACK])
        m_bf1 = [sb([P, 1, P, PACK], BF16, f"m_bf1_{g}") for g in range(PASSES)]
        on_gpsimd(m_bf1[0][:, 0, :, :], xm_block(1, 0).rearrange("p t m -> p m t"))
        row_roots(1)
        g_bf01 = weave_g(0, 1, factor0[:, 0:PACK])
        m_bf0 = weave_block(nc.scalar.copy, 0)
        weave_m(nc.scalar.copy, m_bf1[1][:, 0, :, :], 1, 1)
        m_bf2 = weave_block(nc.scalar.copy, 2)
        m_bf3 = weave_block(nc.scalar.copy, 3)

        lesser(1)
        quantize_g(0, first, g_bf00)
        factor1 = sb([P, PACK], F32, "factor1")[:]
        nc.vector.tensor_tensor(factor1, bounds[:, 1, 0:PACK], wt_sb[:, 1, :], ALU.mult)
        quantize_m(0, 0, m_bf0, "m_codes0")
        quarters = (slice(0, QUARTER), slice(QUARTER, HALF))
        g_quarter = [sb([P, QUARTER, PACK], BF16, f"g_bf1_q{i}") for i in range(2)]
        for woven, slots in zip(g_quarter, quarters):
            scale_and_weave(woven[:], 1, slots, factor1)
        dw = {(0, 0): sb([P, HALF], F32, "dw0_0")}
        for woven, slots, index in zip(g_quarter, quarters, (2, 3)):
            quantize_g(1, slots, woven[:])
            nc.scalar.activation(dw[0, 0][:, slots], product(0, slots, index)[:], ACT.Copy, scale=-1.0)
        scatter_on_scalar(0, first, dw[0, 0])

        quantize_m(1, 0, m_bf1[0][:], "m_codes1_0")
        quantize_g(0, second, g_bf01)
        third, fourth = slice(HALF, HALF + QUARTER), slice(HALF + QUARTER, N)
        g_third = sb([P, QUARTER, PACK], BF16, "g_bf1_q2")
        g_fourth = sb([P, QUARTER, PACK], BF16, "g_bf1_q3")
        scale_and_weave(g_third[:], 1, third, factor1)
        scale_and_weave(g_fourth[:], 1, fourth, factor1)
        quantize_g(1, third, g_third[:])
        quantize_g(1, fourth, g_fourth[:])
        acc02 = product(0, third, 0)
        acc03 = product(0, fourth, 4)
        quantize_m(1, 1, m_bf1[1][:], "m_codes1_1")
        acc = {(1, 0): product(1, first, 5), (1, 1): product(1, second, 6)}
        quantize_m(2, 0, m_bf2, "m_codes2")
        acc[2, 0], acc[2, 1] = product(2, first, 7), product(2, second, 3)
        dw[0, 1] = sb([P, HALF], F32, "dw0_1")
        leave_on_vector(dw[0, 1][:, 0:QUARTER], acc02[:])
        leave_on_vector(dw[0, 1][:, QUARTER:], acc03[:])

        def first_half_on_vector(b):
            dw[b, 0] = sb([P, HALF], F32, f"dw{b}_0")
            leave_on_vector(dw[b, 0][:], acc[b, 0][:])

        first_half_on_vector(1)
        scatter_on_vector(0, second, dw[0, 1])
        store(0)
        first_half_on_vector(2)
        quantize_m(3, 0, m_bf3, "m_codes3")
        acc[3, 0], acc[3, 1] = product(3, first, 2), product(3, second, 1)

        for b in range(1, D_BLOCKS):
            dw[b, 1] = leave_on_scalar(acc[b, 1][:], f"dw{b}_1")
            scatter_on_scalar(b, first, dw[b, 0])
            scatter_on_vector(b, second, dw[b, 1])
            store(b)
            if b == 1:
                first_half_on_vector(3)
